import numpy as np, ml_dtypes
CORES = [2,3,42,43,82,83,122,123]
N = 8
import mx_ref
BF = ml_dtypes.bfloat16
def gcols(t, e):
    v = np.concatenate([t.reshape(8, 16, -1, 4), np.zeros((8, 16, 1, 4), BF)], axis=2)
    return np.ascontiguousarray(np.stack([v[g][:, e[g]] for g in range(8)])).reshape(128, -1)
def tile(rs):
    return np.stack(rs, axis=2).reshape(128, -1).astype(BF)
def pick(q, e):
    c = np.concatenate([q[0].reshape(128, -1, 4), np.zeros((128, 1, 4), np.uint8)], axis=1); s = np.concatenate([q[1], np.ones((16, 1), np.uint8)], axis=1)
    return (np.ascontiguousarray(c[:, e].reshape(128, -1)), np.ascontiguousarray(s[:, e]))
def join(*qs):
    return (np.concatenate([q[0] for q in qs], axis=1), np.concatenate([q[1] for q in qs], axis=1))
def put(q, e, v):
    c, s = q[0].reshape(128, -1, 4).copy(), q[1].copy(); c[:, e] = v[0].reshape(128, -1, 4); s[:, e] = v[1]
    return (c.reshape(128, -1), s)
def pk(c, s):
    return (np.ascontiguousarray(c), mx_ref.live(s))
def emit(q):
    return q[0], q[1]
def packed(v, rng):
    q = [mx_ref.quantize(np.ascontiguousarray(v[r])) for r in range(N)]
    return np.stack([a for a, b in q]), np.stack([mx_ref.plane(b, rng) for a, b in q])
def values_of_codes():
    e, c = np.zeros((128, 128, 4), np.float32), np.zeros((128, 2, 4), np.uint8)
    e[np.arange(128), np.arange(128), 0] = 1
    c[:127, :, 0] = np.arange(256).reshape(2, 128).T[:127]
    return mx_ref.matmul(mx_ref.quantize(e.reshape(128, 512).astype(BF)), (c.reshape(128, 8), np.full((16, 2), 127, np.uint8))).T.reshape(-1).astype(np.float64)
CODE_VALUE, SCALE_VALUE = values_of_codes(), 2.0 ** (np.arange(256) - 127.0)
def decode(q):
    return (CODE_VALUE[q[0]].reshape(16, 8, -1, 4) * SCALE_VALUE[q[1]][:, None, :, None] + 0.0).reshape(128, -1).astype(np.float32)
def f(rng, *shape):
    return mx_ref.flush((rng.standard_normal(shape, dtype=np.float32) * np.exp2(rng.integers(-2, 3, shape[:-1] + (1,)))).astype(BF))
def wide(rng, *shape, cols=0):
    v = rng.standard_normal(shape, dtype=np.float32) * np.exp2(rng.integers(-12, 13, shape)).astype(np.float32)
    if cols: v *= np.repeat(np.exp2(rng.integers(-cols, cols + 1, shape[:-2] + (1, shape[-1] // 4))) * (rng.random(shape[:-2] + (1, shape[-1] // 4)) > 0.0625), 4, axis=-1).astype(np.float32)
    return mx_ref.flush(v.astype(BF))
C, K = 384, 192
STEP = [1, 2, 4]
def numbers_of(rng):
    return {"x": np.array(f(rng, N, 128, 4 * C)), "u": np.array(f(rng, N, 128, 512)), "v": np.array(f(rng, N, 128, 512))}
def same(rng, w):
    c, s = packed(np.stack([w] * N), rng)
    return {"wc": c, "ws": np.stack([s[0]] * N)}
def weights(rng, still=[]):
    w = np.array(f(rng, 128, 2048)).reshape(8, 16, 4, 8, 16, 4)
    for i in still:
        w[:, i] = 0
        w[:, :, :, :, i] = 0
    return same(rng, w.reshape(128, 2048))
def setup_inputs(rng):
    return {**numbers_of(rng), **weights(rng)}
def setup_inputs_ties(rng):
    d = numbers_of(rng)
    x = d["x"].reshape(N, 8, 16, C, 4)
    x[:, :, 0] = 0
    x[:, :, 0, :, 0] = rng.integers(0, 3, (N, 8, C)).astype(np.float32).astype(BF)
    u = d["u"].reshape(N, 128, 128, 4)
    u[:, :, ::16] = 0
    o = rng.permutation(N)
    for r in range(N):
        for h in range(0, 128, 16): u[r, h, h, 0] = 0.0 if r == o[0] else -1.0 if r == o[1] else 1.0
    return {"x": x.reshape(N, 128, 4 * C), "u": u.reshape(N, 128, 512), "v": d["v"], **weights(rng, [0])}
def setup_inputs_near(rng):
    d = numbers_of(rng)
    x = d["x"].astype(np.float32).reshape(N, 8, 16, C, 4)
    x[:, :, 0] = 0
    x[:, :, 8:] = 0
    s = rng.integers(0, 16, (N, 8, C))
    c = rng.permuted(np.tile(np.arange(8) % 2 * 2.0 - 1.0, (N, 1)), axis=1)
    u = d["u"].reshape(N, 128, 128, 4)
    u[:, :, ::16] = 0
    o = rng.permutation(N) % 4
    for r in range(N):
        k = 1.0 if o[r] == 0 else 2.0 ** -30
        if o[r] < 2:
            x[r, :, 0, :, 0] = c[r][:, None]
            x[r, :, 11, :, 0] = 2.0 ** -10
        else:
            for g in rng.permutation(8)[:4]:
                far = int(rng.integers(C))
                x[r, g, :8, far] = 0
                x[r, g, 0, far, 0] = 2.0 ** 30 * rng.choice([-1.0, 1.0])
        if o[r] == 2:
            t = rng.integers(0, 2, (8, C)) == 1
            x[r, :, 9, :, 0] = np.where(t, 1.125 * 2.0 ** -30 * c[r][:, None], 0.0)
            x[r, :, 10, :, 0] = np.where(t, 0.0, 2.0 ** -30 * c[r][:, None])
        else: x[r, :, 8] = ((s[r][:, :, None] >> np.arange(4)) & 1) * np.exp2(np.arange(4) - 23.0)
        for h in range(0, 128, 16):
            u[r, h, h, 0] = k
            if o[r] == 2:
                u[r, h + 9, h, 0] = k * 1.125
                u[r, h + 10, h, 0] = k * 1.25
            else: u[r, h + 8, h] = k
            if o[r] < 2: u[r, h + 11, h, 0] = k
    return {"x": x.reshape(N, 128, 4 * C).astype(BF), "u": u.reshape(N, 128, 512), "v": d["v"], **weights(rng, [0, 8, 9, 10, 11, 12, 13, 14, 15])}
def setup_inputs_huge(rng):
    d = numbers_of(rng)
    o = rng.permutation(N)
    c = rng.integers(0, 2, (N, 1, 1, C, 1)) * 2.0 - 1.0
    c[o < N // 2] = -1.0
    x = (0.6 + 0.09 * rng.random((N, 8, 16, C, 4))) * c
    x[o == 0] = -0.9 - 0.1 * rng.random((1, 8, 16, C, 4))
    a = 1.0 - 0.1 * rng.random((N, 8, 16, 8, 4))
    for r in range(N): a[r] *= (rng.permutation(8) % 2 * 2.0 - 1.0)[None, None, :, None]
    u = d["u"].reshape(N, 128, 128, 4)
    u[:, :, ::16] = (2.0 ** 30 * a).reshape(N, 128, 8, 4).astype(np.float32).astype(BF)
    w = np.zeros((128, 4, 128, 4), np.float32)
    i = np.arange(128)
    for b in range(4): w[i, b, i, b] = 4
    return {"x": (2.0 ** 30 * x).astype(np.float32).reshape(N, 128, 4 * C).astype(BF), "u": u.reshape(N, 128, 512), "v": d["v"], **same(rng, w.reshape(128, 2048).astype(BF))}
def setup_inputs_jam(rng):
    d = numbers_of(rng)
    x = d["x"].reshape(N, 8, 16, C, 4)
    o = rng.permutation(N) % 4
    a = np.argsort(rng.random((N, 8, C)), axis=2) < K
    i = np.arange(C)
    for r in range(N):
        if o[r] == 0:
            a[r, ::2] = i >= C - K
            a[r, 1::2] = i < K
        if o[r] == 1: a[r] = a[r, 0].copy()
        if o[r] == 2:
            for g in range(8): a[r, g] = (i + int(rng.integers(C))) % C < K
    x[:, :, :2] = 0
    x[:, :, 0, :, 0] = np.where(a, -4.0, -3.0).astype(np.float32).astype(BF)
    x[:, :, 1, :, 0] = 1.0
    t = (1.0 + (2 * rng.integers(0, 64, (N, 8, 8, C, 4)) + 1) / 128.0) * np.exp2(rng.integers(-14, -8, (N, 8, 8, C, 4))) * (rng.integers(0, 2, (N, 8, 8, C, 4)) * 2.0 - 1.0)
    x[:, :, 8:] = t.astype(np.float32).astype(BF)
    x[:, :, 8, :, 0] = 1.96875
    u = d["u"].reshape(N, 128, 128, 4)
    u[:, :, ::16] = 0
    for h in range(0, 128, 16): u[:, h, h, 0] = -1.0
    for r in range(N):
        if o[r] == 3:
            x[r, :, 0, :, 0] = -4.0
            x[r, :, 9] = 0
            x[r, :, 9, :, 0] = (np.where(a[r], 4.0, 3.0) * np.exp2(-13.0 - np.arange(8) % 4)[:, None]).astype(np.float32).astype(BF)
            for h in range(0, 128, 16): u[r, h + 9, h, 0] = 1.0
    w = np.array(f(rng, 128, 2048)).reshape(8, 16, 4, 8, 16, 4)
    w[:, :, :, :, :2] = 0
    w[:, :, :, :, 8:] = 0
    return {"x": x.reshape(N, 128, 4 * C), "u": u.reshape(N, 128, 512), "v": d["v"], **same(rng, fall(w))}
def fall(v):
    for g in range(8): v[g, 1, 0, g, 0, 0] = 128.0
    return v.reshape(128, 2048)
def setup_inputs_spread(rng):
    d = setup_inputs(rng)
    d["x"] = wide(rng, N, 128, 4 * C, cols=6)
    return d
def check_inputs(d):
    b = []
    for k in ("x", "u", "v"):
        a = np.abs(d[k].astype(np.float32))
        if not (np.isfinite(a).all() and ((a == 0) | (a >= 2.0 ** -30) & (a <= 2.0 ** 30)).all()): b.append("a value of " + k)
    if ((d["wc"] & 0x7F) == 0x7F).any(): b.append("a code of wc that is no number")
    for k in ("wc", "ws"):
        if (d[k] != d[k][:1]).any(): b.append(k + " isn't the same on all ranks")
    none, least, most = [emit(mx_ref.quantize(np.full((128, 16), k, np.float32).astype(BF)))[1][0, 0] for k in (0.0, 2.0 ** -30, 2.0 ** 30)]
    for r in range(N):
        s = mx_ref.live(d["ws"][r])
        if ((s != none) & ((s < least) | (s > most))).any(): b.append("a scale of ws")
    return b
def places(s):
    a = np.sort(np.argsort(-s, axis=2, kind="stable")[:, :, :K], axis=2)
    j = np.arange(K)
    c = a.copy()
    at = np.stack([j] * N)
    for g in range(7):
        n = np.sum(a[:, g + 1][:, None, :] < a[:, g][:, :, None], axis=2)
        p = np.maximum.accumulate(n - j, axis=1) + j
        for r in range(N):
            m = int(np.sum(p[r] < K))
            p[r, m:] = np.setdiff1d(j, p[r, :m])
            at[r] = p[r][at[r]]
            c[r, g + 1] = a[r, g + 1][at[r]]
    return c
def reference(x, u, v, wc, ws):
    qu = [mx_ref.quantize(u[r]) for r in range(N)]
    lay = [pk(wc[r], ws[r]) for r in range(N)]
    now = [x[r] for r in range(N)]
    for e in STEP:
        q = [mx_ref.quantize(now[r]) for r in range(N)]
        own = [decode(q[r]) for r in range(N)]
        c = places(np.stack([mx_ref.matmul(qu[r], q[r])[::16] for r in range(N)]) + np.float32(0.0))
        made = []
        for r in range(N):
            z = mx_ref.quantize(gcols(own[r].astype(BF), c[r]))
            h = tile([np.maximum(mx_ref.matmul(pick(lay[r], np.arange(128 * b, 128 * b + 128)), z), np.float32(0.0)) * np.float32(0.015625) for b in range(4)])
            made.append(decode(mx_ref.quantize(h)))
        for r in range(N):
            a, b = own[r].reshape(8, 16, C, 4).copy(), made[r ^ e].reshape(8, 16, K, 4)
            for g in range(8): a[g][:, c[r, g]] += b[g]
            now[r] = a.reshape(128, 4 * C).astype(BF)
    y, pl = np.zeros((N, 128, C), np.float32), np.zeros((N, 8, K), np.float32)
    oc, osc = np.zeros((N, 128, 4 * C), np.uint8), np.zeros((N, 16, C), np.uint8)
    for r in range(N):
        q = mx_ref.quantize(now[r])
        y[r] = mx_ref.matmul(mx_ref.quantize(v[r]), q)
        pl[r] = c[r]
        oc[r], osc[r] = emit(q)
    return {"y": y, "pl": pl, "oc": oc, "osc": osc}

@@ -1,0 +1,561 @@
+from concourse.mybir import dt, AluOpType, AxisListType, ActivationFunctionType
+
+STEP = [1, 2, 4]
+F32, BF, I32, U16, Q4, U8 = "float32", "bfloat16", "int32", "uint16", "float8_e4m3fn_x4", "uint8"
+
+
+def _sb(n, d):
+    return ("sbuf", [128, n], d)
+
+
+SCRATCH = {
+    "xt": _sb(1536, BF), "xn": _sb(1536, BF), "ut": _sb(512, BF), "vt": _sb(512, BF),
+    "qx": _sb(384, Q4), "sx": _sb(384, U8), "qu": _sb(128, Q4), "su": _sb(128, U8),
+    "qup": _sb(384, Q4), "sup": _sb(384, U8), "qv": _sb(128, Q4), "sv": _sb(128, U8),
+    "qw": _sb(512, Q4), "sw": _sb(512, U8),
+    "et": _sb(2048, BF), "qe": _sb(512, Q4), "se": _sb(512, U8), "idn": _sb(128, BF), "one": _sb(128, BF),
+    "gt": _sb(512, BF), "qg": _sb(128, Q4), "sg": _sb(128, U8),
+    "ci": _sb(64, I32), "cj": _sb(4, I32), "cf": _sb(128, F32), "col": _sb(24, F32), "offc": _sb(48, U16),
+    "msame": _sb(32, F32), "mge": _sb(32, F32), "mlt": _sb(32, F32), "mltn": _sb(32, F32), "mall": _sb(32, F32),
+    "cc": _sb(32, F32), "idl": _sb(12, F32), "rst": _sb(99, F32), "ci2": _sb(72, F32),
+    "kv": _sb(192, F32), "pre": _sb(400, F32),
+    "ts": _sb(384, F32), "rs": _sb(24, F32), "tk": _sb(384, F32),
+    "stl": _sb(32, F32), "sml": _sb(32, F32), "kt": _sb(32, F32), "km": _sb(32, F32), "ww": _sb(32, F32),
+    "yy": _sb(64, F32), "r1": _sb(2, F32), "m1": _sb(64, F32), "m1t": _sb(64, F32), "ab": _sb(2, F32),
+    "fl": _sb(99, F32), "cum": _sb(99, F32), "m2": _sb(128, F32), "m2t": _sb(130, F32), "kk": _sb(4, F32),
+    "junk": _sb(66, F32), "rr": _sb(66, F32), "cb": _sb(66, F32), "mn": _sb(66, F32), "bb": _sb(33, F32),
+    "bt": _sb(32, F32), "ee": _sb(32, F32), "em": _sb(32, F32), "nl": _sb(33, F32),
+    "m3": _sb(64, F32), "m3t": _sb(64, F32), "cr": _sb(2, F32),
+    "w1": _sb(256, F32), "w2": _sb(96, F32),
+    "tau": _sb(32, F32), "tb": _sb(64, F32), "tbt": _sb(64, F32), "tl": _sb(24, F32), "offs": _sb(24, U16),
+    "vx": _sb(384, F32), "vr": _sb(384, F32),
+    "wa": _sb(400, F32), "wb": _sb(192, F32), "wd": _sb(200, F32), "we": _sb(384, F32),
+    "ds": _sb(384, BF), "dst": _sb(384, BF),
+    "ta": _sb(384, F32), "tc": _sb(384, F32), "l1": _sb(12, F32),
+    "off1": _sb(36, U16), "off2": _sb(36, U16), "off3": _sb(24, U16),
+    "fi": _sb(24, I32), "offz": _sb(12, U16), "offi": _sb(12, U16), "offx": _sb(24, U16),
+    "iw": _sb(400, F32), "ib": _sb(72, F32),
+    "fz": _sb(4 * 576, BF), "zt": _sb(768, BF), "qz": _sb(192, Q4), "sz": _sb(192, U8), "ht": _sb(768, BF),
+    "cmp": _sb(4 * (384 + 320 + 256 + 3 * 192), BF), "qc": _sb(320 + 256 + 4 * 192, Q4), "sc": _sb(320 + 256 + 4 * 192, U8),
+    "plr": _sb(192, F32), "yo": _sb(384, F32),
+}
+for _r in range(3):
+    SCRATCH["qh%d" % _r] = _sb(192, Q4)
+    SCRATCH["sh%d" % _r] = _sb(192, U8)
+    SCRATCH["ql%d" % _r] = _sb(192, Q4)
+    SCRATCH["sl%d" % _r] = _sb(192, U8)
+for _b in range(8):
+    SCRATCH["pb%d" % _b] = ("psum", [128, 512], F32)
+
+NDMA = 24
+SEMAPHORES = ["cV", "cS", "cP", "cG", "sent", "arr0", "arr1", "arr2"] + ["d%d" % i for i in range(NDMA)]
+
+OP = AluOpType
+FN = ActivationFunctionType
+BIG = 2.0 ** 80
+FAR = 2.0 ** 95
+
+
+def rank_program(g, core, T, topo):
+    rank = T.rank_of(core)
+    if rank is None:
+        return
+    queue = {"V": g.vector, "S": g.scalar, "P": g.tensor, "G": g, "Y": g.sync}
+    count = {"cV": 0, "cS": 0, "cP": 0, "cG": 0}
+    known = {e: {} for e in queue}
+    recs = {}
+    ndma = [0]
+
+    def A(name, c0=0, c1=None, st=1, p0=0, p1=128):
+        n = SCRATCH[name][1][1]
+        c1 = n if c1 is None else c1
+        ap = T[name][p0:p1, c0:c1:st] if st != 1 else T[name][p0:p1, c0:c1]
+        cols = 0
+        for c in range(c0, c1, st):
+            cols |= 1 << c
+        pm = 0
+        for b in range(p0 // 32, (p1 + 31) // 32):
+            pm |= 1 << b
+        if name.startswith("pb"):
+            cols, pm = 1, 15
+        return (ap, [(name, pm, cols)])
+
+    def ind(win, off):
+        return (win[0].indirect(off[0]), win[1], off[1])
+
+    def words(v):
+        return (v[0].bitcast(dt.uint32), v[1])
+
+    def wait(e, sem, val, snap=None):
+        if known[e].get(sem, 0) < val:
+            queue[e].wait_ge(T.sem[sem], val)
+            known[e][sem] = val
+        if snap:
+            for s, x in snap.items():
+                if known[e].get(s, 0) < x:
+                    known[e][s] = x
+
+    def issue(e, call, outs, ins, sem=None, inc=1, chain=False):
+        acc = []
+        for v in outs:
+            acc += [(x, True) for x in v[1]]
+            if len(v) > 2:
+                acc += [(x, False) for x in v[2]]
+        for v in ins:
+            if isinstance(v, tuple):
+                acc += [(x, False) for x in v[1]]
+                if len(v) > 2:
+                    acc += [(x, False) for x in v[2]]
+        need = {}
+        for (name, pm, cols), wr in acc:
+            psum = name.startswith("pb")
+            for r in recs.get(name, []):
+                if r[1] & pm and r[2] & cols and (wr or r[0] or (psum and r[3] != e)):
+                    if chain and psum and r[3] == e:
+                        continue
+                    if need.get(r[4], (0, None))[0] < r[5]:
+                        need[r[4]] = (r[5], r[6])
+        for s in sorted(need, key=lambda s: s == "c" + e):
+            wait(e, s, need[s][0], need[s][1])
+        ins_ = call()
+        if sem is None:
+            sem = "c" + e
+            count[sem] += 1
+            val = count[sem]
+            ins_.then_inc(T.sem[sem], 1)
+        elif inc:
+            val = inc
+            ins_.then_inc(T.sem[sem], inc)
+            count[sem] = inc
+        else:
+            val = count[sem]
+        snap = dict(known[e])
+        for (name, pm, cols), wr in acc:
+            lst = recs.setdefault(name, [])
+            if wr:
+                lst[:] = [r for r in lst if (r[1] & ~pm) or (r[2] & ~cols)]
+            lst.append((wr, pm, cols, e, sem, val, snap))
+
+    def raw(v):
+        return v[0] if isinstance(v, tuple) else v
+
+    def tt(o, a, b, op):
+        issue("V", lambda: g.vector.tensor_tensor(o[0], a[0], b[0], op), [o], [a, b])
+
+    def ts(o, a, s1, op0, s2=None, op1=None):
+        if op1 is None:
+            issue("V", lambda: g.vector.tensor_scalar(o[0], a[0], raw(s1), None, op0), [o], [a, s1])
+        else:
+            issue("V", lambda: g.vector.tensor_scalar(o[0], a[0], raw(s1), raw(s2), op0, op1), [o], [a, s1, s2])
+
+    def cp(o, a):
+        issue("V", lambda: g.vector.tensor_copy(o[0], a[0]), [o], [a])
+
+    def tr(o, a):
+        issue("V", lambda: g.vector.transpose(o[0], a[0]), [o], [a])
+
+    def red(o, a, op, neg=False):
+        issue("V", lambda: g.vector.tensor_reduce(o[0], a[0], AxisListType.X, op, negate=neg), [o], [a])
+
+    def scan(o, a, b, init, op0, op1):
+        issue("V", lambda: g.vector.tensor_tensor_scan(o[0], a[0], b[0], init, op0, op1), [o], [a, b])
+
+    def fill(o, x):
+        issue("V", lambda: g.vector.memset(o[0], x), [o], [])
+
+    def quant(q, s, a):
+        issue("V", lambda: g.vector.quantize_mx(q[0], s[0], a[0]), [q, s], [a])
+
+    def act(o, a, fn, bias=None, scale=None, accum=None):
+        kw = {}
+        if bias is not None:
+            kw["bias"] = raw(bias)
+        if scale is not None:
+            kw["scale"] = raw(scale)
+        if accum is not None:
+            kw["accum_out"] = accum[0]
+        issue("S", lambda: g.scalar.activation(o[0], a[0], fn, **kw), [o] + ([accum] if accum else []), [a, bias, scale])
+
+    def lin(o, a, scale=None, bias=None, accum=None):
+        act(o, a, FN.Identity, bias, scale, accum)
+
+    def mm(bank, n, wq, ws_, xq, xs, start=True, stop=True):
+        o = A("pb%d" % bank, 0, n)
+        issue("P", lambda: g.tensor.matmul_mx(o[0], wq[0], ws_[0], xq[0], xs[0], start, stop), [o], [wq, ws_, xq, xs], chain=not start)
+
+    def iota(o, pattern, base, mult=0):
+        if SCRATCH[o[1][0][0]][2] == I32:
+            issue("G", lambda: g.iota(o[0], pattern, base, mult), [o], [])
+        else:
+            issue("G", lambda: g.iota(o[0], pattern, base, mult, allow_small_or_imprecise_dtypes=True), [o], [])
+
+    def gfill(o, n, x):
+        iota(o, [[0, n]], x)
+
+    def sel(o, a, pattern, op, other, base, mult):
+        issue("G", lambda: g.affine_select(o[0], a[0], pattern, op, other, base, mult), [o], [a])
+
+    def dma(e, o, a):
+        sem = "d%d" % ndma[0]
+        ndma[0] += 1
+        issue(e, lambda: queue[e].dma_start(o[0], a[0]), [o], [a], sem=sem, inc=16)
+
+    def ext(ap):
+        return (ap, [])
+
+    def bytes_(v):
+        return (v[0].bitcast(dt.uint8), v[1])
+
+    def P(b, c0, c1, st=1):
+        return A("pb%d" % b, c0, c1, st)
+
+    dma("S", A("ut"), ext(T.u[:]))
+    dma("Y", A("xt"), ext(T.x[:]))
+    dma("Y", bytes_(A("qw")), ext(T.wc[:]))
+    dma("Y", A("sw"), ext(T.ws[:]))
+    dma("Y", A("vt"), ext(T.v[:]))
+
+    iota(A("ci", 48, 49), [[0, 1]], 0, 1)
+    gfill(A("one"), 128, 1)
+    sel(A("idn"), A("one"), [[-1, 128]], OP.is_equal, 0.0, 0, 1)
+    iota(A("ci", 0, 8), [[16, 8]], 0)
+    iota(A("ci", 8, 24), [[16, 2], [32, 4], [0, 2]], 0)
+    iota(A("ci", 24, 48), [[1, 24]], 0)
+    iota(A("cf", 0, 32), [[1, 32]], 0)
+    iota(A("cf", 32, 64), [[0, 16], [1, 2]], 0)
+    fill(A("et"), 0.0)
+    for i, m in enumerate((31, 1, 16, 15)):
+        ts(A("cj", i, i + 1), A("ci", 48, 49), m, OP.bitwise_and)
+    cp(A("col", 0, 4), A("cj", 0, 4))
+    fill(A("gt"), 0.0)
+    for a in range(4):
+        fill(A("gt", 128 * a, 128 * a + 64, 2, 32 * a, 32 * a + 32), 1.0)
+        fill(A("gt", 128 * a + 65, 128 * a + 128, 2, 32 * a, 32 * a + 32), 1.0)
+    for b in range(4):
+        act(A("et", 512 * b + b, 512 * (b + 1), 4), A("idn"), FN.Copy)
+    cp(A("offc"), A("ci", 0, 48))
+    quant(A("qg"), A("sg"), A("gt"))
+    fill(A("stl", 24, 32), -FAR)
+    (n_, par_, h16, q_, pm0, me, mo, e1000, z0, z1, me11, mo11, nh16, sgn, npar, c192, ccol, vb, me2k) = (A("col", i, i + 1) for i in range(19))
+    pm = [pm0, par_]
+    xr, xpar, same, s1000, bcol = A("cf", 0, 32), A("cf", 32, 64), A("cf", 64, 96), A("cf", 96, 128), A("m2t", 0, 1)
+    lin(pm0, par_, -1.0, 1.0)
+    lin(sgn, par_, 2.0, -1.0)
+    lin(npar, par_, -1.0 / 128)
+    lin(me, h16, -0.0625, 1.0)
+    lin(mo, h16, 0.0625)
+    lin(same, xpar, sgn, pm0)
+    lin(bcol, n_, 1.0 / 128, npar)
+    lin(A("m2t", 129, 130), n_, 1.0 / 128, npar)
+    lin(s1000, same, 1000.0, -1000.0)
+    quant(A("qu"), A("su"), A("ut"))
+    cp(words(A("qup")), ind(words(A("qu")), A("offc", 0, 24)))
+    act(A("sup"), ind(A("su"), A("offc", 0, 24)), FN.Copy)
+    quant(A("qe"), A("se"), A("et"))
+    lin(A("msame"), same, FAR, -FAR)
+    lin(A("mall"), same, 1809.0, -1000.0)
+    lin(c192, bcol, 1.0, 192.0)
+    lin(ccol, bcol, 2049.0, 192.0)
+    lin(e1000, h16, -62.5, 1000.0)
+    lin(z0, h16, 12.0)
+    lin(z1, h16, -12.0, 192.0)
+    lin(me11, h16, -2.0 ** -15, 2.0 ** -11)
+    lin(mo11, h16, 2.0 ** -15)
+    lin(nh16, h16, -1.0)
+    lin(vb, n_, 1.0, -2048.0)
+    lin(me2k, h16, -128.0, 2048.0)
+    lin(A("ci2", 60, 72), A("cf", 0, 12), 16.0, q_)
+
+    def late_constants():
+        ident = A("ci2", 60, 72)
+        lin(A("cc"), xr, 1.0, ccol)
+        lin(A("ci2", 0, 12), ident, 1.0, 1000.0)
+        lin(A("ci2", 12, 36, 2), ident, me, z0)
+        lin(A("ci2", 13, 36, 2), ident, mo, z1)
+        lin(A("ci2", 36, 60, 2), ident)
+        lin(A("ci2", 37, 60, 2), ident)
+        lin(A("idl"), A("ci2", 0, 12), me2k)
+
+    gfill(A("rs", 0, 12), 12, 192)
+    gfill(A("tk", 320, 384), 64, 0)
+    gfill(A("kt", 24, 32), 8, 1000)
+    gfill(A("rst"), 99, 1)
+    gfill(A("fl", 0, 99, 33), 3, 0)
+    gfill(A("rst", 0, 99, 33), 3, 0)
+    for a in range(4):
+        blk = (32 * a, 32 * a + 32)
+        for out, src, pat, op, other, mult in (("mlt", 64, 1, OP.is_gt, 0.0, -1), ("mge", 64, -1, OP.is_ge, 0.0, 1),
+                                               ("mltn", 96, 1, OP.is_gt, -1000.0, -1)):
+            wait("G", "cG", count["cG"])
+            sel(A(out, 0, 32, 1, *blk), A("cf", src, src + 32, 1, *blk), [[pat, 32]], op, other, 0, mult)
+    wait("G", "cG", count["cG"])
+    gfill(A("ee"), 32, 0)
+    gfill(A("nl", 0, 1), 1, 0)
+    gfill(A("wa", 0, 16), 16, 0)
+    gfill(A("wd", 192, 200), 8, 0)
+    iota(A("kv"), [[1, 192]], 384)
+    iota(A("pre"), [[1, 400]], 0)
+
+    def E(b):
+        return A("qe", 128 * b, 128 * b + 128), A("se", 128 * b, 128 * b + 128)
+
+    def U(i):
+        return A("qup", 128 * i, 128 * i + 128), A("sup", 128 * i, 128 * i + 128)
+
+    def X(n, c0=0):
+        return A("qx", c0, n), A("sx", c0, n)
+
+    cbase = {10: 0, 8: 1536, 6: 2816, 0: 3840, 2: 4608, 4: 5376}
+    qbase = {10: 0, 8: 320, 6: 576, 0: 768, 2: 960, 4: 1152}
+    width = {10: 320, 8: 256, 6: 192, 0: 192, 2: 192, 4: 192}
+    count["sent"] = 0
+
+    def shared(c):
+        r = T.rank_of(c)
+        sets = [topo.engines(c, T.cores[r ^ e]) for e in STEP]
+        return [x for x in sets[0] if all(x in s for s in sets)]
+
+    quant(A("qx"), A("sx"), A("xt"))
+    for rnd, e in enumerate(STEP):
+        peer = T.cores[rank ^ e]
+        mm(0, 384, *U(0), *X(384))
+        mm(1, 384, *U(1), *X(384))
+        mm(3, 192, *U(1), *X(192))
+        mm(2, 384, *U(2), *X(384))
+        mm(4, 192, *U(2), *X(192))
+        mm(6, 384, *E(0), *X(384))
+        mm(7, 384, *E(1), *X(384))
+        tr(A("ts", 320, 384), P(0, 320, 384))
+        tr(A("ts", 0, 192), P(0, 0, 192))
+        tr(A("ts", 192, 320), P(0, 192, 320))
+
+        def srows(b0):
+            w = 32 * (b0 + 2)
+            for t in (0, 2, 1, 3):
+                n = 2 * b0 + t
+                act(A("cmp", cbase[b0] + t, cbase[b0] + 4 * w, 4), P(1 + t % 2, 0, w), FN.Sign,
+                    bias=A("ts", 16 * n, 16 * n + 1), scale=-1.0, accum=A("rs", n, n + 1))
+
+        def vrows(b0):
+            for t in (0, 2, 1, 3):
+                n = 2 * b0 + t
+                ts(A("cmp", cbase[b0] + t, cbase[b0] + 768, 4), P(3 + t % 2, 0, 192), A("ts", 16 * n, 16 * n + 1), OP.is_lt, 2.0, OP.mult)
+
+        def cq(b0):
+            return A("qc", qbase[b0], qbase[b0] + width[b0]), A("sc", qbase[b0], qbase[b0] + width[b0])
+
+        def cquant(b0):
+            quant(*cq(b0), A("cmp", cbase[b0], cbase[b0] + 4 * width[b0]))
+
+        def csum(b0, start=False, stop=False):
+            mm(5, width[b0], A("qg"), A("sg"), *cq(b0), start, stop)
+
+        def unpack(b, bank):
+            act(A("fz", 576 * b, 576 * b + 384), P(bank, 0, 384), FN.Copy)
+
+        srows(10)
+        vrows(0)
+        srows(8)
+        vrows(2)
+        cquant(0)
+        cquant(10)
+        cquant(2)
+        csum(10, start=True)
+        csum(0)
+        csum(2)
+        srows(6)
+        vrows(4)
+        cquant(8)
+        cquant(4)
+        csum(8)
+        csum(4)
+        cp(A("stl", 0, 24), A("ts", 0, 384, 16))
+        tr(A("sml"), A("stl"))
+        cquant(6)
+        csum(6, stop=True)
+        mm(1, 384, *E(2), *X(384))
+        mm(2, 384, *E(3), *X(384))
+        if rnd == 0:
+            late_constants()
+        unpack(0, 6)
+        if rnd:
+            unpack(1, 7)
+        tr(A("tk", 0, 320), P(5, 0, 320))
+        tt(A("kt", 0, 24), A("tk", 0, 384, 16), A("rs"), OP.subtract)
+        tr(A("km"), A("kt"))
+        ts(A("ww"), A("km"), 0.5, OP.add, BIG, OP.mult)
+        tt(A("yy", 32, 64), A("sml"), A("ww"), OP.max)
+        tt(A("yy", 0, 32), A("sml"), A("ww"), OP.min)
+        red(A("r1", 1, 2), A("yy", 32, 64), OP.min, True)
+        red(A("r1", 0, 1), A("yy", 0, 32), OP.max)
+        lin(A("m1", 32, 64), A("msame"), None, A("r1", 1, 2))
+        ts(A("m1", 0, 32), A("msame"), A("r1", 0, 1), OP.add)
+        if rnd == 0:
+            unpack(1, 7)
+        tr(A("m1t"), A("m1"))
+        red(A("ab", 1, 2), A("m1t", 32, 64), OP.max, True)
+        red(A("ab", 0, 1), A("m1t", 0, 32), OP.max)
+        ts(A("fl", 1, 33), A("sml"), A("ab", 1, 2), OP.is_gt)
+        ts(A("fl", 34, 66), A("sml"), A("ab", 1, 2), OP.is_ge)
+        ts(A("fl", 67, 99), A("sml"), A("ab", 0, 1), OP.is_ge)
+        scan(A("cum"), A("rst"), A("fl"), 0.0, OP.mult, OP.add)
+        lin(A("m2", 0, 32), A("mlt"), A("cum", 65, 66))
+        lin(A("m2", 96, 128), A("mlt"), A("cum", 98, 99))
+        ts(A("m2", 32, 64), A("mge"), A("cum", 32, 33), OP.mult)
+        ts(A("m2", 64, 96), A("mge"), A("cum", 65, 66), OP.mult)
+        tr(A("m2t", 1, 129), A("m2"))
+        lin(A("junk", 0, 33), A("m2t", 0, 33), accum=A("kk", 2, 3))
+        lin(A("junk", 33, 66), A("m2t", 97, 130), accum=A("kk", 3, 4))
+        red(A("kk", 0, 1), A("m2t", 33, 65), OP.add)
+        red(A("kk", 1, 2), A("m2t", 65, 97), OP.add)
+        lin(A("cb", 0, 33), A("cum", 33, 66), None, A("kk", 2, 3))
+        lin(A("cb", 33, 66), A("cum", 66, 99), None, A("kk", 3, 4))
+        ts(A("rr", 0, 33), A("cum", 0, 33), A("kk", 0, 1), OP.subtract, c192, OP.add)
+        ts(A("rr", 33, 66), A("cum", 33, 66), A("kk", 1, 2), OP.subtract, c192, OP.add)
+        tt(A("mn", 0, 33), A("rr", 0, 33), A("cb", 0, 33), OP.min)
+        tt(A("mn", 33, 66), A("rr", 33, 66), A("cb", 33, 66), OP.min)
+        tt(A("bb"), A("mn", 0, 33), A("mn", 33, 66), OP.max)
+        bc, bp = A("bb", 1, 33), A("bb", 0, 32)
+        tr(A("bt"), bc)
+        lin(A("w2", 0, 32), bc, -1001.0)
+        lin(A("w2", 32, 64), bp, 1000.0)
+        act(A("vx"), ind(A("bt"), A("offc", 24, 48)), FN.Identity, bias=vb, scale=2048.0)
+        tt(A("ee", 1, 24, 2), A("bt", 1, 24, 2), A("bt", 0, 24, 2), OP.subtract)
+        for a in range(1, 4):
+            tt(A("ee", 0, 24, 2, 32 * a, 32 * a + 32), A("bt", 0, 24, 2, 32 * a, 32 * a + 32),
+               A("bt", 1, 24, 2, 32 * a - 32, 32 * a), OP.subtract)
+        tt(A("w2", 64, 96), A("w2", 0, 32), A("w2", 32, 64), OP.add)
+        tr(A("em"), A("ee"))
+        tt(A("w1", 0, 32), A("w2", 64, 96), A("cc"), OP.add)
+        scan(A("nl", 1, 33), A("em"), A("em"), 0.0, OP.max, OP.max)
+        if rnd == 0:
+            cp(A("off2"), A("ci2", 36, 72))
+        ts(A("m3", 0, 32), A("mltn"), A("nl", 32, 33), OP.add)
+        ts(A("m3", 32, 64), A("mall"), A("nl", 32, 33), OP.add)
+        if rnd == 0:
+            cp(A("off3"), A("ci2", 12, 36))
+        tr(A("m3t"), A("m3"))
+        tr(A("vr", 0, 96), A("vx", 0, 96))
+        red(A("cr", 1, 2), A("m3t", 32, 64), OP.max, True)
+        red(A("cr", 0, 1), A("m3t", 0, 32), OP.max)
+        c0, c1 = A("cr", 0, 1), A("cr", 1, 2)
+        lin(A("w1", 64, 96), A("em"), 1001.0, c1)
+        tr(A("vr", 96, 192), A("vx", 96, 192))
+        ts(A("w1", 32, 64), A("nl", 1, 33), c0, OP.max, 1.0, OP.add)
+        ts(A("w1", 96, 128), A("nl", 0, 32), c0, OP.max, -1000.0, OP.mult)
+        tt(A("w1", 128, 160), bc, A("w1", 32, 64), OP.subtract)
+        tt(A("w1", 160, 192), A("w1", 64, 96), A("w1", 96, 128), OP.add)
+        tt(A("w1", 192, 224), A("w1", 128, 160), A("w1", 0, 32), OP.max)
+        tr(A("vr", 192, 288), A("vx", 192, 288))
+        tt(A("tau"), A("w1", 160, 192), A("w1", 192, 224), OP.max)
+        tr(A("vr", 288, 384), A("vx", 288, 384))
+        for h in range(2):
+            lin(A("tb", 32 * h + 16, 32 * h + 32), A("tau", 16 * h, 16 * h + 16), pm[1])
+            ts(A("tb", 32 * h, 32 * h + 16), A("tau", 16 * h, 16 * h + 16), pm[0], OP.mult)
+        tr(A("tbt"), A("tb"))
+        for h in range(2):
+            tt(A("tl", h, 24, 2), A("tbt", 32 * h, 32 * h + 24, 2), A("tbt", 32 * h + 1, 32 * h + 24, 2), OP.add)
+        cp(A("offs"), A("tl"))
+        unpack(2, 1)
+        unpack(3, 2)
+        cp(ind(A("wa", 16, 400), A("offs")), A("vr"))
+
+        def spread(win, off):
+            act(A("ds", 192, 384), ind(win, A(off, 12, 24)), FN.Copy)
+            cp(A("ds", 0, 192), ind(win, A(off, 0, 12)))
+
+        def compact(out, win, off):
+            act(out, ind(win, A(off, 24, 36)), FN.Copy)
+            tr(A("dst"), A("ds"))
+
+        tr(A("ta", 0, 192), A("wa", 0, 192))
+        tr(A("ta", 192, 384), A("wa", 16, 208))
+        for h in range(2):
+            tt(A("l1", h, 12, 2), A("ta", 192 * h, 192 * h + 192, 32), A("idl", h, 12, 2), OP.max)
+        for d in range(2):
+            ts(A("off1", d, 24, 2), A("l1"), 2.0 ** -11, OP.mult, e1000, OP.subtract)
+        spread(A("wa", 16, 208), "off1")
+        ts(A("off1", 24, 36), A("l1"), 2.0 ** -11, OP.mult, e1000, OP.subtract)
+        compact(A("wb"), A("wa", 16, 208), "off1")
+        for d in range(2):
+            ts(A("off2", d, 24, 2, 32, 64), A("dst", 16, 384, 32, 0, 32), 2.0 ** -11, OP.mult)
+        spread(A("wb"), "off2")
+        for a in (1, 3):
+            ts(A("off2", 24, 36, 1, 32 * a, 32 * a + 32), A("dst", 16, 384, 32, 32 * a - 32, 32 * a), 2.0 ** -11, OP.mult)
+        compact(A("wd", 0, 192), A("wb"), "off2")
+        for d in range(2):
+            for a in (2, 3):
+                ts(A("off3", d, 24, 2, 32 * a, 32 * a + 32), A("dst", 16, 384, 32, 32, 64),
+                   A("col", 10 + d, 11 + d, 1, 32, 64), OP.mult, A("col", 8 + d, 9 + d, 1, 32, 64), OP.add)
+        act(A("we", 192, 384), ind(A("wd"), A("off3", 12, 24)), FN.Copy)
+        cp(A("we", 0, 192), ind(A("wd"), A("off3", 0, 12)))
+        tr(A("tc"), A("we"))
+        tt(A("fi", 0, 12), A("tc", 0, 384, 32), A("tc", 16, 384, 32), OP.add)
+        ts(A("fi", 12, 24), A("fi", 0, 12), 2047, OP.bitwise_and)
+        cp(A("offz"), A("fi", 12, 24))
+        for b in (2, 0, 3, 1):
+            src = ind(A("fz", 576 * b, 576 * b + 384), A("offz"))
+            if b >= 2:
+                act(A("zt", b, 768, 4), src, FN.Copy)
+            else:
+                cp(A("zt", b, 768, 4), src)
+        quant(A("qz"), A("sz"), A("zt"))
+        wbank = (3, 4, 5, 0)
+        for b in range(4):
+            mm(wbank[b], 192, A("qw", 128 * b, 128 * b + 128), A("sw", 128 * b, 128 * b + 128), A("qz"), A("sz"))
+        for b in range(4):
+            if b % 2 == 0:
+                act(A("ht", b, 768, 4), P(wbank[b], 0, 192), FN.Relu, scale=0.015625)
+            else:
+                ts(A("ht", b, 768, 4), P(wbank[b], 0, 192), 0.0, OP.max, 0.015625, OP.mult)
+        qh, sh, ql, sl = ("%s%d" % (s, rnd) for s in ("qh", "sh", "ql", "sl"))
+        quant(A(qh), A(sh), A("ht"))
+        eng = shared(core)
+        mask = sum(1 << x for x in eng)
+        rid, pid = topo.addr(peer)[:2]
+        arr = "arr%d" % rnd
+        for src, dst in ((bytes_(A(qh)), bytes_(A(ql))), (A(sh), A(sl))):
+            count["sent"] += len(eng)
+            issue("G", lambda: g.remote_dma(dst[0], src[0], T.sem[arr], T.sem["sent"], pid, rid, mask), [], [src], sem="sent", inc=0)
+        count[arr] = 2 * len(shared(peer))
+        ts(A("offi"), A("fi", 12, 24), h16, OP.add)
+        lin(A("iw"), A("pre"), None, nh16)
+        cp(ind(A("iw"), A("offi")), A("kv"))
+        tr(A("ta"), A("iw", 0, 384))
+        tr(A("tc"), A("iw", 16, 400))
+        for h, t in enumerate(("ta", "tc")):
+            ts(A("ib", 24 * h, 24 * h + 12), A(t, 0, 384, 32), me, OP.mult)
+            lin(A("ib", 24 * h + 12, 24 * h + 24), A(t, 16, 384, 32), mo)
+        for h in range(2):
+            tt(A("ib", 48 + h, 72, 2), A("ib", 24 * h, 24 * h + 12), A("ib", 24 * h + 12, 24 * h + 24), OP.add)
+        cp(A("offx"), A("ib", 48, 72))
+        if rnd == 1:
+            quant(A("qv"), A("sv"), A("vt"))
+        if rnd == 2:
+            act(A("plr"), ind(A("pre"), A("offz")), FN.Copy)
+            for l in range(8):
+                dma("Y", ext(T.pl[l:l + 1, :]), A("plr", 0, 192, 1, 16 * l, 16 * l + 1))
+        wait("P", arr, count[arr])
+        dbank = (1, 2, 6, 7)
+        for b in range(4):
+            mm(dbank[b], 192, *E(b), A(ql), A(sl))
+        for b in range(4):
+            tt(A("fz", 576 * b + 384, 576 * b + 576), P(dbank[b], 0, 192), A("zt", b, 768, 4), OP.add)
+            if b < 2:
+                act(A("xn", b, 1536, 4), ind(A("fz", 576 * b, 576 * b + 576), A("offx")), FN.Copy)
+        act(A("xn", 2, 768, 4), ind(A("fz", 1152, 1728), A("offx", 0, 12)), FN.Copy)
+        cp(A("xn", 3, 1536, 4), ind(A("fz", 1728, 2304), A("offx")))
+        cp(A("xn", 770, 1536, 4), ind(A("fz", 1152, 1728), A("offx", 12, 24)))
+        quant(A("qx"), A("sx"), A("xn"))
+
+    mm(0, 192, A("qv"), A("sv"), *X(192))
+    mm(3, 192, A("qv"), A("sv"), *X(384, 192))
+    dma("Y", ext(T.oc[:]), bytes_(A("qx")))
+    for a in range(4):
+        dma("Y", ext(T.osc[4 * a:4 * a + 4, :]), A("sx", 0, 384, 1, 32 * a, 32 * a + 4))
+    act(A("yo", 0, 192), P(0, 0, 192), FN.Copy)
+    cp(A("yo", 192, 384), P(3, 0, 192))
+    dma("S", ext(T.y[:]), A("yo"))
+    for s in sorted(count):
+        if count[s]:
+            g.wait_ge(T.sem[s], count[s])

@@ -16,27 +16,27 @@ SCRATCH = {
     "et": _sb(2048, BF), "qe": _sb(512, Q4), "se": _sb(512, U8), "idn": _sb(128, BF), "one": _sb(128, BF),
     "gt": _sb(512, BF), "qg": _sb(128, Q4), "sg": _sb(128, U8),
     "ci": _sb(64, I32), "cj": _sb(4, I32), "cf": _sb(128, F32), "col": _sb(24, F32), "offc": _sb(48, U16),
-    "msame": _sb(32, F32), "mge": _sb(32, F32), "mlt": _sb(32, F32), "mltn": _sb(32, F32), "mall": _sb(32, F32),
-    "cc": _sb(32, F32), "idl": _sb(12, F32), "rst": _sb(99, F32), "ci2": _sb(72, F32),
+    "mge": _sb(32, F32), "mlt": _sb(32, F32), "mltn": _sb(32, F32), "mall": _sb(32, F32),
+    "cc": _sb(32, F32), "rst": _sb(99, F32), "ci2": _sb(84, F32), "lr": _sb(192, F32), "offk": _sb(6, U16),
     "kv": _sb(192, F32), "pre": _sb(400, F32),
-    "ts": _sb(384, F32), "rs": _sb(24, F32), "tk": _sb(384, F32),
-    "stl": _sb(32, F32), "sml": _sb(32, F32), "kt": _sb(32, F32), "km": _sb(32, F32), "ww": _sb(32, F32),
-    "yy": _sb(64, F32), "r1": _sb(2, F32), "m1": _sb(64, F32), "m1t": _sb(64, F32), "ab": _sb(2, F32),
+    "ts": _sb(384, F32), "rs": _sb(72, F32), "tk": _sb(384, F32), "dg": _sb(1024, BF),
+    "stl": _sb(32, F32), "sml": _sb(32, F32), "kt": _sb(24, F32), "ww": _sb(24, F32),
+    "yy": _sb(48, F32), "r1": _sb(4, F32), "m1": _sb(64, F32), "m1t": _sb(64, F32), "ab": _sb(2, F32),
     "fl": _sb(99, F32), "cum": _sb(99, F32), "m2": _sb(128, F32), "m2t": _sb(130, F32), "kk": _sb(4, F32),
-    "junk": _sb(66, F32), "rr": _sb(66, F32), "cb": _sb(66, F32), "mn": _sb(66, F32), "bb": _sb(33, F32),
+    "junk": _sb(66, F32), "sa": _sb(99, F32), "sb": _sb(99, F32), "bb": _sb(99, F32),
     "bt": _sb(32, F32), "ee": _sb(32, F32), "em": _sb(32, F32), "nl": _sb(33, F32),
     "m3": _sb(64, F32), "m3t": _sb(64, F32), "cr": _sb(2, F32),
     "w1": _sb(256, F32), "w2": _sb(96, F32),
-    "tau": _sb(32, F32), "tb": _sb(64, F32), "tbt": _sb(64, F32), "tl": _sb(24, F32), "offs": _sb(24, U16),
+    "tau": _sb(64, F32), "tbt": _sb(96, F32), "offs": _sb(32, U16),
     "vx": _sb(384, F32), "vr": _sb(384, F32),
-    "wa": _sb(400, F32), "wb": _sb(192, F32), "wd": _sb(200, F32), "we": _sb(384, F32),
+    "wa": _sb(800, F32), "wd": _sb(200, F32), "we": _sb(384, F32),
     "ds": _sb(384, BF), "dst": _sb(384, BF),
-    "ta": _sb(384, F32), "tc": _sb(384, F32), "l1": _sb(12, F32),
-    "off1": _sb(36, U16), "off2": _sb(36, U16), "off3": _sb(24, U16),
+    "ta": _sb(384, F32), "tc": _sb(384, F32),
+    "off1": _sb(48, U16), "off2": _sb(36, U16), "off3": _sb(24, U16),
     "fi": _sb(24, I32), "offz": _sb(12, U16), "offi": _sb(12, U16), "offx": _sb(24, U16),
     "iw": _sb(400, F32), "ib": _sb(72, F32),
     "fz": _sb(4 * 576, BF), "zt": _sb(768, BF), "qz": _sb(192, Q4), "sz": _sb(192, U8), "ht": _sb(768, BF),
-    "cmp": _sb(4 * (384 + 320 + 256 + 3 * 192), BF), "qc": _sb(320 + 256 + 4 * 192, Q4), "sc": _sb(320 + 256 + 4 * 192, U8),
+    "cmp": _sb(4 * 1280, BF), "qc": _sb(1280, Q4), "sc": _sb(1280, U8),
     "plr": _sb(192, F32), "yo": _sb(384, F32),
 }
 for _r in range(3):
@@ -226,59 +226,60 @@ def rank_program(g, core, T, topo):
     fill(A("et"), 0.0)
     for i, m in enumerate((31, 1, 16, 15)):
         ts(A("cj", i, i + 1), A("ci", 48, 49), m, OP.bitwise_and)
-    cp(A("col", 0, 4), A("cj", 0, 4))
     fill(A("gt"), 0.0)
+    cp(A("col", 0, 4), A("cj", 0, 4))
     for a in range(4):
         fill(A("gt", 128 * a, 128 * a + 64, 2, 32 * a, 32 * a + 32), 1.0)
         fill(A("gt", 128 * a + 65, 128 * a + 128, 2, 32 * a, 32 * a + 32), 1.0)
     for b in range(4):
         act(A("et", 512 * b + b, 512 * (b + 1), 4), A("idn"), FN.Copy)
     cp(A("offc"), A("ci", 0, 48))
-    quant(A("qg"), A("sg"), A("gt"))
     fill(A("stl", 24, 32), -FAR)
-    (n_, par_, h16, q_, pm0, me, mo, e1000, z0, z1, me11, mo11, nh16, sgn, npar, c192, ccol, vb, me2k) = (A("col", i, i + 1) for i in range(19))
-    pm = [pm0, par_]
+    quant(A("qe"), A("se"), A("et"))
+    (n_, par_, h16, q_, pm0, me, mo, b592, z0, z1, me11, mo11, nh16, sgn, npar, c192, ccol, vb, k1, k2, k3) = (A("col", i, i + 1) for i in range(21))
     xr, xpar, same, s1000, bcol = A("cf", 0, 32), A("cf", 32, 64), A("cf", 64, 96), A("cf", 96, 128), A("m2t", 0, 1)
     lin(pm0, par_, -1.0, 1.0)
     lin(sgn, par_, 2.0, -1.0)
     lin(npar, par_, -1.0 / 128)
     lin(me, h16, -0.0625, 1.0)
     lin(mo, h16, 0.0625)
+    lin(k1, par_, 31.0, q_)
     lin(same, xpar, sgn, pm0)
     lin(bcol, n_, 1.0 / 128, npar)
     lin(A("m2t", 129, 130), n_, 1.0 / 128, npar)
+    lin(k2, h16, -31.0 / 16, k1)
     lin(s1000, same, 1000.0, -1000.0)
     quant(A("qu"), A("su"), A("ut"))
+    quant(A("qg"), A("sg"), A("gt"))
     cp(words(A("qup")), ind(words(A("qu")), A("offc", 0, 24)))
     act(A("sup"), ind(A("su"), A("offc", 0, 24)), FN.Copy)
-    quant(A("qe"), A("se"), A("et"))
-    lin(A("msame"), same, FAR, -FAR)
     lin(A("mall"), same, 1809.0, -1000.0)
     lin(c192, bcol, 1.0, 192.0)
-    lin(ccol, bcol, 2049.0, 192.0)
-    lin(e1000, h16, -62.5, 1000.0)
+    lin(ccol, bcol, -2048.0, 578.0)
+    lin(k3, k2, 1.0, 32.0)
+    lin(b592, h16, 37.0)
     lin(z0, h16, 12.0)
     lin(z1, h16, -12.0, 192.0)
     lin(me11, h16, -2.0 ** -15, 2.0 ** -11)
     lin(mo11, h16, 2.0 ** -15)
     lin(nh16, h16, -1.0)
     lin(vb, n_, 1.0, -2048.0)
-    lin(me2k, h16, -128.0, 2048.0)
-    lin(A("ci2", 60, 72), A("cf", 0, 12), 16.0, q_)
+    lin(A("ci2", 0, 12), A("cf", 0, 12), 16.0, q_)
+    lin(A("cc"), xr, -1.0, ccol)
+    lin(A("ci2", 72, 74), A("cf", 0, 2), 16.0, k3)
 
     def late_constants():
-        ident = A("ci2", 60, 72)
-        lin(A("cc"), xr, 1.0, ccol)
-        lin(A("ci2", 0, 12), ident, 1.0, 1000.0)
+        ident = A("ci2", 0, 12)
         lin(A("ci2", 12, 36, 2), ident, me, z0)
         lin(A("ci2", 13, 36, 2), ident, mo, z1)
-        lin(A("ci2", 36, 60, 2), ident)
-        lin(A("ci2", 37, 60, 2), ident)
-        lin(A("idl"), A("ci2", 0, 12), me2k)
+        lin(A("ci2", 36, 60, 2), ident, None, b592)
+        lin(A("ci2", 37, 60, 2), ident, None, b592)
+        lin(A("ci2", 60, 72), ident, None, b592)
 
-    gfill(A("rs", 0, 12), 12, 192)
+    gfill(A("rs", 0, 8), 8, 192)
+    gfill(A("rs", 8, 12), 4, 128)
+    gfill(A("rs", 24, 32), 8, 0)
     gfill(A("tk", 320, 384), 64, 0)
-    gfill(A("kt", 24, 32), 8, 1000)
     gfill(A("rst"), 99, 1)
     gfill(A("fl", 0, 99, 33), 3, 0)
     gfill(A("rst", 0, 99, 33), 3, 0)
@@ -289,9 +290,15 @@ def rank_program(g, core, T, topo):
             wait("G", "cG", count["cG"])
             sel(A(out, 0, 32, 1, *blk), A("cf", src, src + 32, 1, *blk), [[pat, 32]], op, other, 0, mult)
     wait("G", "cG", count["cG"])
+    gfill(A("sa", 0, 99, 3), 33, 5000)
+    gfill(A("sa", 2, 99, 3), 33, -5000)
     gfill(A("ee"), 32, 0)
     gfill(A("nl", 0, 1), 1, 0)
-    gfill(A("wa", 0, 16), 16, 0)
+    iota(A("lr", 0, 32), [[0, 2], [32, 8], [192, 2]], 0)
+    for i in range(4):
+        iota(A("lr", 32 + 16 * i, 48 + 16 * i), [[32, 4], [192, 2], [0, 2]], 128 * (i // 2))
+    gfill(A("tau"), 64, 0)
+    gfill(A("wa"), 800, 0)
     gfill(A("wd", 192, 200), 8, 0)
     iota(A("kv"), [[1, 192]], 384)
     iota(A("pre"), [[1, 400]], 0)
@@ -305,9 +312,8 @@ def rank_program(g, core, T, topo):
     def X(n, c0=0):
         return A("qx", c0, n), A("sx", c0, n)
 
-    cbase = {10: 0, 8: 1536, 6: 2816, 0: 3840, 2: 4608, 4: 5376}
     qbase = {10: 0, 8: 320, 6: 576, 0: 768, 2: 960, 4: 1152}
-    width = {10: 320, 8: 256, 6: 192, 0: 192, 2: 192, 4: 192}
+    width = {10: 320, 8: 256, 6: 192, 0: 192, 2: 192, 4: 128}
     count["sent"] = 0
 
     def shared(c):
@@ -329,23 +335,31 @@ def rank_program(g, core, T, topo):
         tr(A("ts", 0, 192), P(0, 0, 192))
         tr(A("ts", 192, 320), P(0, 192, 320))
 
+        def slot(b0, t):
+            return A("cmp", 4 * qbase[b0] + t, 4 * (qbase[b0] + width[b0]), 4)
+
         def srows(b0):
-            w = 32 * (b0 + 2)
             for t in (0, 2, 1, 3):
                 n = 2 * b0 + t
-                act(A("cmp", cbase[b0] + t, cbase[b0] + 4 * w, 4), P(1 + t % 2, 0, w), FN.Sign,
+                act(slot(b0, t), P(1 + t % 2, 0, width[b0]), FN.Sign,
                     bias=A("ts", 16 * n, 16 * n + 1), scale=-1.0, accum=A("rs", n, n + 1))
+
+        def sdiag(b0):
+            for t in (0, 2, 1, 3):
+                n = 2 * b0 + t
+                act(A("dg", 64 * (n - 8), 64 * (n - 7)), P(1 + t % 2, 32 * b0, 32 * b0 + 64), FN.Sign,
+                    bias=A("ts", 16 * n, 16 * n + 1), scale=-1.0, accum=A("rs", 24 + n, 25 + n))
 
         def vrows(b0):
             for t in (0, 2, 1, 3):
                 n = 2 * b0 + t
-                ts(A("cmp", cbase[b0] + t, cbase[b0] + 768, 4), P(3 + t % 2, 0, 192), A("ts", 16 * n, 16 * n + 1), OP.is_lt, 2.0, OP.mult)
+                ts(slot(b0, t), P(3 + t % 2, 0, width[b0]), A("ts", 16 * n, 16 * n + 1), OP.is_lt, 2.0, OP.mult)
 
         def cq(b0):
             return A("qc", qbase[b0], qbase[b0] + width[b0]), A("sc", qbase[b0], qbase[b0] + width[b0])
 
         def cquant(b0):
-            quant(*cq(b0), A("cmp", cbase[b0], cbase[b0] + 4 * width[b0]))
+            quant(*cq(b0), A("cmp", 4 * qbase[b0], 4 * (qbase[b0] + width[b0])))
 
         def csum(b0, start=False, stop=False):
             mm(5, width[b0], A("qg"), A("sg"), *cq(b0), start, stop)
@@ -359,41 +373,44 @@ def rank_program(g, core, T, topo):
         vrows(2)
         cquant(0)
         cquant(10)
-        cquant(2)
         csum(10, start=True)
         csum(0)
-        csum(2)
         srows(6)
         vrows(4)
+        cquant(2)
         cquant(8)
         cquant(4)
+        csum(2)
         csum(8)
         csum(4)
-        cp(A("stl", 0, 24), A("ts", 0, 384, 16))
-        tr(A("sml"), A("stl"))
         cquant(6)
         csum(6, stop=True)
+        for b0 in (4, 6, 8, 10):
+            sdiag(b0)
+        cp(A("stl", 0, 24), A("ts", 0, 384, 16))
         mm(1, 384, *E(2), *X(384))
         mm(2, 384, *E(3), *X(384))
+        unpack(0, 6)
+        tr(A("tk", 0, 320), P(5, 0, 320))
+        tr(A("sml"), A("stl"))
+        tt(A("rs", 48, 72), A("rs", 0, 24), A("rs", 24, 48), OP.add)
+        tt(A("kt"), A("tk", 0, 384, 16), A("rs", 48, 72), OP.subtract)
+        ts(A("ww"), A("kt"), 0.5, OP.add, BIG, OP.mult)
+        tt(A("yy", 24, 48), A("stl", 0, 24), A("ww"), OP.max)
+        tt(A("yy", 0, 24), A("stl", 0, 24), A("ww"), OP.min)
+        for p in range(2):
+            red(A("r1", 2 + p, 3 + p), A("yy", 24 + p, 48, 2), OP.min)
+        for p in range(2):
+            red(A("r1", p, p + 1), A("yy", p, 24, 2), OP.max)
+        for p in range(2):
+            lin(A("m1", 32 + p, 64, 2), A("cf", 0, 16), 0.0, A("r1", 2 + p, 3 + p))
+        for p in range(2):
+            ts(A("m1", p, 32, 2), A("cf", 0, 16), 0.0, OP.mult, A("r1", p, p + 1), OP.add)
+        unpack(1, 7)
         if rnd == 0:
             late_constants()
-        unpack(0, 6)
-        if rnd:
-            unpack(1, 7)
-        tr(A("tk", 0, 320), P(5, 0, 320))
-        tt(A("kt", 0, 24), A("tk", 0, 384, 16), A("rs"), OP.subtract)
-        tr(A("km"), A("kt"))
-        ts(A("ww"), A("km"), 0.5, OP.add, BIG, OP.mult)
-        tt(A("yy", 32, 64), A("sml"), A("ww"), OP.max)
-        tt(A("yy", 0, 32), A("sml"), A("ww"), OP.min)
-        red(A("r1", 1, 2), A("yy", 32, 64), OP.min, True)
-        red(A("r1", 0, 1), A("yy", 0, 32), OP.max)
-        lin(A("m1", 32, 64), A("msame"), None, A("r1", 1, 2))
-        ts(A("m1", 0, 32), A("msame"), A("r1", 0, 1), OP.add)
-        if rnd == 0:
-            unpack(1, 7)
         tr(A("m1t"), A("m1"))
-        red(A("ab", 1, 2), A("m1t", 32, 64), OP.max, True)
+        red(A("ab", 1, 2), A("m1t", 32, 64), OP.min)
         red(A("ab", 0, 1), A("m1t", 0, 32), OP.max)
         ts(A("fl", 1, 33), A("sml"), A("ab", 1, 2), OP.is_gt)
         ts(A("fl", 34, 66), A("sml"), A("ab", 1, 2), OP.is_ge)
@@ -408,18 +425,18 @@ def rank_program(g, core, T, topo):
         lin(A("junk", 33, 66), A("m2t", 97, 130), accum=A("kk", 3, 4))
         red(A("kk", 0, 1), A("m2t", 33, 65), OP.add)
         red(A("kk", 1, 2), A("m2t", 65, 97), OP.add)
-        lin(A("cb", 0, 33), A("cum", 33, 66), None, A("kk", 2, 3))
-        lin(A("cb", 33, 66), A("cum", 66, 99), None, A("kk", 3, 4))
-        ts(A("rr", 0, 33), A("cum", 0, 33), A("kk", 0, 1), OP.subtract, c192, OP.add)
-        ts(A("rr", 33, 66), A("cum", 33, 66), A("kk", 1, 2), OP.subtract, c192, OP.add)
-        tt(A("mn", 0, 33), A("rr", 0, 33), A("cb", 0, 33), OP.min)
-        tt(A("mn", 33, 66), A("rr", 33, 66), A("cb", 33, 66), OP.min)
-        tt(A("bb"), A("mn", 0, 33), A("mn", 33, 66), OP.max)
-        bc, bp = A("bb", 1, 33), A("bb", 0, 32)
+        lin(A("sa", 1, 99, 3), A("cum", 33, 66), None, A("kk", 2, 3))
+        lin(A("sb", 2, 99, 3), A("cum", 66, 99), None, A("kk", 3, 4))
+        ts(A("sb", 1, 99, 3), A("cum", 0, 33), A("kk", 0, 1), OP.subtract, c192, OP.add)
+        ts(A("sb", 0, 99, 3), A("cum", 33, 66), A("kk", 1, 2), OP.subtract, c192, OP.add)
+        scan(A("bb"), A("sa"), A("sb"), 0.0, OP.max, OP.min)
+        bc, bp = A("bb", 5, 99, 3), A("bb", 2, 96, 3)
         tr(A("bt"), bc)
-        lin(A("w2", 0, 32), bc, -1001.0)
+        lin(A("w2", 0, 32), bc, -999.0)
         lin(A("w2", 32, 64), bp, 1000.0)
         act(A("vx"), ind(A("bt"), A("offc", 24, 48)), FN.Identity, bias=vb, scale=2048.0)
+        if rnd == 0:
+            tr(A("lr", 96, 192), A("lr", 0, 96))
         tt(A("ee", 1, 24, 2), A("bt", 1, 24, 2), A("bt", 0, 24, 2), OP.subtract)
         for a in range(1, 4):
             tt(A("ee", 0, 24, 2, 32 * a, 32 * a + 32), A("bt", 0, 24, 2, 32 * a, 32 * a + 32),
@@ -427,12 +444,15 @@ def rank_program(g, core, T, topo):
         tt(A("w2", 64, 96), A("w2", 0, 32), A("w2", 32, 64), OP.add)
         tr(A("em"), A("ee"))
         tt(A("w1", 0, 32), A("w2", 64, 96), A("cc"), OP.add)
-        scan(A("nl", 1, 33), A("em"), A("em"), 0.0, OP.max, OP.max)
         if rnd == 0:
-            cp(A("off2"), A("ci2", 36, 72))
+            ts(A("offk", 2, 5), A("lr", 96, 192, 32), 383.0, OP.min)
+            cp(A("offk", 0, 2), A("ci2", 72, 74))
+        scan(A("nl", 1, 33), A("em"), A("em"), 0.0, OP.max, OP.max)
+        tt(A("w1", 192, 224), A("w1", 0, 32), bc, OP.max)
         ts(A("m3", 0, 32), A("mltn"), A("nl", 32, 33), OP.add)
         ts(A("m3", 32, 64), A("mall"), A("nl", 32, 33), OP.add)
         if rnd == 0:
+            cp(A("off2"), A("ci2", 36, 72))
             cp(A("off3"), A("ci2", 12, 36))
         tr(A("m3t"), A("m3"))
         tr(A("vr", 0, 96), A("vx", 0, 96))
@@ -443,53 +463,47 @@ def rank_program(g, core, T, topo):
         tr(A("vr", 96, 192), A("vx", 96, 192))
         ts(A("w1", 32, 64), A("nl", 1, 33), c0, OP.max, 1.0, OP.add)
         ts(A("w1", 96, 128), A("nl", 0, 32), c0, OP.max, -1000.0, OP.mult)
-        tt(A("w1", 128, 160), bc, A("w1", 32, 64), OP.subtract)
+        tt(A("w1", 128, 160), A("w1", 192, 224), A("w1", 32, 64), OP.subtract)
         tt(A("w1", 160, 192), A("w1", 64, 96), A("w1", 96, 128), OP.add)
-        tt(A("w1", 192, 224), A("w1", 128, 160), A("w1", 0, 32), OP.max)
         tr(A("vr", 192, 288), A("vx", 192, 288))
-        tt(A("tau"), A("w1", 160, 192), A("w1", 192, 224), OP.max)
+        tt(A("tau", 16, 48), A("w1", 160, 192), A("w1", 128, 160), OP.max)
         tr(A("vr", 288, 384), A("vx", 288, 384))
-        for h in range(2):
-            lin(A("tb", 32 * h + 16, 32 * h + 32), A("tau", 16 * h, 16 * h + 16), pm[1])
-            ts(A("tb", 32 * h, 32 * h + 16), A("tau", 16 * h, 16 * h + 16), pm[0], OP.mult)
-        tr(A("tbt"), A("tb"))
-        for h in range(2):
-            tt(A("tl", h, 24, 2), A("tbt", 32 * h, 32 * h + 24, 2), A("tbt", 32 * h + 1, 32 * h + 24, 2), OP.add)
-        cp(A("offs"), A("tl"))
         unpack(2, 1)
         unpack(3, 2)
-        cp(ind(A("wa", 16, 400), A("offs")), A("vr"))
-
-        def spread(win, off):
-            act(A("ds", 192, 384), ind(win, A(off, 12, 24)), FN.Copy)
-            cp(A("ds", 0, 192), ind(win, A(off, 0, 12)))
-
-        def compact(out, win, off):
-            act(out, ind(win, A(off, 24, 36)), FN.Copy)
-            tr(A("dst"), A("ds"))
+        for i in range(3):
+            tr(A("tbt", 32 * i, 32 * i + 32), A("tau", 16 * i, 16 * i + 32))
+        cp(A("offs"), ind(A("tbt"), A("offk", 0, 2)))
+        cp(ind(A("wa", 16, 608), A("offs", 0, 24)), A("vr"))
 
         tr(A("ta", 0, 192), A("wa", 0, 192))
         tr(A("ta", 192, 384), A("wa", 16, 208))
-        for h in range(2):
-            tt(A("l1", h, 12, 2), A("ta", 192 * h, 192 * h + 192, 32), A("idl", h, 12, 2), OP.max)
+        ts(A("off1"), ind(A("ta"), A("offk", 2, 5)), 2.0 ** -11, OP.mult)
+        win = A("wa", 16, 208)
+        act(A("ds", 192, 384), ind(win, A("off1", 28, 40)), FN.Copy)
+        cp(A("ds", 0, 192), ind(win, A("off1", 16, 28)))
+        act(A("wa", 608, 800), ind(win, A("off1", 0, 12)), FN.Copy)
+        tr(A("dst"), A("ds"))
+
+        def level2(out, a):
+            ts(out, A("dst", 16, 384, 32, 32 * a - 32, 32 * a), 2.0 ** -11, OP.mult, A("col", 7, 8, 1, 32 * a - 32, 32 * a), OP.add)
+
+        win = A("wa", 16, 800)
         for d in range(2):
-            ts(A("off1", d, 24, 2), A("l1"), 2.0 ** -11, OP.mult, e1000, OP.subtract)
-        spread(A("wa", 16, 208), "off1")
-        ts(A("off1", 24, 36), A("l1"), 2.0 ** -11, OP.mult, e1000, OP.subtract)
-        compact(A("wb"), A("wa", 16, 208), "off1")
-        for d in range(2):
-            ts(A("off2", d, 24, 2, 32, 64), A("dst", 16, 384, 32, 0, 32), 2.0 ** -11, OP.mult)
-        spread(A("wb"), "off2")
+            level2(A("off2", d, 24, 2, 32, 64), 1)
+        act(A("ds", 192, 384), ind(win, A("off2", 12, 24)), FN.Copy)
         for a in (1, 3):
-            ts(A("off2", 24, 36, 1, 32 * a, 32 * a + 32), A("dst", 16, 384, 32, 32 * a - 32, 32 * a), 2.0 ** -11, OP.mult)
-        compact(A("wd", 0, 192), A("wb"), "off2")
+            level2(A("off2", 24, 36, 1, 32 * a, 32 * a + 32), a)
+        cp(A("ds", 0, 192), ind(win, A("off2", 0, 12)))
+        act(A("wd", 0, 192), ind(win, A("off2", 24, 36)), FN.Copy)
+        tr(A("dst"), A("ds"))
         for d in range(2):
             for a in (2, 3):
                 ts(A("off3", d, 24, 2, 32 * a, 32 * a + 32), A("dst", 16, 384, 32, 32, 64),
                    A("col", 10 + d, 11 + d, 1, 32, 64), OP.mult, A("col", 8 + d, 9 + d, 1, 32, 64), OP.add)
         act(A("we", 192, 384), ind(A("wd"), A("off3", 12, 24)), FN.Copy)
         cp(A("we", 0, 192), ind(A("wd"), A("off3", 0, 12)))
-        tr(A("tc"), A("we"))
+        tr(A("tc", 0, 192), A("we", 0, 192))
+        tr(A("tc", 192, 384), A("we", 192, 384))
         tt(A("fi", 0, 12), A("tc", 0, 384, 32), A("tc", 16, 384, 32), OP.add)
         ts(A("fi", 12, 24), A("fi", 0, 12), 2047, OP.bitwise_and)
         cp(A("offz"), A("fi", 12, 24))
@@ -504,7 +518,7 @@ def rank_program(g, core, T, topo):
         for b in range(4):
             mm(wbank[b], 192, A("qw", 128 * b, 128 * b + 128), A("sw", 128 * b, 128 * b + 128), A("qz"), A("sz"))
         for b in range(4):
-            if b % 2 == 0:
+            if b % 2 == 1:
                 act(A("ht", b, 768, 4), P(wbank[b], 0, 192), FN.Relu, scale=0.015625)
             else:
                 ts(A("ht", b, 768, 4), P(wbank[b], 0, 192), 0.0, OP.max, 0.015625, OP.mult)
@@ -525,7 +539,7 @@ def rank_program(g, core, T, topo):
         tr(A("tc"), A("iw", 16, 400))
         for h, t in enumerate(("ta", "tc")):
             ts(A("ib", 24 * h, 24 * h + 12), A(t, 0, 384, 32), me, OP.mult)
-            lin(A("ib", 24 * h + 12, 24 * h + 24), A(t, 16, 384, 32), mo)
+            ts(A("ib", 24 * h + 12, 24 * h + 24), A(t, 16, 384, 32), mo, OP.mult)
         for h in range(2):
             tt(A("ib", 48 + h, 72, 2), A("ib", 24 * h, 24 * h + 12), A("ib", 24 * h + 12, 24 * h + 24), OP.add)
         cp(A("offx"), A("ib", 48, 72))
@@ -543,9 +557,9 @@ def rank_program(g, core, T, topo):
             tt(A("fz", 576 * b + 384, 576 * b + 576), P(dbank[b], 0, 192), A("zt", b, 768, 4), OP.add)
             if b < 2:
                 act(A("xn", b, 1536, 4), ind(A("fz", 576 * b, 576 * b + 576), A("offx")), FN.Copy)
-        act(A("xn", 2, 768, 4), ind(A("fz", 1152, 1728), A("offx", 0, 12)), FN.Copy)
+        act(A("xn", 2, 384, 4), ind(A("fz", 1152, 1728), A("offx", 0, 6)), FN.Copy)
+        cp(A("xn", 386, 1536, 4), ind(A("fz", 1152, 1728), A("offx", 6, 24)))
         cp(A("xn", 3, 1536, 4), ind(A("fz", 1728, 2304), A("offx")))
-        cp(A("xn", 770, 1536, 4), ind(A("fz", 1152, 1728), A("offx", 12, 24)))
         quant(A("qx"), A("sx"), A("xn"))
 
     mm(0, 192, A("qv"), A("sv"), *X(192))

@@ -16,25 +16,25 @@ SCRATCH = {
     "et": _sb(2048, BF), "qe": _sb(512, Q4), "se": _sb(512, U8), "idn": _sb(128, BF), "one": _sb(128, BF),
     "gt": _sb(512, BF), "qg": _sb(128, Q4), "sg": _sb(128, U8),
     "ci": _sb(64, I32), "cj": _sb(4, I32), "cf": _sb(128, F32), "col": _sb(24, F32), "offc": _sb(48, U16),
-    "mge": _sb(32, F32), "mlt": _sb(32, F32), "mltn": _sb(32, F32), "mall": _sb(32, F32),
-    "cc": _sb(32, F32), "rst": _sb(99, F32), "ci2": _sb(84, F32), "lr": _sb(192, F32), "offk": _sb(6, U16),
+    "mge": _sb(32, F32), "mlt": _sb(32, F32),
+    "cc": _sb(32, F32), "rst": _sb(99, F32), "ci2": _sb(84, F32), "lr": _sb(192, F32), "offk": _sb(8, U16),
     "kv": _sb(192, F32), "pre": _sb(400, F32),
-    "ts": _sb(384, F32), "rs": _sb(72, F32), "tk": _sb(384, F32), "dg": _sb(1024, BF),
-    "stl": _sb(32, F32), "sml": _sb(32, F32), "kt": _sb(24, F32), "ww": _sb(24, F32),
-    "yy": _sb(48, F32), "r1": _sb(4, F32), "m1": _sb(64, F32), "m1t": _sb(64, F32), "ab": _sb(2, F32),
+    "ts": _sb(384, F32), "rs": _sb(120, F32), "rw": _sb(120, F32), "ww": _sb(120, F32), "tk": _sb(384, F32), "dg": _sb(1024, BF),
+    "stl": _sb(32, F32), "sml": _sb(32, F32),
+    "yy": _sb(112, F32), "m1": _sb(112, F32), "m1t": _sb(64, F32), "ab": _sb(2, F32),
     "fl": _sb(99, F32), "cum": _sb(99, F32), "m2": _sb(128, F32), "m2t": _sb(130, F32), "kk": _sb(4, F32),
     "junk": _sb(66, F32), "sa": _sb(99, F32), "sb": _sb(99, F32), "bb": _sb(99, F32),
-    "bt": _sb(32, F32), "ee": _sb(32, F32), "em": _sb(32, F32), "nl": _sb(33, F32),
-    "m3": _sb(64, F32), "m3t": _sb(64, F32), "cr": _sb(2, F32),
-    "w1": _sb(256, F32), "w2": _sb(96, F32),
+    "bt": _sb(32, F32), "ee": _sb(48, F32), "em": _sb(32, F32), "nl": _sb(33, F32),
+    "m3": _sb(56, F32), "m3t": _sb(64, F32), "cr": _sb(2, F32),
+    "w1": _sb(256, F32), "w2": _sb(128, F32),
     "tau": _sb(64, F32), "tbt": _sb(96, F32), "offs": _sb(32, U16),
     "vx": _sb(384, F32), "vr": _sb(384, F32),
     "wa": _sb(800, F32), "wd": _sb(200, F32), "we": _sb(384, F32),
     "ds": _sb(384, BF), "dst": _sb(384, BF),
-    "ta": _sb(384, F32), "tc": _sb(384, F32),
+    "ta": _sb(384, F32), "tc": _sb(384, F32), "ti": _sb(768, F32),
     "off1": _sb(48, U16), "off2": _sb(36, U16), "off3": _sb(24, U16),
-    "fi": _sb(24, I32), "offz": _sb(12, U16), "offi": _sb(12, U16), "offx": _sb(24, U16),
-    "iw": _sb(400, F32), "ib": _sb(72, F32),
+    "fi": _sb(24, I32), "offz": _sb(12, U16), "offi": _sb(12, U16), "offx": _sb(32, U16),
+    "iw": _sb(400, F32),
     "fz": _sb(4 * 576, BF), "zt": _sb(768, BF), "qz": _sb(192, Q4), "sz": _sb(192, U8), "ht": _sb(768, BF),
     "cmp": _sb(4 * 1280, BF), "qc": _sb(1280, Q4), "sc": _sb(1280, U8),
     "plr": _sb(192, F32), "yo": _sb(384, F32),
@@ -236,24 +236,24 @@ def rank_program(g, core, T, topo):
     cp(A("offc"), A("ci", 0, 48))
     fill(A("stl", 24, 32), -FAR)
     quant(A("qe"), A("se"), A("et"))
-    (n_, par_, h16, q_, pm0, me, mo, b592, z0, z1, me11, mo11, nh16, sgn, npar, c192, ccol, vb, k1, k2, k3) = (A("col", i, i + 1) for i in range(21))
-    xr, xpar, same, s1000, bcol = A("cf", 0, 32), A("cf", 32, 64), A("cf", 64, 96), A("cf", 96, 128), A("m2t", 0, 1)
+    (n_, par_, h16, q_, pm0, me, mo, b592, z0, z1, me11, mo11, nh16, sgn, npar, c192, ccol, vb, k1, k2, k3, k4, k5) = (A("col", i, i + 1) for i in range(23))
+    xr, xpar, same, bcol = A("cf", 0, 32), A("cf", 32, 64), A("cf", 64, 96), A("m2t", 0, 1)
     lin(pm0, par_, -1.0, 1.0)
     lin(sgn, par_, 2.0, -1.0)
     lin(npar, par_, -1.0 / 128)
     lin(me, h16, -0.0625, 1.0)
     lin(mo, h16, 0.0625)
     lin(k1, par_, 31.0, q_)
+    lin(k4, par_, 368.0, h16)
     lin(same, xpar, sgn, pm0)
     lin(bcol, n_, 1.0 / 128, npar)
     lin(A("m2t", 129, 130), n_, 1.0 / 128, npar)
     lin(k2, h16, -31.0 / 16, k1)
-    lin(s1000, same, 1000.0, -1000.0)
+    lin(k5, q_, 16.0, k4)
     quant(A("qu"), A("su"), A("ut"))
     quant(A("qg"), A("sg"), A("gt"))
     cp(words(A("qup")), ind(words(A("qu")), A("offc", 0, 24)))
     act(A("sup"), ind(A("su"), A("offc", 0, 24)), FN.Copy)
-    lin(A("mall"), same, 1809.0, -1000.0)
     lin(c192, bcol, 1.0, 192.0)
     lin(ccol, bcol, -2048.0, 578.0)
     lin(k3, k2, 1.0, 32.0)
@@ -267,6 +267,7 @@ def rank_program(g, core, T, topo):
     lin(A("ci2", 0, 12), A("cf", 0, 12), 16.0, q_)
     lin(A("cc"), xr, -1.0, ccol)
     lin(A("ci2", 72, 74), A("cf", 0, 2), 16.0, k3)
+    lin(A("ci2", 74, 76), A("cf", 0, 2), 256.0, k5)
 
     def late_constants():
         ident = A("ci2", 0, 12)
@@ -276,23 +277,25 @@ def rank_program(g, core, T, topo):
         lin(A("ci2", 37, 60, 2), ident, None, b592)
         lin(A("ci2", 60, 72), ident, None, b592)
 
-    gfill(A("rs", 0, 8), 8, 192)
-    gfill(A("rs", 8, 12), 4, 128)
-    gfill(A("rs", 24, 32), 8, 0)
-    gfill(A("tk", 320, 384), 64, 0)
+    gfill(A("rs"), 120, 0)
+    gfill(A("rw"), 120, 1)
+    gfill(A("rs", 2, 40, 5), 8, 192)
+    gfill(A("rs", 42, 60, 5), 4, 128)
+    gfill(A("rw", 0, 120, 5), 24, 0)
+    gfill(A("rw", 2, 120, 5), 24, -1)
     gfill(A("rst"), 99, 1)
     gfill(A("fl", 0, 99, 33), 3, 0)
     gfill(A("rst", 0, 99, 33), 3, 0)
     for a in range(4):
         blk = (32 * a, 32 * a + 32)
-        for out, src, pat, op, other, mult in (("mlt", 64, 1, OP.is_gt, 0.0, -1), ("mge", 64, -1, OP.is_ge, 0.0, 1),
-                                               ("mltn", 96, 1, OP.is_gt, -1000.0, -1)):
+        for out, pat, op, mult in (("mlt", 1, OP.is_gt, -1), ("mge", -1, OP.is_ge, 1)):
             wait("G", "cG", count["cG"])
-            sel(A(out, 0, 32, 1, *blk), A("cf", src, src + 32, 1, *blk), [[pat, 32]], op, other, 0, mult)
+            sel(A(out, 0, 32, 1, *blk), A("cf", 64, 96, 1, *blk), [[pat, 32]], op, 0.0, 0, mult)
     wait("G", "cG", count["cG"])
     gfill(A("sa", 0, 99, 3), 33, 5000)
     gfill(A("sa", 2, 99, 3), 33, -5000)
-    gfill(A("ee"), 32, 0)
+    gfill(A("ee"), 48, 0)
+    gfill(A("m3"), 56, 0)
     gfill(A("nl", 0, 1), 1, 0)
     iota(A("lr", 0, 32), [[0, 2], [32, 8], [192, 2]], 0)
     for i in range(4):
@@ -342,13 +345,13 @@ def rank_program(g, core, T, topo):
             for t in (0, 2, 1, 3):
                 n = 2 * b0 + t
                 act(slot(b0, t), P(1 + t % 2, 0, width[b0]), FN.Sign,
-                    bias=A("ts", 16 * n, 16 * n + 1), scale=-1.0, accum=A("rs", n, n + 1))
+                    bias=A("ts", 16 * n, 16 * n + 1), scale=-1.0, accum=A("rs", 5 * n + 2, 5 * n + 3))
 
         def sdiag(b0):
             for t in (0, 2, 1, 3):
                 n = 2 * b0 + t
                 act(A("dg", 64 * (n - 8), 64 * (n - 7)), P(1 + t % 2, 32 * b0, 32 * b0 + 64), FN.Sign,
-                    bias=A("ts", 16 * n, 16 * n + 1), scale=-1.0, accum=A("rs", 24 + n, 25 + n))
+                    bias=A("ts", 16 * n, 16 * n + 1), scale=-1.0, accum=A("rs", 5 * n + 3, 5 * n + 4))
 
         def vrows(b0):
             for t in (0, 2, 1, 3):
@@ -388,28 +391,29 @@ def rank_program(g, core, T, topo):
         for b0 in (4, 6, 8, 10):
             sdiag(b0)
         cp(A("stl", 0, 24), A("ts", 0, 384, 16))
+        if rnd == 0:
+            fill(A("rs", 1, 120, 5), 0.5)
+            fill(A("rw", 4, 120, 5), BIG)
+            fill(A("yy", 24, 56), -FAR)
+            fill(A("yy", 80, 112), FAR)
         mm(1, 384, *E(2), *X(384))
         mm(2, 384, *E(3), *X(384))
         unpack(0, 6)
-        tr(A("tk", 0, 320), P(5, 0, 320))
-        tr(A("sml"), A("stl"))
-        tt(A("rs", 48, 72), A("rs", 0, 24), A("rs", 24, 48), OP.add)
-        tt(A("kt"), A("tk", 0, 384, 16), A("rs", 48, 72), OP.subtract)
-        ts(A("ww"), A("kt"), 0.5, OP.add, BIG, OP.mult)
-        tt(A("yy", 24, 48), A("stl", 0, 24), A("ww"), OP.max)
-        tt(A("yy", 0, 24), A("stl", 0, 24), A("ww"), OP.min)
-        for p in range(2):
-            red(A("r1", 2 + p, 3 + p), A("yy", 24 + p, 48, 2), OP.min)
-        for p in range(2):
-            red(A("r1", p, p + 1), A("yy", p, 24, 2), OP.max)
-        for p in range(2):
-            lin(A("m1", 32 + p, 64, 2), A("cf", 0, 16), 0.0, A("r1", 2 + p, 3 + p))
-        for p in range(2):
-            ts(A("m1", p, 32, 2), A("cf", 0, 16), 0.0, OP.mult, A("r1", p, p + 1), OP.add)
         unpack(1, 7)
         if rnd == 0:
             late_constants()
-        tr(A("m1t"), A("m1"))
+        tr(A("tk", 0, 320), P(5, 0, 320))
+        tr(A("sml"), A("stl"))
+        cp(A("rs", 4, 100, 5), A("tk", 0, 320, 16))
+        scan(A("ww"), A("rs"), A("rw"), 0.0, OP.subtract, OP.mult)
+        tt(A("yy", 56, 80), A("stl", 0, 24), A("ww", 4, 120, 5), OP.max)
+        tt(A("yy", 0, 24), A("stl", 0, 24), A("ww", 4, 120, 5), OP.min)
+        for p in range(2):
+            scan(A("m1", 56 + p, 112, 2), A("yy", 56 + p, 112, 2), A("yy", 56 + p, 112, 2), FAR, OP.min, OP.min)
+        for p in range(2):
+            scan(A("m1", p, 56, 2), A("yy", p, 56, 2), A("yy", p, 56, 2), -FAR, OP.max, OP.max)
+        tr(A("m1t", 32, 64), A("m1", 80, 112))
+        tr(A("m1t", 0, 32), A("m1", 24, 56))
         red(A("ab", 1, 2), A("m1t", 32, 64), OP.min)
         red(A("ab", 0, 1), A("m1t", 0, 32), OP.max)
         ts(A("fl", 1, 33), A("sml"), A("ab", 1, 2), OP.is_gt)
@@ -442,36 +446,38 @@ def rank_program(g, core, T, topo):
             tt(A("ee", 0, 24, 2, 32 * a, 32 * a + 32), A("bt", 0, 24, 2, 32 * a, 32 * a + 32),
                A("bt", 1, 24, 2, 32 * a - 32, 32 * a), OP.subtract)
         tt(A("w2", 64, 96), A("w2", 0, 32), A("w2", 32, 64), OP.add)
-        tr(A("em"), A("ee"))
+        for p in range(2):
+            scan(A("m3", 2 + p, 50, 2), A("ee", p, 48, 2), A("ee", p, 48, 2), 0.0, OP.max, OP.max)
+        tr(A("em"), A("ee", 0, 32))
         tt(A("w1", 0, 32), A("w2", 64, 96), A("cc"), OP.add)
-        if rnd == 0:
-            ts(A("offk", 2, 5), A("lr", 96, 192, 32), 383.0, OP.min)
-            cp(A("offk", 0, 2), A("ci2", 72, 74))
+        tr(A("m3t", 32, 64), A("m3", 24, 56))
+        tr(A("m3t", 0, 32), A("m3", 0, 32))
+        lin(A("w2", 96, 128), A("em"), 1001.0, -809.0)
         scan(A("nl", 1, 33), A("em"), A("em"), 0.0, OP.max, OP.max)
         tt(A("w1", 192, 224), A("w1", 0, 32), bc, OP.max)
-        ts(A("m3", 0, 32), A("mltn"), A("nl", 32, 33), OP.add)
-        ts(A("m3", 32, 64), A("mall"), A("nl", 32, 33), OP.add)
-        if rnd == 0:
-            cp(A("off2"), A("ci2", 36, 72))
-            cp(A("off3"), A("ci2", 12, 36))
-        tr(A("m3t"), A("m3"))
-        tr(A("vr", 0, 96), A("vx", 0, 96))
         red(A("cr", 1, 2), A("m3t", 32, 64), OP.max, True)
         red(A("cr", 0, 1), A("m3t", 0, 32), OP.max)
         c0, c1 = A("cr", 0, 1), A("cr", 1, 2)
-        lin(A("w1", 64, 96), A("em"), 1001.0, c1)
-        tr(A("vr", 96, 192), A("vx", 96, 192))
+        lin(A("w1", 64, 96), A("w2", 96, 128), None, c1)
+        if rnd == 0:
+            ts(A("offk", 2, 5), A("lr", 96, 192, 32), 383.0, OP.min)
+            cp(A("offk", 0, 2), A("ci2", 72, 74))
+        tr(A("vr", 0, 128), A("vx", 0, 128))
         ts(A("w1", 32, 64), A("nl", 1, 33), c0, OP.max, 1.0, OP.add)
         ts(A("w1", 96, 128), A("nl", 0, 32), c0, OP.max, -1000.0, OP.mult)
+        tr(A("vr", 128, 224), A("vx", 128, 224))
         tt(A("w1", 128, 160), A("w1", 192, 224), A("w1", 32, 64), OP.subtract)
         tt(A("w1", 160, 192), A("w1", 64, 96), A("w1", 96, 128), OP.add)
-        tr(A("vr", 192, 288), A("vx", 192, 288))
+        tr(A("vr", 224, 320), A("vx", 224, 320))
         tt(A("tau", 16, 48), A("w1", 160, 192), A("w1", 128, 160), OP.max)
-        tr(A("vr", 288, 384), A("vx", 288, 384))
+        tr(A("vr", 320, 384), A("vx", 320, 384))
         unpack(2, 1)
         unpack(3, 2)
         for i in range(3):
             tr(A("tbt", 32 * i, 32 * i + 32), A("tau", 16 * i, 16 * i + 32))
+        if rnd == 0:
+            cp(A("off2"), A("ci2", 36, 72))
+            cp(A("off3"), A("ci2", 12, 36))
         cp(A("offs"), ind(A("tbt"), A("offk", 0, 2)))
         cp(ind(A("wa", 16, 608), A("offs", 0, 24)), A("vr"))
 
@@ -507,16 +513,20 @@ def rank_program(g, core, T, topo):
         tt(A("fi", 0, 12), A("tc", 0, 384, 32), A("tc", 16, 384, 32), OP.add)
         ts(A("fi", 12, 24), A("fi", 0, 12), 2047, OP.bitwise_and)
         cp(A("offz"), A("fi", 12, 24))
+        ts(A("offi"), A("fi", 12, 24), h16, OP.add)
         for b in (2, 0, 3, 1):
             src = ind(A("fz", 576 * b, 576 * b + 384), A("offz"))
             if b >= 2:
                 act(A("zt", b, 768, 4), src, FN.Copy)
             else:
                 cp(A("zt", b, 768, 4), src)
+        lin(A("iw"), A("pre"), None, nh16)
         quant(A("qz"), A("sz"), A("zt"))
         wbank = (3, 4, 5, 0)
         for b in range(4):
             mm(wbank[b], 192, A("qw", 128 * b, 128 * b + 128), A("sw", 128 * b, 128 * b + 128), A("qz"), A("sz"))
+        if rnd == 0:
+            ts(A("offk", 6, 8), A("ci2", 74, 76), 767.0, OP.min)
         for b in range(4):
             if b % 2 == 1:
                 act(A("ht", b, 768, 4), P(wbank[b], 0, 192), FN.Relu, scale=0.015625)
@@ -532,17 +542,10 @@ def rank_program(g, core, T, topo):
             count["sent"] += len(eng)
             issue("G", lambda: g.remote_dma(dst[0], src[0], T.sem[arr], T.sem["sent"], pid, rid, mask), [], [src], sem="sent", inc=0)
         count[arr] = 2 * len(shared(peer))
-        ts(A("offi"), A("fi", 12, 24), h16, OP.add)
-        lin(A("iw"), A("pre"), None, nh16)
         cp(ind(A("iw"), A("offi")), A("kv"))
-        tr(A("ta"), A("iw", 0, 384))
-        tr(A("tc"), A("iw", 16, 400))
-        for h, t in enumerate(("ta", "tc")):
-            ts(A("ib", 24 * h, 24 * h + 12), A(t, 0, 384, 32), me, OP.mult)
-            ts(A("ib", 24 * h + 12, 24 * h + 24), A(t, 16, 384, 32), mo, OP.mult)
-        for h in range(2):
-            tt(A("ib", 48 + h, 72, 2), A("ib", 24 * h, 24 * h + 12), A("ib", 24 * h + 12, 24 * h + 24), OP.add)
-        cp(A("offx"), A("ib", 48, 72))
+        tr(A("ti", 0, 384), A("iw", 0, 384))
+        tr(A("ti", 384, 768), A("iw", 16, 400))
+        cp(A("offx"), ind(A("ti"), A("offk", 6, 8)))
         if rnd == 1:
             quant(A("qv"), A("sv"), A("vt"))
         if rnd == 2:
@@ -556,10 +559,10 @@ def rank_program(g, core, T, topo):
         for b in range(4):
             tt(A("fz", 576 * b + 384, 576 * b + 576), P(dbank[b], 0, 192), A("zt", b, 768, 4), OP.add)
             if b < 2:
-                act(A("xn", b, 1536, 4), ind(A("fz", 576 * b, 576 * b + 576), A("offx")), FN.Copy)
+                act(A("xn", b, 1536, 4), ind(A("fz", 576 * b, 576 * b + 576), A("offx", 0, 24)), FN.Copy)
         act(A("xn", 2, 384, 4), ind(A("fz", 1152, 1728), A("offx", 0, 6)), FN.Copy)
         cp(A("xn", 386, 1536, 4), ind(A("fz", 1152, 1728), A("offx", 6, 24)))
-        cp(A("xn", 3, 1536, 4), ind(A("fz", 1728, 2304), A("offx")))
+        cp(A("xn", 3, 1536, 4), ind(A("fz", 1728, 2304), A("offx", 0, 24)))
         quant(A("qx"), A("sx"), A("xn"))
 
     mm(0, 192, A("qv"), A("sv"), *X(192))
@@ -570,6 +573,6 @@ def rank_program(g, core, T, topo):
     act(A("yo", 0, 192), P(0, 0, 192), FN.Copy)
     cp(A("yo", 192, 384), P(3, 0, 192))
     dma("S", ext(T.y[:]), A("yo"))
-    for s in sorted(count):
+    for s in sorted(count, key=lambda s: int(s[1:]) if s[0] == "d" else -1):
         if count[s]:
             g.wait_ge(T.sem[s], count[s])

@@ -15,25 +15,24 @@ SCRATCH = {
     "qw": _sb(512, Q4), "sw": _sb(512, U8),
     "et": _sb(2048, BF), "qe": _sb(512, Q4), "se": _sb(512, U8), "idn": _sb(128, BF), "one": _sb(128, BF),
     "gt": _sb(512, BF), "qg": _sb(128, Q4), "sg": _sb(128, U8),
-    "ci": _sb(64, I32), "cj": _sb(4, I32), "cf": _sb(128, F32), "col": _sb(24, F32), "offc": _sb(48, U16),
+    "ci": _sb(64, I32), "cj": _sb(4, I32), "cf": _sb(128, F32), "col": _sb(32, F32), "offc": _sb(24, U16),
     "mge": _sb(32, F32), "mlt": _sb(32, F32),
-    "cc": _sb(32, F32), "rst": _sb(99, F32), "ci2": _sb(84, F32), "lr": _sb(192, F32), "offk": _sb(8, U16),
+    "rst": _sb(99, F32), "ci2": _sb(24, F32), "offk": _sb(10, U16),
     "kv": _sb(192, F32), "pre": _sb(400, F32),
-    "ts": _sb(384, F32), "rs": _sb(120, F32), "rw": _sb(120, F32), "ww": _sb(120, F32), "tk": _sb(384, F32), "dg": _sb(1024, BF),
+    "ts": _sb(384, F32), "rs": _sb(72, F32), "rw": _sb(72, F32), "ww": _sb(72, F32), "tk": _sb(384, F32), "dg": _sb(1024, BF),
     "stl": _sb(32, F32), "sml": _sb(32, F32),
-    "yy": _sb(112, F32), "m1": _sb(112, F32), "m1t": _sb(64, F32), "ab": _sb(2, F32),
+    "ya": _sb(120, F32), "yb": _sb(120, F32), "m1": _sb(120, F32), "m1t": _sb(96, F32), "ab": _sb(2, F32),
     "fl": _sb(99, F32), "cum": _sb(99, F32), "m2": _sb(128, F32), "m2t": _sb(130, F32), "kk": _sb(4, F32),
     "junk": _sb(66, F32), "sa": _sb(99, F32), "sb": _sb(99, F32), "bb": _sb(99, F32),
-    "bt": _sb(32, F32), "ee": _sb(48, F32), "em": _sb(32, F32), "nl": _sb(33, F32),
-    "m3": _sb(56, F32), "m3t": _sb(64, F32), "cr": _sb(2, F32),
-    "w1": _sb(256, F32), "w2": _sb(128, F32),
-    "tau": _sb(64, F32), "tbt": _sb(96, F32), "offs": _sb(32, U16),
-    "vx": _sb(384, F32), "vr": _sb(384, F32),
-    "wa": _sb(800, F32), "wd": _sb(200, F32), "we": _sb(384, F32),
-    "ds": _sb(384, BF), "dst": _sb(384, BF),
-    "ta": _sb(384, F32), "tc": _sb(384, F32), "ti": _sb(768, F32),
-    "off1": _sb(48, U16), "off2": _sb(36, U16), "off3": _sb(24, U16),
-    "fi": _sb(24, I32), "offz": _sb(12, U16), "offi": _sb(12, U16), "offx": _sb(32, U16),
+    "bt": _sb(32, F32), "ee": _sb(64, F32), "kd": _sb(64, F32), "em": _sb(32, F32), "nl": _sb(33, F32),
+    "m3": _sb(64, F32), "m3t": _sb(64, F32), "cr": _sb(1, F32), "wr": _sb(32, F32),
+    "f0": _sb(96, F32), "f1": _sb(96, F32),
+    "tau": _sb(192, F32), "tbt": _sb(96, F32), "offs": _sb(32, U16),
+    "vx": _sb(384, BF), "vr": _sb(384, BF),
+    "wa": _sb(592, BF), "w1": _sb(192, BF), "w2": _sb(224, BF), "w3": _sb(192, BF), "w4": _sb(224, BF),
+    "ta": _sb(432, BF), "ti": _sb(768, F32),
+    "oa": _sb(48, U16), "ob": _sb(32, U16), "oi": _sb(16, U16), "od": _sb(16, U16),
+    "offz": _sb(16, U16), "offi": _sb(16, U16), "offx": _sb(32, U16),
     "iw": _sb(400, F32),
     "fz": _sb(4 * 576, BF), "zt": _sb(768, BF), "qz": _sb(192, Q4), "sz": _sb(192, U8), "ht": _sb(768, BF),
     "cmp": _sb(4 * 1280, BF), "qc": _sb(1280, Q4), "sc": _sb(1280, U8),
@@ -54,6 +53,7 @@ OP = AluOpType
 FN = ActivationFunctionType
 BIG = 2.0 ** 80
 FAR = 2.0 ** 95
+KK = 1024.0
 
 
 def rank_program(g, core, T, topo):
@@ -79,6 +79,9 @@ def rank_program(g, core, T, topo):
         if name.startswith("pb"):
             cols, pm = 1, 15
         return (ap, [(name, pm, cols)])
+
+    def B(name, a, c0, c1, st=1):
+        return A(name, c0, c1, st, 32 * a, 32 * a + 32)
 
     def ind(win, off):
         return (win[0].indirect(off[0]), win[1], off[1])
@@ -158,7 +161,7 @@ def rank_program(g, core, T, topo):
         issue("V", lambda: g.vector.tensor_reduce(o[0], a[0], AxisListType.X, op, negate=neg), [o], [a])
 
     def scan(o, a, b, init, op0, op1):
-        issue("V", lambda: g.vector.tensor_tensor_scan(o[0], a[0], b[0], init, op0, op1), [o], [a, b])
+        issue("V", lambda: g.vector.tensor_tensor_scan(o[0], a[0], b[0], raw(init), op0, op1), [o], [a, b, init])
 
     def fill(o, x):
         issue("V", lambda: g.vector.memset(o[0], x), [o], [])
@@ -220,89 +223,91 @@ def rank_program(g, core, T, topo):
     sel(A("idn"), A("one"), [[-1, 128]], OP.is_equal, 0.0, 0, 1)
     iota(A("ci", 0, 8), [[16, 8]], 0)
     iota(A("ci", 8, 24), [[16, 2], [32, 4], [0, 2]], 0)
-    iota(A("ci", 24, 48), [[1, 24]], 0)
     iota(A("cf", 0, 32), [[1, 32]], 0)
     iota(A("cf", 32, 64), [[0, 16], [1, 2]], 0)
+    iota(A("cf", 96, 120), [[32, 12], [0, 2]], -192)
     fill(A("et"), 0.0)
     for i, m in enumerate((31, 1, 16, 15)):
         ts(A("cj", i, i + 1), A("ci", 48, 49), m, OP.bitwise_and)
     fill(A("gt"), 0.0)
     cp(A("col", 0, 4), A("cj", 0, 4))
     for a in range(4):
-        fill(A("gt", 128 * a, 128 * a + 64, 2, 32 * a, 32 * a + 32), 1.0)
-        fill(A("gt", 128 * a + 65, 128 * a + 128, 2, 32 * a, 32 * a + 32), 1.0)
+        fill(B("gt", a, 128 * a, 128 * a + 64, 2), 1.0)
+        fill(B("gt", a, 128 * a + 65, 128 * a + 128, 2), 1.0)
     for b in range(4):
         act(A("et", 512 * b + b, 512 * (b + 1), 4), A("idn"), FN.Copy)
-    cp(A("offc"), A("ci", 0, 48))
+    cp(A("offc"), A("ci", 0, 24))
     fill(A("stl", 24, 32), -FAR)
     quant(A("qe"), A("se"), A("et"))
-    (n_, par_, h16, q_, pm0, me, mo, b592, z0, z1, me11, mo11, nh16, sgn, npar, c192, ccol, vb, k1, k2, k3, k4, k5) = (A("col", i, i + 1) for i in range(23))
-    xr, xpar, same, bcol = A("cf", 0, 32), A("cf", 32, 64), A("cf", 64, 96), A("m2t", 0, 1)
+    (n_, par_, h16, q_, pm0, me, mo, nh16, sgn, h192, ccol, k1, k2, k3, k4, k5, k6, k7, k8, k9, k10, k11) = (A("col", i, i + 1) for i in range(22))
+    xr, xpar, same = A("cf", 0, 32), A("cf", 32, 64), A("cf", 64, 96)
     lin(pm0, par_, -1.0, 1.0)
     lin(sgn, par_, 2.0, -1.0)
-    lin(npar, par_, -1.0 / 128)
+    lin(same, xpar, sgn, pm0)
     lin(me, h16, -0.0625, 1.0)
     lin(mo, h16, 0.0625)
-    lin(k1, par_, 31.0, q_)
-    lin(k4, par_, 368.0, h16)
-    lin(same, xpar, sgn, pm0)
-    lin(bcol, n_, 1.0 / 128, npar)
-    lin(A("m2t", 129, 130), n_, 1.0 / 128, npar)
-    lin(k2, h16, -31.0 / 16, k1)
-    lin(k5, q_, 16.0, k4)
+    lin(k1, par_, 416.0, -224.0)
+    lin(k2, par_, -208.0, 224.0)
+    lin(k3, par_, 96.0, -63.0)
+    lin(k4, par_, -33.0, 64.0)
+    lin(k5, par_, 368.0, h16)
+    lin(k6, par_, -16.0 / KK, 192.0 / KK)
     quant(A("qu"), A("su"), A("ut"))
     quant(A("qg"), A("sg"), A("gt"))
     cp(words(A("qup")), ind(words(A("qu")), A("offc", 0, 24)))
     act(A("sup"), ind(A("su"), A("offc", 0, 24)), FN.Copy)
-    lin(c192, bcol, 1.0, 192.0)
-    lin(ccol, bcol, -2048.0, 578.0)
-    lin(k3, k2, 1.0, 32.0)
-    lin(b592, h16, 37.0)
-    lin(z0, h16, 12.0)
-    lin(z1, h16, -12.0, 192.0)
-    lin(me11, h16, -2.0 ** -15, 2.0 ** -11)
-    lin(mo11, h16, 2.0 ** -15)
+    ident, even = A("ci2", 0, 12), A("ci2", 15, 16)
+    lin(k7, q_, 16.0, k2)
+    lin(k8, q_, 1.0, k4)
+    lin(k9, q_, 16.0, k5)
+    lin(k10, q_, 1.0, 416.0)
+    lin(ccol, n_, 16.0 / KK, k6)
     lin(nh16, h16, -1.0)
-    lin(vb, n_, 1.0, -2048.0)
-    lin(A("ci2", 0, 12), A("cf", 0, 12), 16.0, q_)
-    lin(A("cc"), xr, -1.0, ccol)
-    lin(A("ci2", 72, 74), A("cf", 0, 2), 16.0, k3)
-    lin(A("ci2", 74, 76), A("cf", 0, 2), 256.0, k5)
+    lin(h192, h16, 1.0, 192.0)
+    lin(ident, A("cf", 0, 12), 16.0, q_)
+    lin(even, k1, mo, k7)
+    lin(k11, k3, mo, k8)
+    lin(k2, k10, me)
+    lin(k4, h16, 1.0, 1.0)
 
     def late_constants():
-        ident = A("ci2", 0, 12)
-        lin(A("ci2", 12, 36, 2), ident, me, z0)
-        lin(A("ci2", 13, 36, 2), ident, mo, z1)
-        lin(A("ci2", 36, 60, 2), ident, None, b592)
-        lin(A("ci2", 37, 60, 2), ident, None, b592)
-        lin(A("ci2", 60, 72), ident, None, b592)
+        lin(A("ci2", 14, 15), even, 1.0, 16.0)
+        lin(A("ci2", 16, 17), even, mo, k2)
+        lin(A("ci2", 18, 19), even, 1.0, k4)
+        lin(A("ci2", 12, 14), A("cf", 0, 2), 16.0, k11)
+        lin(A("ci2", 20, 22), A("cf", 0, 2), 256.0, k9)
+        lin(A("f0", 1, 96, 3), xr, 1.0 / KK, ccol)
+        lin(A("ta", 416, 428), ident)
+        lin(A("vx", 1, 384, 16), A("cf", 96, 120), None, n_)
 
-    gfill(A("rs"), 120, 0)
-    gfill(A("rw"), 120, 1)
-    gfill(A("rs", 2, 40, 5), 8, 192)
-    gfill(A("rs", 42, 60, 5), 4, 128)
-    gfill(A("rw", 0, 120, 5), 24, 0)
-    gfill(A("rw", 2, 120, 5), 24, -1)
+    gfill(A("rs"), 72, 0)
+    gfill(A("rw"), 72, 1)
+    gfill(A("rs", 1, 24, 3), 8, 192)
+    gfill(A("rs", 25, 36, 3), 4, 128)
+    gfill(A("rw", 0, 72, 3), 24, 0)
     gfill(A("rst"), 99, 1)
     gfill(A("fl", 0, 99, 33), 3, 0)
     gfill(A("rst", 0, 99, 33), 3, 0)
+    gfill(A("vx"), 384, 0)
     for a in range(4):
-        blk = (32 * a, 32 * a + 32)
         for out, pat, op, mult in (("mlt", 1, OP.is_gt, -1), ("mge", -1, OP.is_ge, 1)):
             wait("G", "cG", count["cG"])
-            sel(A(out, 0, 32, 1, *blk), A("cf", 64, 96, 1, *blk), [[pat, 32]], op, 0.0, 0, mult)
+            sel(B(out, a, 0, 32), B("cf", a, 64, 96), [[pat, 32]], op, 0.0, 0, mult)
     wait("G", "cG", count["cG"])
+    gfill(A("m2t", 0, 130, 129), 2, -1)
     gfill(A("sa", 0, 99, 3), 33, 5000)
     gfill(A("sa", 2, 99, 3), 33, -5000)
-    gfill(A("ee"), 48, 0)
-    gfill(A("m3"), 56, 0)
-    gfill(A("nl", 0, 1), 1, 0)
-    iota(A("lr", 0, 32), [[0, 2], [32, 8], [192, 2]], 0)
-    for i in range(4):
-        iota(A("lr", 32 + 16 * i, 48 + 16 * i), [[32, 4], [192, 2], [0, 2]], 128 * (i // 2))
-    gfill(A("tau"), 64, 0)
-    gfill(A("wa"), 800, 0)
-    gfill(A("wd", 192, 200), 8, 0)
+    gfill(A("ee"), 64, 0)
+    gfill(A("m3", 0, 2), 2, 0)
+    gfill(A("kd"), 64, 1)
+    gfill(A("f0", 0, 96, 3), 32, 0)
+    gfill(A("f0", 2, 96, 3), 32, int(KK))
+    gfill(A("tau"), 192, 0)
+    gfill(A("wa", 0, 224), 224, 0)
+    gfill(A("ta", 428, 432), 4, 0)
+    for w in ("w2", "w4"):
+        gfill(A(w, 0, 16), 16, 0)
+        gfill(A(w, 208, 224), 16, 0)
     iota(A("kv"), [[1, 192]], 384)
     iota(A("pre"), [[1, 400]], 0)
 
@@ -345,13 +350,13 @@ def rank_program(g, core, T, topo):
             for t in (0, 2, 1, 3):
                 n = 2 * b0 + t
                 act(slot(b0, t), P(1 + t % 2, 0, width[b0]), FN.Sign,
-                    bias=A("ts", 16 * n, 16 * n + 1), scale=-1.0, accum=A("rs", 5 * n + 2, 5 * n + 3))
+                    bias=A("ts", 16 * n, 16 * n + 1), scale=-1.0, accum=A("rs", 3 * n + 1, 3 * n + 2))
 
         def sdiag(b0):
             for t in (0, 2, 1, 3):
                 n = 2 * b0 + t
                 act(A("dg", 64 * (n - 8), 64 * (n - 7)), P(1 + t % 2, 32 * b0, 32 * b0 + 64), FN.Sign,
-                    bias=A("ts", 16 * n, 16 * n + 1), scale=-1.0, accum=A("rs", 5 * n + 3, 5 * n + 4))
+                    bias=A("ts", 16 * n, 16 * n + 1), scale=-1.0, accum=A("rs", 3 * n, 3 * n + 1))
 
         def vrows(b0):
             for t in (0, 2, 1, 3):
@@ -392,30 +397,29 @@ def rank_program(g, core, T, topo):
             sdiag(b0)
         cp(A("stl", 0, 24), A("ts", 0, 384, 16))
         if rnd == 0:
-            fill(A("rs", 1, 120, 5), 0.5)
-            fill(A("rw", 4, 120, 5), BIG)
-            fill(A("yy", 24, 56), -FAR)
-            fill(A("yy", 80, 112), FAR)
+            fill(A("rs", 62, 72, 3), BIG / 2)
+            fill(A("rw", 2, 72, 3), -BIG)
+            fill(A("ya"), -FAR)
+            fill(A("yb", 24, 120), FAR)
+            fill(A("yb", 62, 64), -FAR)
+            fill(A("kd", 30, 32), 1.0 / KK)
         mm(1, 384, *E(2), *X(384))
         mm(2, 384, *E(3), *X(384))
-        unpack(0, 6)
-        unpack(1, 7)
         if rnd == 0:
             late_constants()
+        unpack(0, 6)
+        unpack(1, 7)
         tr(A("tk", 0, 320), P(5, 0, 320))
         tr(A("sml"), A("stl"))
-        cp(A("rs", 4, 100, 5), A("tk", 0, 320, 16))
-        scan(A("ww"), A("rs"), A("rw"), 0.0, OP.subtract, OP.mult)
-        tt(A("yy", 56, 80), A("stl", 0, 24), A("ww", 4, 120, 5), OP.max)
-        tt(A("yy", 0, 24), A("stl", 0, 24), A("ww", 4, 120, 5), OP.min)
+        ts(A("rs", 2, 60, 3), A("tk", 0, 320, 16), BIG, OP.mult, BIG / 2, OP.add)
+        scan(A("ww"), A("rw"), A("rs"), 0.0, OP.mult, OP.add)
+        tt(A("yb", 0, 24), A("stl", 0, 24), A("ww", 2, 72, 3), OP.max)
+        tt(A("ya", 64, 88), A("stl", 0, 24), A("ww", 2, 72, 3), OP.min)
         for p in range(2):
-            scan(A("m1", 56 + p, 112, 2), A("yy", 56 + p, 112, 2), A("yy", 56 + p, 112, 2), FAR, OP.min, OP.min)
-        for p in range(2):
-            scan(A("m1", p, 56, 2), A("yy", p, 56, 2), A("yy", p, 56, 2), -FAR, OP.max, OP.max)
-        tr(A("m1t", 32, 64), A("m1", 80, 112))
-        tr(A("m1t", 0, 32), A("m1", 24, 56))
-        red(A("ab", 1, 2), A("m1t", 32, 64), OP.min)
-        red(A("ab", 0, 1), A("m1t", 0, 32), OP.max)
+            scan(A("m1", p, 120, 2), A("ya", p, 120, 2), A("yb", p, 120, 2), FAR, OP.max, OP.min)
+        tr(A("m1t"), A("m1", 24, 120))
+        red(A("ab", 1, 2), A("m1t", 0, 32), OP.min)
+        red(A("ab", 0, 1), A("m1t", 64, 96), OP.max)
         ts(A("fl", 1, 33), A("sml"), A("ab", 1, 2), OP.is_gt)
         ts(A("fl", 34, 66), A("sml"), A("ab", 1, 2), OP.is_ge)
         ts(A("fl", 67, 99), A("sml"), A("ab", 0, 1), OP.is_ge)
@@ -431,91 +435,72 @@ def rank_program(g, core, T, topo):
         red(A("kk", 1, 2), A("m2t", 65, 97), OP.add)
         lin(A("sa", 1, 99, 3), A("cum", 33, 66), None, A("kk", 2, 3))
         lin(A("sb", 2, 99, 3), A("cum", 66, 99), None, A("kk", 3, 4))
-        ts(A("sb", 1, 99, 3), A("cum", 0, 33), A("kk", 0, 1), OP.subtract, c192, OP.add)
-        ts(A("sb", 0, 99, 3), A("cum", 33, 66), A("kk", 1, 2), OP.subtract, c192, OP.add)
+        ts(A("sb", 1, 99, 3), A("cum", 0, 33), A("kk", 0, 1), OP.subtract, 191.0, OP.add)
+        ts(A("sb", 0, 99, 3), A("cum", 33, 66), A("kk", 1, 2), OP.subtract, 191.0, OP.add)
         scan(A("bb"), A("sa"), A("sb"), 0.0, OP.max, OP.min)
         bc, bp = A("bb", 5, 99, 3), A("bb", 2, 96, 3)
         tr(A("bt"), bc)
-        lin(A("w2", 0, 32), bc, -999.0)
-        lin(A("w2", 32, 64), bp, 1000.0)
-        act(A("vx"), ind(A("bt"), A("offc", 24, 48)), FN.Identity, bias=vb, scale=2048.0)
-        if rnd == 0:
-            tr(A("lr", 96, 192), A("lr", 0, 96))
+        tt(A("f1", 0, 96, 3), bc, bp, OP.is_equal)
+        lin(A("vx", 0, 384, 16), A("bt", 0, 24))
         tt(A("ee", 1, 24, 2), A("bt", 1, 24, 2), A("bt", 0, 24, 2), OP.subtract)
         for a in range(1, 4):
-            tt(A("ee", 0, 24, 2, 32 * a, 32 * a + 32), A("bt", 0, 24, 2, 32 * a, 32 * a + 32),
-               A("bt", 1, 24, 2, 32 * a - 32, 32 * a), OP.subtract)
-        tt(A("w2", 64, 96), A("w2", 0, 32), A("w2", 32, 64), OP.add)
+            tt(B("ee", a, 0, 24, 2), B("bt", a, 0, 24, 2), B("bt", a - 1, 1, 24, 2), OP.subtract)
         for p in range(2):
-            scan(A("m3", 2 + p, 50, 2), A("ee", p, 48, 2), A("ee", p, 48, 2), 0.0, OP.max, OP.max)
+            scan(A("m3", 2 + p, 64, 2), A("kd", p, 62, 2), A("ee", p, 62, 2), 0.0, OP.mult, OP.max)
         tr(A("em"), A("ee", 0, 32))
-        tt(A("w1", 0, 32), A("w2", 64, 96), A("cc"), OP.add)
-        tr(A("m3t", 32, 64), A("m3", 24, 56))
-        tr(A("m3t", 0, 32), A("m3", 0, 32))
-        lin(A("w2", 96, 128), A("em"), 1001.0, -809.0)
-        scan(A("nl", 1, 33), A("em"), A("em"), 0.0, OP.max, OP.max)
-        tt(A("w1", 192, 224), A("w1", 0, 32), bc, OP.max)
-        red(A("cr", 1, 2), A("m3t", 32, 64), OP.max, True)
-        red(A("cr", 0, 1), A("m3t", 0, 32), OP.max)
-        c0, c1 = A("cr", 0, 1), A("cr", 1, 2)
-        lin(A("w1", 64, 96), A("w2", 96, 128), None, c1)
+        tr(A("m3t"), A("m3"))
+        lin(A("wr"), A("em"), 1.0 + 1.0 / KK, 191.0 / KK - 1.0)
         if rnd == 0:
-            ts(A("offk", 2, 5), A("lr", 96, 192, 32), 383.0, OP.min)
-            cp(A("offk", 0, 2), A("ci2", 72, 74))
+            ts(A("offk", 0, 5), A("ci2", 12, 17), 431.0, OP.min)
+            ts(A("offk", 6, 7), A("ci2", 18, 19), 431.0, OP.min)
+        red(A("cr"), A("m3t", 32, 64), OP.max, True)
+        red(A("nl", 0, 1), A("m3t", 0, 32), OP.max)
+        lin(A("wr"), A("wr"), None, A("cr"))
         tr(A("vr", 0, 128), A("vx", 0, 128))
-        ts(A("w1", 32, 64), A("nl", 1, 33), c0, OP.max, 1.0, OP.add)
-        ts(A("w1", 96, 128), A("nl", 0, 32), c0, OP.max, -1000.0, OP.mult)
-        tr(A("vr", 128, 224), A("vx", 128, 224))
-        tt(A("w1", 128, 160), A("w1", 192, 224), A("w1", 32, 64), OP.subtract)
-        tt(A("w1", 160, 192), A("w1", 64, 96), A("w1", 96, 128), OP.add)
-        tr(A("vr", 224, 320), A("vx", 224, 320))
-        tt(A("tau", 16, 48), A("w1", 160, 192), A("w1", 128, 160), OP.max)
-        tr(A("vr", 320, 384), A("vx", 320, 384))
+        scan(A("nl", 1, 33), A("em"), A("em"), A("nl", 0, 1), OP.max, OP.max)
+        tr(A("vr", 128, 256), A("vx", 128, 256))
+        tt(A("f1", 2, 96, 3), bc, A("nl", 1, 33), OP.subtract)
+        tt(A("f1", 1, 96, 3), A("wr"), A("nl", 0, 32), OP.subtract)
+        tr(A("vr", 256, 384), A("vx", 256, 384))
+        scan(A("tau", 48, 144), A("f0"), A("f1"), 0.0, OP.mult, OP.max)
         unpack(2, 1)
         unpack(3, 2)
-        for i in range(3):
-            tr(A("tbt", 32 * i, 32 * i + 32), A("tau", 16 * i, 16 * i + 32))
         if rnd == 0:
-            cp(A("off2"), A("ci2", 36, 72))
-            cp(A("off3"), A("ci2", 12, 36))
+            cp(A("ob", 0, 12), ident)
+        tr(A("tbt", 0, 64), A("tau", 2, 192, 3))
+        tr(A("tbt", 64, 96), A("tau", 50, 146, 3))
+        if rnd == 0:
+            cp(A("ob", 16, 28), ident)
+            cp(A("od", 0, 12), ident)
         cp(A("offs"), ind(A("tbt"), A("offk", 0, 2)))
-        cp(ind(A("wa", 16, 608), A("offs", 0, 24)), A("vr"))
+        cp(ind(A("wa", 16, 592), A("offs", 0, 24)), A("vr"))
 
-        tr(A("ta", 0, 192), A("wa", 0, 192))
-        tr(A("ta", 192, 384), A("wa", 16, 208))
-        ts(A("off1"), ind(A("ta"), A("offk", 2, 5)), 2.0 ** -11, OP.mult)
-        win = A("wa", 16, 208)
-        act(A("ds", 192, 384), ind(win, A("off1", 28, 40)), FN.Copy)
-        cp(A("ds", 0, 192), ind(win, A("off1", 16, 28)))
-        act(A("wa", 608, 800), ind(win, A("off1", 0, 12)), FN.Copy)
-        tr(A("dst"), A("ds"))
+        def turn(w):
+            tr(A("ta", 0, 224), A(w, 0, 224))
+            tr(A("ta", 224, 416), A(w, 16, 208))
 
-        def level2(out, a):
-            ts(out, A("dst", 16, 384, 32, 32 * a - 32, 32 * a), 2.0 ** -11, OP.mult, A("col", 7, 8, 1, 32 * a - 32, 32 * a), OP.add)
+        def step(out, o0, win, w0, off, c0, cut):
+            w = A(win, w0, w0 + 192)
+            act(A(out, o0, o0 + 16 * cut), ind(w, A(off, c0, c0 + cut)), FN.Copy)
+            if cut < 12:
+                cp(A(out, o0 + 16 * cut, o0 + 192), ind(w, A(off, c0 + cut, c0 + 12)))
 
-        win = A("wa", 16, 800)
-        for d in range(2):
-            level2(A("off2", d, 24, 2, 32, 64), 1)
-        act(A("ds", 192, 384), ind(win, A("off2", 12, 24)), FN.Copy)
+        turn("wa")
+        cp(A("oa"), ind(A("ta"), A("offk", 2, 5)))
         for a in (1, 3):
-            level2(A("off2", 24, 36, 1, 32 * a, 32 * a + 32), a)
-        cp(A("ds", 0, 192), ind(win, A("off2", 0, 12)))
-        act(A("wd", 0, 192), ind(win, A("off2", 24, 36)), FN.Copy)
-        tr(A("dst"), A("ds"))
-        for d in range(2):
-            for a in (2, 3):
-                ts(A("off3", d, 24, 2, 32 * a, 32 * a + 32), A("dst", 16, 384, 32, 32, 64),
-                   A("col", 10 + d, 11 + d, 1, 32, 64), OP.mult, A("col", 8 + d, 9 + d, 1, 32, 64), OP.add)
-        act(A("we", 192, 384), ind(A("wd"), A("off3", 12, 24)), FN.Copy)
-        cp(A("we", 0, 192), ind(A("wd"), A("off3", 0, 12)))
-        tr(A("tc", 0, 192), A("we", 0, 192))
-        tr(A("tc", 192, 384), A("we", 192, 384))
-        tt(A("fi", 0, 12), A("tc", 0, 384, 32), A("tc", 16, 384, 32), OP.add)
-        ts(A("fi", 12, 24), A("fi", 0, 12), 2047, OP.bitwise_and)
-        cp(A("offz"), A("fi", 12, 24))
-        ts(A("offi"), A("fi", 12, 24), h16, OP.add)
+            cp(B("ob", a, 0, 32), B("oa", a - 1, 0, 32))
+        step("w1", 0, "wa", 16, "oa", 32, 8)
+        step("w2", 16, "w1", 0, "ob", 0, 6)
+        step("w3", 0, "w2", 16, "ob", 16, 12)
+        turn("w2")
+        cp(A("oi"), ind(A("ta"), A("offk", 2, 3)))
+        for a in (2, 3):
+            cp(B("od", a, 0, 12), B("oi", 1, 0, 12))
+        step("w4", 16, "w3", 0, "od", 0, 6)
+        turn("w4")
+        ts(A("offz"), ind(A("ta"), A("offk", 6, 7)), 192.0, OP.add)
         for b in (2, 0, 3, 1):
-            src = ind(A("fz", 576 * b, 576 * b + 384), A("offz"))
+            src = ind(A("fz", 576 * b, 576 * b + 384), A("offz", 0, 12))
             if b >= 2:
                 act(A("zt", b, 768, 4), src, FN.Copy)
             else:
@@ -525,8 +510,9 @@ def rank_program(g, core, T, topo):
         wbank = (3, 4, 5, 0)
         for b in range(4):
             mm(wbank[b], 192, A("qw", 128 * b, 128 * b + 128), A("sw", 128 * b, 128 * b + 128), A("qz"), A("sz"))
+        ts(A("offi"), ind(A("ta"), A("offk", 6, 7)), h192, OP.add)
         if rnd == 0:
-            ts(A("offk", 6, 8), A("ci2", 74, 76), 767.0, OP.min)
+            ts(A("offk", 8, 10), A("ci2", 20, 22), 767.0, OP.min)
         for b in range(4):
             if b % 2 == 1:
                 act(A("ht", b, 768, 4), P(wbank[b], 0, 192), FN.Relu, scale=0.015625)
@@ -542,14 +528,14 @@ def rank_program(g, core, T, topo):
             count["sent"] += len(eng)
             issue("G", lambda: g.remote_dma(dst[0], src[0], T.sem[arr], T.sem["sent"], pid, rid, mask), [], [src], sem="sent", inc=0)
         count[arr] = 2 * len(shared(peer))
-        cp(ind(A("iw"), A("offi")), A("kv"))
+        cp(ind(A("iw"), A("offi", 0, 12)), A("kv"))
         tr(A("ti", 0, 384), A("iw", 0, 384))
         tr(A("ti", 384, 768), A("iw", 16, 400))
-        cp(A("offx"), ind(A("ti"), A("offk", 6, 8)))
+        cp(A("offx"), ind(A("ti"), A("offk", 8, 10)))
         if rnd == 1:
             quant(A("qv"), A("sv"), A("vt"))
         if rnd == 2:
-            act(A("plr"), ind(A("pre"), A("offz")), FN.Copy)
+            act(A("plr"), ind(A("pre"), A("offz", 0, 12)), FN.Copy)
             for l in range(8):
                 dma("Y", ext(T.pl[l:l + 1, :]), A("plr", 0, 192, 1, 16 * l, 16 * l + 1))
         wait("P", arr, count[arr])

@@ -11,27 +11,25 @@ def _sb(n, d):
 SCRATCH = {
     "xt": _sb(1536, BF), "xn": _sb(1536, BF), "ut": _sb(512, BF), "vt": _sb(512, BF),
     "qx": _sb(384, Q4), "sx": _sb(384, U8), "qu": _sb(128, Q4), "su": _sb(128, U8),
-    "qup": _sb(384, Q4), "sup": _sb(384, U8), "qv": _sb(128, Q4), "sv": _sb(128, U8),
+    "qup": _sb(256, Q4), "sup": _sb(256, U8), "qv": _sb(128, Q4), "sv": _sb(128, U8),
     "qw": _sb(512, Q4), "sw": _sb(512, U8),
-    "et": _sb(2048, BF), "qe": _sb(512, Q4), "se": _sb(512, U8), "idn": _sb(128, BF), "one": _sb(128, BF),
+    "et": _sb(516, BF), "qe": _sb(512, Q4), "se": _sb(512, U8), "idn": _sb(128, BF), "one": _sb(128, BF),
     "gt": _sb(512, BF), "qg": _sb(128, Q4), "sg": _sb(128, U8),
-    "ci": _sb(64, I32), "cj": _sb(4, I32), "cf": _sb(128, F32), "col": _sb(32, F32), "offc": _sb(24, U16),
-    "mge": _sb(32, F32), "mlt": _sb(32, F32),
-    "rst": _sb(99, F32), "ci2": _sb(24, F32), "offk": _sb(10, U16),
+    "ci": _sb(64, I32), "cj": _sb(4, I32), "cf": _sb(128, F32), "col": _sb(32, F32), "offc": _sb(16, U16),
+    "mk": _sb(192, F32), "on": _sb(97, F32), "ci2": _sb(24, F32), "offk": _sb(12, U16),
     "kv": _sb(192, F32), "pre": _sb(400, F32),
-    "ts": _sb(384, F32), "rs": _sb(72, F32), "rw": _sb(72, F32), "ww": _sb(72, F32), "tk": _sb(384, F32), "dg": _sb(1024, BF),
+    "ts": _sb(384, F32), "rs": _sb(1920, F32), "rw": _sb(120, F32), "ww": _sb(120, F32), "dg": _sb(1024, BF),
     "stl": _sb(32, F32), "sml": _sb(32, F32),
-    "ya": _sb(120, F32), "yb": _sb(120, F32), "m1": _sb(120, F32), "m1t": _sb(96, F32), "ab": _sb(2, F32),
-    "fl": _sb(99, F32), "cum": _sb(99, F32), "m2": _sb(128, F32), "m2t": _sb(130, F32), "kk": _sb(4, F32),
-    "junk": _sb(66, F32), "sa": _sb(99, F32), "sb": _sb(99, F32), "bb": _sb(99, F32),
-    "bt": _sb(32, F32), "ee": _sb(64, F32), "kd": _sb(64, F32), "em": _sb(32, F32), "nl": _sb(33, F32),
-    "m3": _sb(64, F32), "m3t": _sb(64, F32), "cr": _sb(1, F32), "wr": _sb(32, F32),
-    "f0": _sb(96, F32), "f1": _sb(96, F32),
-    "tau": _sb(192, F32), "tbt": _sb(96, F32), "offs": _sb(32, U16),
+    "ya": _sb(56, F32), "yb": _sb(56, F32), "m1": _sb(112, F32), "m1t": _sb(64, F32), "ab": _sb(2, F32),
+    "fl": _sb(3 * 161, F32), "m2": _sb(3 * 96, F32), "sa": _sb(291, F32), "sb": _sb(291, F32), "bb": _sb(99, F32),
+    "bt": _sb(32, F32), "ee": _sb(188, F32), "kd": _sb(93, F32), "em": _sb(128, F32), "ek": _sb(128, F32),
+    "m3": _sb(194, F32), "m3t": _sb(64, F32), "wr": _sb(128, F32), "xs": _sb(128, F32), "ns": _sb(64, F32),
+    "cc": _sb(32, F32), "f0": _sb(256, F32), "f1": _sb(256, F32),
+    "tau": _sb(256, F32), "tbt": _sb(96, F32), "offs": _sb(32, U16),
     "vx": _sb(384, BF), "vr": _sb(384, BF),
     "wa": _sb(592, BF), "w1": _sb(192, BF), "w2": _sb(224, BF), "w3": _sb(192, BF), "w4": _sb(224, BF),
     "ta": _sb(432, BF), "ti": _sb(768, F32),
-    "oa": _sb(48, U16), "ob": _sb(32, U16), "oi": _sb(16, U16), "od": _sb(16, U16),
+    "oa": _sb(48, U16), "ob": _sb(32, U16), "od": _sb(16, U16),
     "offz": _sb(16, U16), "offi": _sb(16, U16), "offx": _sb(32, U16),
     "iw": _sb(400, F32),
     "fz": _sb(4 * 576, BF), "zt": _sb(768, BF), "qz": _sb(192, Q4), "sz": _sb(192, U8), "ht": _sb(768, BF),
@@ -54,6 +52,8 @@ FN = ActivationFunctionType
 BIG = 2.0 ** 80
 FAR = 2.0 ** 95
 KK = 1024.0
+TINY = 2.0 ** -40
+LOW = -(1 << 20)
 
 
 def rank_program(g, core, T, topo):
@@ -218,32 +218,40 @@ def rank_program(g, core, T, topo):
     dma("Y", A("sw"), ext(T.ws[:]))
     dma("Y", A("vt"), ext(T.v[:]))
 
+    iota(A("ci", 0, 16), [[16, 2], [32, 4], [0, 2]], 0)
     iota(A("ci", 48, 49), [[0, 1]], 0, 1)
     gfill(A("one"), 128, 1)
     sel(A("idn"), A("one"), [[-1, 128]], OP.is_equal, 0.0, 0, 1)
-    iota(A("ci", 0, 8), [[16, 8]], 0)
-    iota(A("ci", 8, 24), [[16, 2], [32, 4], [0, 2]], 0)
     iota(A("cf", 0, 32), [[1, 32]], 0)
     iota(A("cf", 32, 64), [[0, 16], [1, 2]], 0)
     iota(A("cf", 96, 120), [[32, 12], [0, 2]], -192)
     fill(A("et"), 0.0)
+    fill(A("gt"), 0.0)
+    cp(A("offc"), A("ci", 0, 16))
     for i, m in enumerate((31, 1, 16, 15)):
         ts(A("cj", i, i + 1), A("ci", 48, 49), m, OP.bitwise_and)
-    fill(A("gt"), 0.0)
-    cp(A("col", 0, 4), A("cj", 0, 4))
     for a in range(4):
-        fill(B("gt", a, 128 * a, 128 * a + 64, 2), 1.0)
-        fill(B("gt", a, 128 * a + 65, 128 * a + 128, 2), 1.0)
-    for b in range(4):
-        act(A("et", 512 * b + b, 512 * (b + 1), 4), A("idn"), FN.Copy)
-    cp(A("offc"), A("ci", 0, 24))
+        for par in range(2):
+            c0 = 128 * a + 64 * par
+            fill(B("gt", a, c0 + par, c0 + 64, 2), 1.0)
+    cp(A("col", 0, 4), A("cj", 0, 4))
     fill(A("stl", 24, 32), -FAR)
-    quant(A("qe"), A("se"), A("et"))
-    (n_, par_, h16, q_, pm0, me, mo, nh16, sgn, h192, ccol, k1, k2, k3, k4, k5, k6, k7, k8, k9, k10, k11) = (A("col", i, i + 1) for i in range(22))
+    quant(A("qg"), A("sg"), A("gt"))
+    act(A("et", 3, 515, 4), A("idn"), FN.Copy)
+    fill(A("ya", 24, 56), -FAR)
+    fill(A("yb", 24, 56), FAR)
+    quant(A("qu"), A("su"), A("ut"))
+    cp(words(A("qup")), ind(words(A("qu")), A("offc")))
+    act(A("sup"), ind(A("su"), A("offc")), FN.Copy)
+
+    def quant_e(b):
+        quant(A("qe", 128 * b, 128 * b + 128), A("se", 128 * b, 128 * b + 128), A("et", 3 - b, 515 - b))
+
+    (n_, par_, h16, q_, pm0, me, mo, nh16, sgn, h192, ccol, k1, k2, k3, k4, k5, k6, k7, k8, k9, k10, k11, k12, k13) = (A("col", i, i + 1) for i in range(24))
     xr, xpar, same = A("cf", 0, 32), A("cf", 32, 64), A("cf", 64, 96)
+    ident, even = A("ci2", 0, 12), A("ci2", 15, 16)
     lin(pm0, par_, -1.0, 1.0)
     lin(sgn, par_, 2.0, -1.0)
-    lin(same, xpar, sgn, pm0)
     lin(me, h16, -0.0625, 1.0)
     lin(mo, h16, 0.0625)
     lin(k1, par_, 416.0, -224.0)
@@ -251,58 +259,62 @@ def rank_program(g, core, T, topo):
     lin(k3, par_, 96.0, -63.0)
     lin(k4, par_, -33.0, 64.0)
     lin(k5, par_, 368.0, h16)
-    lin(k6, par_, -16.0 / KK, 192.0 / KK)
-    quant(A("qu"), A("su"), A("ut"))
-    quant(A("qg"), A("sg"), A("gt"))
-    cp(words(A("qup")), ind(words(A("qu")), A("offc", 0, 24)))
-    act(A("sup"), ind(A("su"), A("offc", 0, 24)), FN.Copy)
-    ident, even = A("ci2", 0, 12), A("ci2", 15, 16)
+    lin(k6, par_, 16.0, 576.0)
+    lin(k10, q_, 1.0, 416.0)
+    lin(same, xpar, sgn, pm0)
     lin(k7, q_, 16.0, k2)
     lin(k8, q_, 1.0, k4)
     lin(k9, q_, 16.0, k5)
-    lin(k10, q_, 1.0, 416.0)
-    lin(ccol, n_, 16.0 / KK, k6)
-    lin(nh16, h16, -1.0)
-    lin(h192, h16, 1.0, 192.0)
-    lin(ident, A("cf", 0, 12), 16.0, q_)
-    lin(even, k1, mo, k7)
-    lin(k11, k3, mo, k8)
-    lin(k2, k10, me)
-    lin(k4, h16, 1.0, 1.0)
+    lin(ccol, n_, -16.0, k6)
+    lin(k12, k10, me)
+    lin(k13, h16, 1.0, 1.0)
 
     def late_constants():
+        lin(A("mk", 33, 64), A("cf", 65, 96), 1.0 / TINY, TINY)
+        lin(A("mk", 32, 33), A("cf", 64, 65), 1.0, TINY)
+        lin(A("mk", 64, 65), A("cf", 64, 65), -1.0 / TINY, -TINY)
+        lin(A("mk", 128, 129), A("cf", 64, 65), -1.0, -TINY)
+        lin(even, k1, mo, k7)
+        lin(k11, k3, mo, k8)
+        lin(ident, A("cf", 0, 12), 16.0, q_)
+        lin(A("cc"), xr, -1.0, ccol)
+        lin(A("vx", 1, 384, 16), A("cf", 96, 120), None, n_)
+        lin(nh16, h16, -1.0)
+        lin(h192, h16, 1.0, 192.0)
         lin(A("ci2", 14, 15), even, 1.0, 16.0)
-        lin(A("ci2", 16, 17), even, mo, k2)
-        lin(A("ci2", 18, 19), even, 1.0, k4)
+        lin(A("ci2", 16, 17), even, mo, k12)
+        lin(A("ci2", 18, 19), even, 1.0, k13)
         lin(A("ci2", 12, 14), A("cf", 0, 2), 16.0, k11)
         lin(A("ci2", 20, 22), A("cf", 0, 2), 256.0, k9)
-        lin(A("f0", 1, 96, 3), xr, 1.0 / KK, ccol)
         lin(A("ta", 416, 428), ident)
-        lin(A("vx", 1, 384, 16), A("cf", 96, 120), None, n_)
 
-    gfill(A("rs"), 72, 0)
-    gfill(A("rw"), 72, 1)
-    gfill(A("rs", 1, 24, 3), 8, 192)
-    gfill(A("rs", 25, 36, 3), 4, 128)
-    gfill(A("rw", 0, 72, 3), 24, 0)
-    gfill(A("rst"), 99, 1)
-    gfill(A("fl", 0, 99, 33), 3, 0)
-    gfill(A("rst", 0, 99, 33), 3, 0)
+    gfill(A("rs", 0, 1920, 16), 120, 0)
+    gfill(A("rw"), 120, 0)
+    gfill(A("rs", 32, 640, 80), 8, 192)
+    gfill(A("rs", 672, 960, 80), 4, 128)
+    gfill(A("rw", 1, 120, 5), 24, -1)
+    gfill(A("rw", 2, 120, 5), 24, 1)
+    gfill(A("on"), 97, 1)
+    gfill(A("mk", 0, 32), 32, 1)
+    gfill(A("mk", 96, 128), 32, 1)
+    for k in range(3):
+        gfill(A("fl", 161 * k + 97, 161 * k + 161), 64, 0)
+    gfill(A("fl", 64, 483, 161), 3, -1)
+    gfill(A("sa", 192, 291, 3), 33, 5000)
+    gfill(A("sa", 194, 291, 3), 33, -5000)
     gfill(A("vx"), 384, 0)
-    for a in range(4):
-        for out, pat, op, mult in (("mlt", 1, OP.is_gt, -1), ("mge", -1, OP.is_ge, 1)):
-            wait("G", "cG", count["cG"])
-            sel(B(out, a, 0, 32), B("cf", a, 64, 96), [[pat, 32]], op, 0.0, 0, mult)
-    wait("G", "cG", count["cG"])
-    gfill(A("m2t", 0, 130, 129), 2, -1)
-    gfill(A("sa", 0, 99, 3), 33, 5000)
-    gfill(A("sa", 2, 99, 3), 33, -5000)
-    gfill(A("ee"), 64, 0)
-    gfill(A("m3", 0, 2), 2, 0)
-    gfill(A("kd"), 64, 1)
-    gfill(A("f0", 0, 96, 3), 32, 0)
-    gfill(A("f0", 2, 96, 3), 32, int(KK))
-    gfill(A("tau"), 192, 0)
+    gfill(A("ee"), 188, 0)
+    gfill(A("m3", 0, 6), 6, 0)
+    gfill(A("kd", 0, 93, 3), 31, 1)
+    gfill(A("kd", 1, 93, 3), 31, int(KK))
+    gfill(A("m3t", 32, 64), 32, 0)
+    gfill(A("em", 0, 128, 2), 64, LOW)
+    gfill(A("ek", 0, 128, 2), 64, LOW)
+    gfill(A("xs", 0, 64), 64, 0)
+    gfill(A("wr", 0, 64), 64, 0)
+    gfill(A("f0", 128, 256, 2), 64, LOW)
+    gfill(A("f1", 130, 256, 4), 32, LOW)
+    gfill(A("tau", 1, 256, 4), 64, 0)
     gfill(A("wa", 0, 224), 224, 0)
     gfill(A("ta", 428, 432), 4, 0)
     for w in ("w2", "w4"):
@@ -315,7 +327,9 @@ def rank_program(g, core, T, topo):
         return A("qe", 128 * b, 128 * b + 128), A("se", 128 * b, 128 * b + 128)
 
     def U(i):
-        return A("qup", 128 * i, 128 * i + 128), A("sup", 128 * i, 128 * i + 128)
+        if i == 0:
+            return A("qu"), A("su")
+        return A("qup", 128 * i - 128, 128 * i), A("sup", 128 * i - 128, 128 * i)
 
     def X(n, c0=0):
         return A("qx", c0, n), A("sx", c0, n)
@@ -329,52 +343,59 @@ def rank_program(g, core, T, topo):
         sets = [topo.engines(c, T.cores[r ^ e]) for e in STEP]
         return [x for x in sets[0] if all(x in s for s in sets)]
 
-    quant(A("qx"), A("sx"), A("xt"))
+    def quant_x(src):
+        quant(*X(384, 256), A(src, 1024, 1536))
+        quant(*X(256), A(src, 0, 1024))
+
+    def slot(b0, t):
+        return A("cmp", 4 * qbase[b0] + t, 4 * (qbase[b0] + width[b0]), 4)
+
+    def srows(b0):
+        for t in (0, 2, 1, 3):
+            n = 2 * b0 + t
+            act(slot(b0, t), P(1 + t % 2, 0, width[b0]), FN.Sign,
+                bias=A("ts", 16 * n, 16 * n + 1), scale=-1.0, accum=A("rs", 80 * n + 32, 80 * n + 33))
+
+    def sdiag(b0):
+        for t in (0, 2, 1, 3):
+            n = 2 * b0 + t
+            act(A("dg", 64 * (n - 8), 64 * (n - 7)), P(1 + t % 2, 32 * b0, 32 * b0 + 64), FN.Sign,
+                bias=A("ts", 16 * n, 16 * n + 1), scale=-1.0, accum=A("rs", 80 * n + 16, 80 * n + 17))
+
+    def vrows(b0):
+        for t in (0, 2, 1, 3):
+            n = 2 * b0 + t
+            ts(slot(b0, t), P(3 + t % 2, 0, width[b0]), A("ts", 16 * n, 16 * n + 1), OP.is_lt, 2.0, OP.mult)
+
+    def cq(b0):
+        return A("qc", qbase[b0], qbase[b0] + width[b0]), A("sc", qbase[b0], qbase[b0] + width[b0])
+
+    def cquant(b0):
+        quant(*cq(b0), A("cmp", 4 * qbase[b0], 4 * (qbase[b0] + width[b0])))
+
+    def csum(b0, start=False, stop=False):
+        mm(5, width[b0], A("qg"), A("sg"), *cq(b0), start, stop)
+
+    def unpack(b, bank):
+        act(A("fz", 576 * b, 576 * b + 384), P(bank, 0, 384), FN.Copy)
+
+    quant_x("xt")
     for rnd, e in enumerate(STEP):
         peer = T.cores[rank ^ e]
-        mm(0, 384, *U(0), *X(384))
+        mm(7, 128, *U(0), *X(384, 256))
+        mm(0, 256, *U(0), *X(256))
         mm(1, 384, *U(1), *X(384))
         mm(3, 192, *U(1), *X(192))
         mm(2, 384, *U(2), *X(384))
         mm(4, 192, *U(2), *X(192))
+        if rnd == 0:
+            quant_e(0)
+            quant_e(1)
+        tr(A("ts", 256, 384), P(7, 0, 128))
+        tr(A("ts", 0, 192), P(0, 0, 192))
+        tr(A("ts", 192, 256), P(0, 192, 256))
         mm(6, 384, *E(0), *X(384))
         mm(7, 384, *E(1), *X(384))
-        tr(A("ts", 320, 384), P(0, 320, 384))
-        tr(A("ts", 0, 192), P(0, 0, 192))
-        tr(A("ts", 192, 320), P(0, 192, 320))
-
-        def slot(b0, t):
-            return A("cmp", 4 * qbase[b0] + t, 4 * (qbase[b0] + width[b0]), 4)
-
-        def srows(b0):
-            for t in (0, 2, 1, 3):
-                n = 2 * b0 + t
-                act(slot(b0, t), P(1 + t % 2, 0, width[b0]), FN.Sign,
-                    bias=A("ts", 16 * n, 16 * n + 1), scale=-1.0, accum=A("rs", 3 * n + 1, 3 * n + 2))
-
-        def sdiag(b0):
-            for t in (0, 2, 1, 3):
-                n = 2 * b0 + t
-                act(A("dg", 64 * (n - 8), 64 * (n - 7)), P(1 + t % 2, 32 * b0, 32 * b0 + 64), FN.Sign,
-                    bias=A("ts", 16 * n, 16 * n + 1), scale=-1.0, accum=A("rs", 3 * n, 3 * n + 1))
-
-        def vrows(b0):
-            for t in (0, 2, 1, 3):
-                n = 2 * b0 + t
-                ts(slot(b0, t), P(3 + t % 2, 0, width[b0]), A("ts", 16 * n, 16 * n + 1), OP.is_lt, 2.0, OP.mult)
-
-        def cq(b0):
-            return A("qc", qbase[b0], qbase[b0] + width[b0]), A("sc", qbase[b0], qbase[b0] + width[b0])
-
-        def cquant(b0):
-            quant(*cq(b0), A("cmp", 4 * qbase[b0], 4 * (qbase[b0] + width[b0])))
-
-        def csum(b0, start=False, stop=False):
-            mm(5, width[b0], A("qg"), A("sg"), *cq(b0), start, stop)
-
-        def unpack(b, bank):
-            act(A("fz", 576 * b, 576 * b + 384), P(bank, 0, 384), FN.Copy)
-
         srows(10)
         vrows(0)
         srows(8)
@@ -397,81 +418,84 @@ def rank_program(g, core, T, topo):
             sdiag(b0)
         cp(A("stl", 0, 24), A("ts", 0, 384, 16))
         if rnd == 0:
-            fill(A("rs", 62, 72, 3), BIG / 2)
-            fill(A("rw", 2, 72, 3), -BIG)
-            fill(A("ya"), -FAR)
-            fill(A("yb", 24, 120), FAR)
-            fill(A("yb", 62, 64), -FAR)
-            fill(A("kd", 30, 32), 1.0 / KK)
+            quant_e(2)
+            quant_e(3)
+            fill(A("rs", 48, 1920, 80), BIG / 2)
+            fill(A("rw", 3, 120, 5), -BIG)
+            fill(A("kd", 2, 93, 3), 1.0 / KK)
         mm(1, 384, *E(2), *X(384))
         mm(2, 384, *E(3), *X(384))
         if rnd == 0:
             late_constants()
         unpack(0, 6)
         unpack(1, 7)
-        tr(A("tk", 0, 320), P(5, 0, 320))
         tr(A("sml"), A("stl"))
-        ts(A("rs", 2, 60, 3), A("tk", 0, 320, 16), BIG, OP.mult, BIG / 2, OP.add)
-        scan(A("ww"), A("rw"), A("rs"), 0.0, OP.mult, OP.add)
-        tt(A("yb", 0, 24), A("stl", 0, 24), A("ww", 2, 72, 3), OP.max)
-        tt(A("ya", 64, 88), A("stl", 0, 24), A("ww", 2, 72, 3), OP.min)
-        for p in range(2):
-            scan(A("m1", p, 120, 2), A("ya", p, 120, 2), A("yb", p, 120, 2), FAR, OP.max, OP.min)
-        tr(A("m1t"), A("m1", 24, 120))
+        tr(A("rs", 0, 1600, 5), P(5, 0, 320))
+        scan(A("ww"), A("rw"), A("rs", 0, 1920, 16), 0.0, OP.mult, OP.add)
+        tt(A("yb", 0, 24), A("stl", 0, 24), A("ww", 3, 120, 5), OP.max)
+        tt(A("ya", 0, 24), A("stl", 0, 24), A("ww", 3, 120, 5), OP.min)
+        for y, m0, far, op in (("yb", 0, FAR, OP.min), ("ya", 56, -FAR, OP.max)):
+            for p in range(2):
+                scan(A("m1", m0 + p, m0 + 56, 2), A(y, p, 56, 2), A(y, p, 56, 2), far, op, op)
+        if rnd == 0:
+            ts(A("mk", 161, 192), A("cf", 1, 32), n_, OP.is_le)
+        tr(A("m1t", 0, 32), A("m1", 24, 56))
+        tr(A("m1t", 32, 64), A("m1", 80, 112))
+        if rnd == 0:
+            tt(A("mk", 65, 96), A("mk", 33, 64), A("mk", 161, 192), OP.mult)
+            tt(A("mk", 129, 160), A("mk", 33, 64), A("mk", 161, 192), OP.mult)
         red(A("ab", 1, 2), A("m1t", 0, 32), OP.min)
-        red(A("ab", 0, 1), A("m1t", 64, 96), OP.max)
-        ts(A("fl", 1, 33), A("sml"), A("ab", 1, 2), OP.is_gt)
-        ts(A("fl", 34, 66), A("sml"), A("ab", 1, 2), OP.is_ge)
-        ts(A("fl", 67, 99), A("sml"), A("ab", 0, 1), OP.is_ge)
-        scan(A("cum"), A("rst"), A("fl"), 0.0, OP.mult, OP.add)
-        lin(A("m2", 0, 32), A("mlt"), A("cum", 65, 66))
-        lin(A("m2", 96, 128), A("mlt"), A("cum", 98, 99))
-        ts(A("m2", 32, 64), A("mge"), A("cum", 32, 33), OP.mult)
-        ts(A("m2", 64, 96), A("mge"), A("cum", 65, 66), OP.mult)
-        tr(A("m2t", 1, 129), A("m2"))
-        lin(A("junk", 0, 33), A("m2t", 0, 33), accum=A("kk", 2, 3))
-        lin(A("junk", 33, 66), A("m2t", 97, 130), accum=A("kk", 3, 4))
-        red(A("kk", 0, 1), A("m2t", 33, 65), OP.add)
-        red(A("kk", 1, 2), A("m2t", 65, 97), OP.add)
-        lin(A("sa", 1, 99, 3), A("cum", 33, 66), None, A("kk", 2, 3))
-        lin(A("sb", 2, 99, 3), A("cum", 66, 99), None, A("kk", 3, 4))
-        ts(A("sb", 1, 99, 3), A("cum", 0, 33), A("kk", 0, 1), OP.subtract, 191.0, OP.add)
-        ts(A("sb", 0, 99, 3), A("cum", 33, 66), A("kk", 1, 2), OP.subtract, 191.0, OP.add)
-        scan(A("bb"), A("sa"), A("sb"), 0.0, OP.max, OP.min)
+        red(A("ab", 0, 1), A("m1t", 32, 64), OP.max)
+        for k, (col, op) in enumerate(((1, OP.is_gt), (1, OP.is_ge), (0, OP.is_ge))):
+            ts(A("fl", 161 * k + 65, 161 * k + 97), A("sml"), A("ab", col, col + 1), op)
+        scan(A("m2", 0, 64), A("mk", 96, 160), A("fl", 65, 129), 0.0, OP.mult, OP.add)
+        for k in (1, 2):
+            scan(A("m2", 96 * k, 96 * k + 96), A("mk", 0, 96), A("fl", 161 * k + 65, 161 * k + 161), 0.0, OP.mult, OP.add)
+        tr(A("fl", 32, 64), A("m2", 32, 64))
+        for k in (1, 2):
+            tr(A("fl", 161 * k, 161 * k + 64), A("m2", 96 * k + 32, 96 * k + 96))
+        for k, c0, init, buf, ph in ((0, 32, 192.0, "sb", 1), (1, 32, 192.0, "sb", 0), (1, 0, 0.0, "sa", 1), (2, 0, 0.0, "sb", 2)):
+            scan(A(buf, 3 * c0 + ph, 291, 3), A("on", c0, 97), A("fl", 161 * k + c0, 161 * k + 97), init, OP.mult, OP.add)
+        scan(A("bb"), A("sa", 192, 291), A("sb", 192, 291), 0.0, OP.max, OP.min)
         bc, bp = A("bb", 5, 99, 3), A("bb", 2, 96, 3)
         tr(A("bt"), bc)
-        tt(A("f1", 0, 96, 3), bc, bp, OP.is_equal)
+        tt(A("ns", 0, 32), bc, bp, OP.is_equal)
         lin(A("vx", 0, 384, 16), A("bt", 0, 24))
-        tt(A("ee", 1, 24, 2), A("bt", 1, 24, 2), A("bt", 0, 24, 2), OP.subtract)
+        tt(A("ee", 3, 72, 6), A("bt", 1, 24, 2), A("bt", 0, 24, 2), OP.subtract)
         for a in range(1, 4):
-            tt(B("ee", a, 0, 24, 2), B("bt", a, 0, 24, 2), B("bt", a - 1, 1, 24, 2), OP.subtract)
-        for p in range(2):
-            scan(A("m3", 2 + p, 64, 2), A("kd", p, 62, 2), A("ee", p, 62, 2), 0.0, OP.mult, OP.max)
-        tr(A("em"), A("ee", 0, 32))
-        tr(A("m3t"), A("m3"))
-        lin(A("wr"), A("em"), 1.0 + 1.0 / KK, 191.0 / KK - 1.0)
+            tt(B("ee", a, 0, 72, 6), B("bt", a, 0, 24, 2), B("bt", a - 1, 1, 24, 2), OP.subtract)
+        tt(A("ns", 32, 64), A("ns", 0, 32), A("cc"), OP.mult)
+        for p in (1, 0):
+            scan(A("m3", 6 + 3 * p, 191 + 3 * p, 2), A("kd"), A("ee", 3 * p, 185 + 3 * p, 2), 0.0, OP.mult, OP.max)
+        em = A("em", 65, 128, 2)
+        tr(em, A("ee", 0, 96, 3))
+        for d in range(2):
+            tt(A("xs", 64 + d, 128, 2), A("ns", 32, 64), bc, OP.add)
+        tr(A("em", 1, 64, 2), A("m3", 0, 96, 3))
+        tr(A("m3t", 0, 32), A("m3", 96, 192, 3))
+        tr(A("ek", 1, 64, 2), A("m3", 2, 98, 3))
+        lin(A("ek", 65, 128, 2), em, KK)
+        for d in range(2):
+            lin(A("wr", 64 + d, 128, 2), em, KK + 1.0, 191.0 - KK)
         if rnd == 0:
             ts(A("offk", 0, 5), A("ci2", 12, 17), 431.0, OP.min)
             ts(A("offk", 6, 7), A("ci2", 18, 19), 431.0, OP.min)
-        red(A("cr"), A("m3t", 32, 64), OP.max, True)
-        red(A("nl", 0, 1), A("m3t", 0, 32), OP.max)
-        lin(A("wr"), A("wr"), None, A("cr"))
         tr(A("vr", 0, 128), A("vx", 0, 128))
-        scan(A("nl", 1, 33), A("em"), A("em"), A("nl", 0, 1), OP.max, OP.max)
-        tr(A("vr", 128, 256), A("vx", 128, 256))
-        tt(A("f1", 2, 96, 3), bc, A("nl", 1, 33), OP.subtract)
-        tt(A("f1", 1, 96, 3), A("wr"), A("nl", 0, 32), OP.subtract)
-        tr(A("vr", 256, 384), A("vx", 256, 384))
-        scan(A("tau", 48, 144), A("f0"), A("f1"), 0.0, OP.mult, OP.max)
+        scan(A("f1", 1, 256, 2), A("xs"), A("em"), 0.0, OP.subtract, OP.max)
+        scan(A("f1", 0, 256, 4), A("m3t"), A("m3t"), 0.0, OP.max, OP.max)
+        scan(A("f0", 1, 256, 2), A("wr"), A("ek"), 0.0, OP.subtract, OP.max)
+        tr(A("vr", 128, 384), A("vx", 128, 384))
+        scan(A("tau", 64, 192), A("f0", 128, 256), A("f1", 128, 256), 0.0, OP.subtract, OP.max)
         unpack(2, 1)
         unpack(3, 2)
         if rnd == 0:
             cp(A("ob", 0, 12), ident)
-        tr(A("tbt", 0, 64), A("tau", 2, 192, 3))
-        tr(A("tbt", 64, 96), A("tau", 50, 146, 3))
+        tr(A("tbt", 0, 64), A("tau", 1, 256, 4))
+        tr(A("tbt", 64, 96), A("tau", 65, 192, 4))
         if rnd == 0:
             cp(A("ob", 16, 28), ident)
-            cp(A("od", 0, 12), ident)
+            cp(A("offk", 10, 11, 1, 0, 64), A("col", 20, 21, 1, 0, 64))
+            cp(A("offk", 10, 11, 1, 64, 128), A("offk", 2, 3, 1, 64, 128))
         cp(A("offs"), ind(A("tbt"), A("offk", 0, 2)))
         cp(ind(A("wa", 16, 592), A("offs", 0, 24)), A("vr"))
 
@@ -492,10 +516,10 @@ def rank_program(g, core, T, topo):
         step("w1", 0, "wa", 16, "oa", 32, 8)
         step("w2", 16, "w1", 0, "ob", 0, 6)
         step("w3", 0, "w2", 16, "ob", 16, 12)
-        turn("w2")
-        cp(A("oi"), ind(A("ta"), A("offk", 2, 3)))
         for a in (2, 3):
-            cp(B("od", a, 0, 12), B("oi", 1, 0, 12))
+            tr(B("ta", a, 0, 224), B("w2", 1, 0, 224))
+            tr(B("ta", a, 224, 416), B("w2", 1, 16, 208))
+        cp(A("od"), ind(A("ta"), A("offk", 10, 11)))
         step("w4", 16, "w3", 0, "od", 0, 6)
         turn("w4")
         ts(A("offz"), ind(A("ta"), A("offk", 6, 7)), 192.0, OP.add)
@@ -542,22 +566,30 @@ def rank_program(g, core, T, topo):
         dbank = (1, 2, 6, 7)
         for b in range(4):
             mm(dbank[b], 192, *E(b), A(ql), A(sl))
+
+        def take(eng, b, m0, m1):
+            o, src = A("xn", 64 * m0 + b, 64 * m1, 4), ind(A("fz", 576 * b, 576 * b + 576), A("offx", m0, m1))
+            if eng == "S":
+                act(o, src, FN.Copy)
+            else:
+                cp(o, src)
+
         for b in range(4):
             tt(A("fz", 576 * b + 384, 576 * b + 576), P(dbank[b], 0, 192), A("zt", b, 768, 4), OP.add)
             if b < 2:
-                act(A("xn", b, 1536, 4), ind(A("fz", 576 * b, 576 * b + 576), A("offx", 0, 24)), FN.Copy)
-        act(A("xn", 2, 384, 4), ind(A("fz", 1152, 1728), A("offx", 0, 6)), FN.Copy)
-        cp(A("xn", 386, 1536, 4), ind(A("fz", 1152, 1728), A("offx", 6, 24)))
-        cp(A("xn", 3, 1536, 4), ind(A("fz", 1728, 2304), A("offx", 0, 24)))
-        quant(A("qx"), A("sx"), A("xn"))
+                take("S", b, 0, 24)
+        take("S", 2, 0, 6)
+        take("V", 2, 6, 24)
+        take("V", 3, 0, 24)
+        quant_x("xn")
 
-    mm(0, 192, A("qv"), A("sv"), *X(192))
-    mm(3, 192, A("qv"), A("sv"), *X(384, 192))
+    mm(3, 128, A("qv"), A("sv"), *X(384, 256))
+    mm(0, 256, A("qv"), A("sv"), *X(256))
     dma("Y", ext(T.oc[:]), bytes_(A("qx")))
     for a in range(4):
         dma("Y", ext(T.osc[4 * a:4 * a + 4, :]), A("sx", 0, 384, 1, 32 * a, 32 * a + 4))
-    act(A("yo", 0, 192), P(0, 0, 192), FN.Copy)
-    cp(A("yo", 192, 384), P(3, 0, 192))
+    cp(A("yo", 256, 384), P(3, 0, 128))
+    act(A("yo", 0, 256), P(0, 0, 256), FN.Copy)
     dma("S", ext(T.y[:]), A("yo"))
     for s in sorted(count, key=lambda s: int(s[1:]) if s[0] == "d" else -1):
         if count[s]:

@@ -32,20 +32,19 @@ SCRATCH = {
     "oa": _sb(48, U16), "ob": _sb(32, U16), "od": _sb(16, U16),
     "offz": _sb(16, U16), "offi": _sb(16, U16), "offx": _sb(32, U16),
     "iw": _sb(400, F32),
-    "fz": _sb(4 * 576, BF), "zt": _sb(768, BF), "qz": _sb(192, Q4), "sz": _sb(192, U8), "ht": _sb(768, BF),
+    "fz": _sb(4 * 576, BF), "zt": _sb(1024, BF), "qo": _sb(128, Q4), "so": _sb(128, U8), "ht": _sb(1024, BF), "zero": _sb(512, BF),
     "cmp": _sb(4 * 1280, BF), "qc": _sb(1280, Q4), "sc": _sb(1280, U8),
     "plr": _sb(192, F32), "yo": _sb(384, F32),
 }
 for _r in range(3):
-    SCRATCH["qh%d" % _r] = _sb(192, Q4)
-    SCRATCH["sh%d" % _r] = _sb(192, U8)
-    SCRATCH["ql%d" % _r] = _sb(192, Q4)
-    SCRATCH["sl%d" % _r] = _sb(192, U8)
+    for _q, _s, _n in (("qz", "sz", 256), ("qh", "sh", 128), ("ql", "sl", 320)):
+        SCRATCH["%s%d" % (_q, _r)] = _sb(_n, Q4)
+        SCRATCH["%s%d" % (_s, _r)] = _sb(_n, U8)
 for _b in range(8):
     SCRATCH["pb%d" % _b] = ("psum", [128, 512], F32)
 
 NDMA = 24
-SEMAPHORES = ["cV", "cS", "cP", "cG", "sent", "arr0", "arr1", "arr2"] + ["d%d" % i for i in range(NDMA)]
+SEMAPHORES = ["cV", "cS", "cP", "cG", "sent"] + ["arr%d%d" % (r, i) for r in range(3) for i in range(2)] + ["d%d" % i for i in range(NDMA)]
 
 OP = AluOpType
 FN = ActivationFunctionType
@@ -213,7 +212,8 @@ def rank_program(g, core, T, topo):
         return A("pb%d" % b, c0, c1, st)
 
     dma("S", A("ut"), ext(T.u[:]))
-    dma("Y", A("xt"), ext(T.x[:]))
+    dma("Y", A("xt", 1024, 1536), ext(T.x[:, 1024:1536]))
+    dma("Y", A("xt", 0, 1024), ext(T.x[:, 0:1024]))
     dma("Y", bytes_(A("qw")), ext(T.wc[:]))
     dma("Y", A("sw"), ext(T.ws[:]))
     dma("Y", A("vt"), ext(T.v[:]))
@@ -240,6 +240,7 @@ def rank_program(g, core, T, topo):
     act(A("et", 3, 515, 4), A("idn"), FN.Copy)
     fill(A("ya", 24, 56), -FAR)
     fill(A("yb", 24, 56), FAR)
+    fill(A("zero"), 0.0)
     quant(A("qu"), A("su"), A("ut"))
     cp(words(A("qup")), ind(words(A("qu")), A("offc")))
     act(A("sup"), ind(A("su"), A("offc")), FN.Copy)
@@ -320,6 +321,9 @@ def rank_program(g, core, T, topo):
     for w in ("w2", "w4"):
         gfill(A(w, 0, 16), 16, 0)
         gfill(A(w, 208, 224), 16, 0)
+    for t in ("zt", "ht"):
+        for i in range(2):
+            gfill(A(t, 512 * i + 384, 512 * i + 512), 128, 0)
     iota(A("kv"), [[1, 192]], 384)
     iota(A("pre"), [[1, 400]], 0)
 
@@ -516,56 +520,79 @@ def rank_program(g, core, T, topo):
         step("w1", 0, "wa", 16, "oa", 32, 8)
         step("w2", 16, "w1", 0, "ob", 0, 6)
         step("w3", 0, "w2", 16, "ob", 16, 12)
+        quant(A("ql%d" % rnd, 0, 128), A("sl%d" % rnd, 0, 128), A("zero"))
         for a in (2, 3):
             tr(B("ta", a, 0, 224), B("w2", 1, 0, 224))
             tr(B("ta", a, 224, 416), B("w2", 1, 16, 208))
         cp(A("od"), ind(A("ta"), A("offk", 10, 11)))
         step("w4", 16, "w3", 0, "od", 0, 6)
+        lin(A("iw"), A("pre"), None, nh16)
         turn("w4")
         ts(A("offz"), ind(A("ta"), A("offk", 6, 7)), 192.0, OP.add)
-        for b in (2, 0, 3, 1):
-            src = ind(A("fz", 576 * b, 576 * b + 384), A("offz", 0, 12))
-            if b >= 2:
-                act(A("zt", b, 768, 4), src, FN.Copy)
-            else:
-                cp(A("zt", b, 768, 4), src)
-        lin(A("iw"), A("pre"), None, nh16)
-        quant(A("qz"), A("sz"), A("zt"))
-        wbank = (3, 4, 5, 0)
-        for b in range(4):
-            mm(wbank[b], 192, A("qw", 128 * b, 128 * b + 128), A("sw", 128 * b, 128 * b + 128), A("qz"), A("sz"))
+        qz, sz, qh, sh, ql, sl = ("%s%d" % (s, rnd) for s in ("qz", "sz", "qh", "sh", "ql", "sl"))
+        first, second = "arr%d0" % rnd, "arr%d1" % rnd
+        eng = shared(core)
+        rid, pid = topo.addr(peer)[:2]
+        mask = sum(1 << x for x in eng)
+
+        def send(arr, q, z, c0):
+            for src, dst in ((bytes_(A(q, 0, 96)), bytes_(A(ql, c0, c0 + 96))), (A(z, 0, 96), A(sl, c0, c0 + 96))):
+                count["sent"] += len(eng)
+                issue("G", lambda: g.remote_dma(dst[0], src[0], T.sem[arr], T.sem["sent"], pid, rid, mask), [], [src], sem="sent", inc=0)
+            count[arr] = 2 * len(shared(peer))
+
+        def layer(q, z, banks):
+            for b in range(4):
+                mm(banks[b], 128, A("qw", 128 * b, 128 * b + 128), A("sw", 128 * b, 128 * b + 128), q, z)
+
+        def make_h(i, banks, c0):
+            for b in range(4):
+                o, src = A("ht", 512 * i + b, 512 * i + 384, 4), P(banks[b], c0, c0 + 96)
+                if b % 2 == 1:
+                    act(o, src, FN.Relu, scale=0.015625)
+                else:
+                    ts(o, src, 0.0, OP.max, 0.015625, OP.mult)
+
+        for i in range(2):
+            for b in (2, 0, 3, 1):
+                src = ind(A("fz", 576 * b, 576 * b + 384), A("offz", 6 * i, 6 * i + 6))
+                if b >= 2:
+                    act(A("zt", 512 * i + b, 512 * i + 384, 4), src, FN.Copy)
+                else:
+                    cp(A("zt", 512 * i + b, 512 * i + 384, 4), src)
+        quant(A(qz, 0, 128), A(sz, 0, 128), A("zt", 0, 512))
+        send(first, qz, sz, 128)
         ts(A("offi"), ind(A("ta"), A("offk", 6, 7)), h192, OP.add)
         if rnd == 0:
             ts(A("offk", 8, 10), A("ci2", 20, 22), 767.0, OP.min)
-        for b in range(4):
-            if b % 2 == 1:
-                act(A("ht", b, 768, 4), P(wbank[b], 0, 192), FN.Relu, scale=0.015625)
-            else:
-                ts(A("ht", b, 768, 4), P(wbank[b], 0, 192), 0.0, OP.max, 0.015625, OP.mult)
-        qh, sh, ql, sl = ("%s%d" % (s, rnd) for s in ("qh", "sh", "ql", "sl"))
-        quant(A(qh), A(sh), A("ht"))
-        eng = shared(core)
-        mask = sum(1 << x for x in eng)
-        rid, pid = topo.addr(peer)[:2]
-        arr = "arr%d" % rnd
-        for src, dst in ((bytes_(A(qh)), bytes_(A(ql))), (A(sh), A(sl))):
-            count["sent"] += len(eng)
-            issue("G", lambda: g.remote_dma(dst[0], src[0], T.sem[arr], T.sem["sent"], pid, rid, mask), [], [src], sem="sent", inc=0)
-        count[arr] = 2 * len(shared(peer))
+        quant(A(qz, 128, 256), A(sz, 128, 256), A("zt", 512, 1024))
+        layer(A(qz, 128, 256), A(sz, 128, 256), (3, 4, 5, 0))
         cp(ind(A("iw"), A("offi", 0, 12)), A("kv"))
+        make_h(1, (3, 4, 5, 0), 0)
+        quant(A(qh), A(sh), A("ht", 512, 1024))
+        send(second, qh, sh, 224)
         tr(A("ti", 0, 384), A("iw", 0, 384))
+        wait("P", first, count[first])
+        layer(A(ql, 96, 224), A(sl, 96, 224), (6, 7, 1, 2))
         tr(A("ti", 384, 768), A("iw", 16, 400))
+        make_h(0, (6, 7, 1, 2), 32)
         cp(A("offx"), ind(A("ti"), A("offk", 8, 10)))
+        quant(A("qo"), A("so"), A("ht", 0, 512))
         if rnd == 1:
             quant(A("qv"), A("sv"), A("vt"))
         if rnd == 2:
             act(A("plr"), ind(A("pre"), A("offz", 0, 12)), FN.Copy)
             for l in range(8):
                 dma("Y", ext(T.pl[l:l + 1, :]), A("plr", 0, 192, 1, 16 * l, 16 * l + 1))
-        wait("P", arr, count[arr])
-        dbank = (1, 2, 6, 7)
-        for b in range(4):
-            mm(dbank[b], 192, *E(b), A(ql), A(sl))
+        planes = (0, 2, 3, 1)
+        dbanks = ((1, 6, 7, 2), (3, 5, 0, 4))
+        for b, bank in zip(planes, dbanks[0]):
+            mm(bank, 128, *E(b), A("qo"), A("so"))
+        wait("P", second, count[second])
+        for b, bank in zip(planes, dbanks[1]):
+            mm(bank, 128, *E(b), A(ql, 192, 320), A(sl, 192, 320))
+        for b, bank in zip(planes, dbanks[0]):
+            tt(A("fz", 576 * b + 384, 576 * b + 480), P(bank, 0, 96), A("zt", b, 384, 4), OP.add)
 
         def take(eng, b, m0, m1):
             o, src = A("xn", 64 * m0 + b, 64 * m1, 4), ind(A("fz", 576 * b, 576 * b + 576), A("offx", m0, m1))
@@ -574,23 +601,31 @@ def rank_program(g, core, T, topo):
             else:
                 cp(o, src)
 
-        for b in range(4):
-            tt(A("fz", 576 * b + 384, 576 * b + 576), P(dbank[b], 0, 192), A("zt", b, 768, 4), OP.add)
+        cut = 24 if rnd < 2 else 16
+        for b, bank in zip(planes, dbanks[1]):
+            tt(A("fz", 576 * b + 480, 576 * b + 576), P(bank, 32, 128), A("zt", 512 + b, 896, 4), OP.add)
             if b < 2:
-                take("S", b, 0, 24)
-        take("S", 2, 0, 6)
-        take("V", 2, 6, 24)
-        take("V", 3, 0, 24)
-        quant_x("xn")
+                take("S", b, 0, cut)
+        if rnd < 2:
+            take("S", 2, 0, 2)
+            take("V", 2, 2, 24)
+            take("V", 3, 0, 24)
+            quant_x("xn")
 
-    mm(3, 128, A("qv"), A("sv"), *X(384, 256))
-    mm(0, 256, A("qv"), A("sv"), *X(256))
-    dma("Y", ext(T.oc[:]), bytes_(A("qx")))
+    take("V", 2, 0, 16)
+    take("V", 3, 0, 16)
+    for b in range(4):
+        take("SSVV"[b], b, 16, 24)
+    for c0, c1, bank in ((0, 256, 0), (256, 384, 3)):
+        quant(*X(c1, c0), A("xn", 4 * c0, 4 * c1))
+        mm(bank, c1 - c0, A("qv"), A("sv"), *X(c1, c0))
+        dma("Y", ext(T.oc[:, 4 * c0:4 * c1]), bytes_(A("qx", c0, c1)))
+    act(A("yo", 0, 256), P(0, 0, 256), FN.Copy)
+    dma("S", ext(T.y[:, 0:256]), A("yo", 0, 256))
+    cp(A("yo", 256, 384), P(3, 0, 128))
     for a in range(4):
         dma("Y", ext(T.osc[4 * a:4 * a + 4, :]), A("sx", 0, 384, 1, 32 * a, 32 * a + 4))
-    cp(A("yo", 256, 384), P(3, 0, 128))
-    act(A("yo", 0, 256), P(0, 0, 256), FN.Copy)
-    dma("S", ext(T.y[:]), A("yo"))
+    dma("S", ext(T.y[:, 256:384]), A("yo", 256, 384))
     for s in sorted(count, key=lambda s: int(s[1:]) if s[0] == "d" else -1):
         if count[s]:
             g.wait_ge(T.sem[s], count[s])

from concourse.mybir import dt, AluOpType, AxisListType, ActivationFunctionType

STEP = [1, 2, 4]
F32, BF, I32, U16, Q4, U8 = "float32", "bfloat16", "int32", "uint16", "float8_e4m3fn_x4", "uint8"


def _sb(n, d):
    return ("sbuf", [128, n], d)


SCRATCH = {
    "xt": _sb(1536, BF), "xn": _sb(1536, BF), "ut": _sb(512, BF), "vt": _sb(512, BF),
    "qx": _sb(384, Q4), "sx": _sb(384, U8), "qu": _sb(128, Q4), "su": _sb(128, U8),
    "qup": _sb(256, Q4), "sup": _sb(256, U8), "qv": _sb(128, Q4), "sv": _sb(128, U8),
    "qw": _sb(512, Q4), "sw": _sb(512, U8),
    "et": _sb(516, BF), "qe": _sb(512, Q4), "se": _sb(512, U8), "idn": _sb(128, BF), "one": _sb(128, BF),
    "gt": _sb(512, BF), "qg": _sb(128, Q4), "sg": _sb(128, U8),
    "ci": _sb(64, I32), "cj": _sb(4, I32), "cf": _sb(128, F32), "col": _sb(32, F32), "offc": _sb(16, U16),
    "mk": _sb(192, F32), "on": _sb(97, F32), "ci2": _sb(24, F32), "offk": _sb(12, U16),
    "kv": _sb(192, F32), "pre": _sb(400, F32),
    "ts": _sb(384, F32), "rs": _sb(1920, F32), "rw": _sb(120, F32), "ww": _sb(120, F32), "dg": _sb(1024, BF),
    "stl": _sb(32, F32), "sml": _sb(32, F32),
    "ya": _sb(56, F32), "yb": _sb(56, F32), "m1": _sb(112, F32), "m1t": _sb(64, F32), "ab": _sb(2, F32),
    "fl": _sb(3 * 161, F32), "m2": _sb(3 * 96, F32), "sa": _sb(291, F32), "sb": _sb(291, F32), "bb": _sb(99, F32),
    "bt": _sb(32, F32), "ee": _sb(188, F32), "kd": _sb(93, F32), "em": _sb(128, F32), "ek": _sb(128, F32),
    "m3": _sb(194, F32), "m3t": _sb(64, F32), "wr": _sb(128, F32), "xs": _sb(128, F32), "ns": _sb(64, F32),
    "cc": _sb(32, F32), "f0": _sb(256, F32), "f1": _sb(256, F32),
    "tau": _sb(256, F32), "tbt": _sb(96, F32), "offs": _sb(32, U16),
    "vx": _sb(384, BF), "vr": _sb(384, BF),
    "wa": _sb(592, BF), "w1": _sb(192, BF), "w2": _sb(224, BF), "w3": _sb(192, BF), "w4": _sb(224, BF),
    "ta": _sb(432, BF), "ti": _sb(768, F32),
    "oa": _sb(48, U16), "ob": _sb(32, U16), "od": _sb(16, U16),
    "offz": _sb(16, U16), "offi": _sb(16, U16), "offx": _sb(32, U16),
    "iw": _sb(400, F32),
    "fz": _sb(4 * 576, BF), "zt": _sb(1024, BF), "qo": _sb(128, Q4), "so": _sb(128, U8), "ht": _sb(1024, BF), "zero": _sb(512, BF),
    "cmp": _sb(4 * 1280, BF), "qc": _sb(1280, Q4), "sc": _sb(1280, U8),
    "plr": _sb(192, F32), "yo": _sb(384, F32),
}
for _r in range(3):
    for _q, _s, _n in (("qz", "sz", 256), ("qh", "sh", 128), ("ql", "sl", 320)):
        SCRATCH["%s%d" % (_q, _r)] = _sb(_n, Q4)
        SCRATCH["%s%d" % (_s, _r)] = _sb(_n, U8)
for _b in range(8):
    SCRATCH["pb%d" % _b] = ("psum", [128, 512], F32)

NDMA = 24
SEMAPHORES = ["cV", "cS", "cP", "cG", "sent"] + ["arr%d%d" % (r, i) for r in range(3) for i in range(2)] + ["d%d" % i for i in range(NDMA)]

OP = AluOpType
FN = ActivationFunctionType
BIG = 2.0 ** 80
FAR = 2.0 ** 95
KK = 1024.0
TINY = 2.0 ** -40
LOW = -(1 << 20)


def rank_program(g, core, T, topo):
    rank = T.rank_of(core)
    if rank is None:
        return
    queue = {"V": g.vector, "S": g.scalar, "P": g.tensor, "G": g, "Y": g.sync}
    count = {"cV": 0, "cS": 0, "cP": 0, "cG": 0}
    known = {e: {} for e in queue}
    recs = {}
    ndma = [0]

    def A(name, c0=0, c1=None, st=1, p0=0, p1=128):
        n = SCRATCH[name][1][1]
        c1 = n if c1 is None else c1
        ap = T[name][p0:p1, c0:c1:st] if st != 1 else T[name][p0:p1, c0:c1]
        cols = 0
        for c in range(c0, c1, st):
            cols |= 1 << c
        pm = 0
        for b in range(p0 // 32, (p1 + 31) // 32):
            pm |= 1 << b
        if name.startswith("pb"):
            cols, pm = 1, 15
        return (ap, [(name, pm, cols)])

    def B(name, a, c0, c1, st=1):
        return A(name, c0, c1, st, 32 * a, 32 * a + 32)

    def ind(win, off):
        return (win[0].indirect(off[0]), win[1], off[1])

    def words(v):
        return (v[0].bitcast(dt.uint32), v[1])

    def wait(e, sem, val, snap=None):
        if known[e].get(sem, 0) < val:
            queue[e].wait_ge(T.sem[sem], val)
            known[e][sem] = val
        if snap:
            for s, x in snap.items():
                if known[e].get(s, 0) < x:
                    known[e][s] = x

    def issue(e, call, outs, ins, sem=None, inc=1, chain=False):
        acc = []
        for v in outs:
            acc += [(x, True) for x in v[1]]
            if len(v) > 2:
                acc += [(x, False) for x in v[2]]
        for v in ins:
            if isinstance(v, tuple):
                acc += [(x, False) for x in v[1]]
                if len(v) > 2:
                    acc += [(x, False) for x in v[2]]
        need = {}
        for (name, pm, cols), wr in acc:
            psum = name.startswith("pb")
            for r in recs.get(name, []):
                if r[1] & pm and r[2] & cols and (wr or r[0] or (psum and r[3] != e)):
                    if chain and psum and r[3] == e:
                        continue
                    if need.get(r[4], (0, None))[0] < r[5]:
                        need[r[4]] = (r[5], r[6])
        for s in sorted(need, key=lambda s: s == "c" + e):
            wait(e, s, need[s][0], need[s][1])
        ins_ = call()
        if sem is None:
            sem = "c" + e
            count[sem] += 1
            val = count[sem]
            ins_.then_inc(T.sem[sem], 1)
        elif inc:
            val = inc
            ins_.then_inc(T.sem[sem], inc)
            count[sem] = inc
        else:
            val = count[sem]
        snap = dict(known[e])
        for (name, pm, cols), wr in acc:
            lst = recs.setdefault(name, [])
            if wr:
                lst[:] = [r for r in lst if (r[1] & ~pm) or (r[2] & ~cols)]
            lst.append((wr, pm, cols, e, sem, val, snap))

    def raw(v):
        return v[0] if isinstance(v, tuple) else v

    def tt(o, a, b, op):
        issue("V", lambda: g.vector.tensor_tensor(o[0], a[0], b[0], op), [o], [a, b])

    def ts(o, a, s1, op0, s2=None, op1=None):
        if op1 is None:
            issue("V", lambda: g.vector.tensor_scalar(o[0], a[0], raw(s1), None, op0), [o], [a, s1])
        else:
            issue("V", lambda: g.vector.tensor_scalar(o[0], a[0], raw(s1), raw(s2), op0, op1), [o], [a, s1, s2])

    def cp(o, a):
        issue("V", lambda: g.vector.tensor_copy(o[0], a[0]), [o], [a])

    def tr(o, a):
        issue("V", lambda: g.vector.transpose(o[0], a[0]), [o], [a])

    def red(o, a, op, neg=False):
        issue("V", lambda: g.vector.tensor_reduce(o[0], a[0], AxisListType.X, op, negate=neg), [o], [a])

    def scan(o, a, b, init, op0, op1):
        issue("V", lambda: g.vector.tensor_tensor_scan(o[0], a[0], b[0], raw(init), op0, op1), [o], [a, b, init])

    def fill(o, x):
        issue("V", lambda: g.vector.memset(o[0], x), [o], [])

    def quant(q, s, a):
        issue("V", lambda: g.vector.quantize_mx(q[0], s[0], a[0]), [q, s], [a])

    def act(o, a, fn, bias=None, scale=None, accum=None):
        kw = {}
        if bias is not None:
            kw["bias"] = raw(bias)
        if scale is not None:
            kw["scale"] = raw(scale)
        if accum is not None:
            kw["accum_out"] = accum[0]
        issue("S", lambda: g.scalar.activation(o[0], a[0], fn, **kw), [o] + ([accum] if accum else []), [a, bias, scale])

    def lin(o, a, scale=None, bias=None, accum=None):
        act(o, a, FN.Identity, bias, scale, accum)

    def mm(bank, n, wq, ws_, xq, xs, start=True, stop=True):
        o = A("pb%d" % bank, 0, n)
        issue("P", lambda: g.tensor.matmul_mx(o[0], wq[0], ws_[0], xq[0], xs[0], start, stop), [o], [wq, ws_, xq, xs], chain=not start)

    def iota(o, pattern, base, mult=0):
        if SCRATCH[o[1][0][0]][2] == I32:
            issue("G", lambda: g.iota(o[0], pattern, base, mult), [o], [])
        else:
            issue("G", lambda: g.iota(o[0], pattern, base, mult, allow_small_or_imprecise_dtypes=True), [o], [])

    def gfill(o, n, x):
        iota(o, [[0, n]], x)

    def sel(o, a, pattern, op, other, base, mult):
        issue("G", lambda: g.affine_select(o[0], a[0], pattern, op, other, base, mult), [o], [a])

    def dma(e, o, a):
        sem = "d%d" % ndma[0]
        ndma[0] += 1
        issue(e, lambda: queue[e].dma_start(o[0], a[0]), [o], [a], sem=sem, inc=16)

    def ext(ap):
        return (ap, [])

    def bytes_(v):
        return (v[0].bitcast(dt.uint8), v[1])

    def P(b, c0, c1, st=1):
        return A("pb%d" % b, c0, c1, st)

    dma("S", A("ut"), ext(T.u[:]))
    dma("Y", A("xt", 1024, 1536), ext(T.x[:, 1024:1536]))
    dma("Y", A("xt", 0, 1024), ext(T.x[:, 0:1024]))
    dma("Y", bytes_(A("qw")), ext(T.wc[:]))
    dma("Y", A("sw"), ext(T.ws[:]))
    dma("Y", A("vt"), ext(T.v[:]))

    iota(A("ci", 0, 16), [[16, 2], [32, 4], [0, 2]], 0)
    iota(A("ci", 48, 49), [[0, 1]], 0, 1)
    gfill(A("one"), 128, 1)
    sel(A("idn"), A("one"), [[-1, 128]], OP.is_equal, 0.0, 0, 1)
    iota(A("cf", 0, 32), [[1, 32]], 0)
    iota(A("cf", 32, 64), [[0, 16], [1, 2]], 0)
    iota(A("cf", 96, 120), [[32, 12], [0, 2]], -192)
    fill(A("et"), 0.0)
    fill(A("gt"), 0.0)
    cp(A("offc"), A("ci", 0, 16))
    for i, m in enumerate((31, 1, 16, 15)):
        ts(A("cj", i, i + 1), A("ci", 48, 49), m, OP.bitwise_and)
    for a in range(4):
        for par in range(2):
            c0 = 128 * a + 64 * par
            fill(B("gt", a, c0 + par, c0 + 64, 2), 1.0)
    cp(A("col", 0, 4), A("cj", 0, 4))
    fill(A("stl", 24, 32), -FAR)
    quant(A("qg"), A("sg"), A("gt"))
    act(A("et", 3, 515, 4), A("idn"), FN.Copy)
    fill(A("ya", 24, 56), -FAR)
    fill(A("yb", 24, 56), FAR)
    fill(A("zero"), 0.0)
    quant(A("qu"), A("su"), A("ut"))
    cp(words(A("qup")), ind(words(A("qu")), A("offc")))
    act(A("sup"), ind(A("su"), A("offc")), FN.Copy)

    def quant_e(b):
        quant(A("qe", 128 * b, 128 * b + 128), A("se", 128 * b, 128 * b + 128), A("et", 3 - b, 515 - b))

    (n_, par_, h16, q_, pm0, me, mo, nh16, sgn, h192, ccol, k1, k2, k3, k4, k5, k6, k7, k8, k9, k10, k11, k12, k13) = (A("col", i, i + 1) for i in range(24))
    xr, xpar, same = A("cf", 0, 32), A("cf", 32, 64), A("cf", 64, 96)
    ident, even = A("ci2", 0, 12), A("ci2", 15, 16)
    lin(pm0, par_, -1.0, 1.0)
    lin(sgn, par_, 2.0, -1.0)
    lin(me, h16, -0.0625, 1.0)
    lin(mo, h16, 0.0625)
    lin(k1, par_, 416.0, -224.0)
    lin(k2, par_, -208.0, 224.0)
    lin(k3, par_, 96.0, -63.0)
    lin(k4, par_, -33.0, 64.0)
    lin(k5, par_, 368.0, h16)
    lin(k6, par_, 16.0, 576.0)
    lin(k10, q_, 1.0, 416.0)
    lin(same, xpar, sgn, pm0)
    lin(k7, q_, 16.0, k2)
    lin(k8, q_, 1.0, k4)
    lin(k9, q_, 16.0, k5)
    lin(ccol, n_, -16.0, k6)
    lin(k12, k10, me)
    lin(k13, h16, 1.0, 1.0)

    def late_constants():
        lin(A("mk", 33, 64), A("cf", 65, 96), 1.0 / TINY, TINY)
        lin(A("mk", 32, 33), A("cf", 64, 65), 1.0, TINY)
        lin(A("mk", 64, 65), A("cf", 64, 65), -1.0 / TINY, -TINY)
        lin(A("mk", 128, 129), A("cf", 64, 65), -1.0, -TINY)
        lin(even, k1, mo, k7)
        lin(k11, k3, mo, k8)
        lin(ident, A("cf", 0, 12), 16.0, q_)
        lin(A("cc"), xr, -1.0, ccol)
        lin(A("vx", 1, 384, 16), A("cf", 96, 120), None, n_)
        lin(nh16, h16, -1.0)
        lin(h192, h16, 1.0, 192.0)
        lin(A("ci2", 14, 15), even, 1.0, 16.0)
        lin(A("ci2", 16, 17), even, mo, k12)
        lin(A("ci2", 18, 19), even, 1.0, k13)
        lin(A("ci2", 12, 14), A("cf", 0, 2), 16.0, k11)
        lin(A("ci2", 20, 22), A("cf", 0, 2), 256.0, k9)
        lin(A("ta", 416, 428), ident)

    gfill(A("rs", 0, 1920, 16), 120, 0)
    gfill(A("rw"), 120, 0)
    gfill(A("rs", 32, 640, 80), 8, 192)
    gfill(A("rs", 672, 960, 80), 4, 128)
    gfill(A("rw", 1, 120, 5), 24, -1)
    gfill(A("rw", 2, 120, 5), 24, 1)
    gfill(A("on"), 97, 1)
    gfill(A("mk", 0, 32), 32, 1)
    gfill(A("mk", 96, 128), 32, 1)
    for k in range(3):
        gfill(A("fl", 161 * k + 97, 161 * k + 161), 64, 0)
    gfill(A("fl", 64, 483, 161), 3, -1)
    gfill(A("sa", 192, 291, 3), 33, 5000)
    gfill(A("sa", 194, 291, 3), 33, -5000)
    gfill(A("vx"), 384, 0)
    gfill(A("ee"), 188, 0)
    gfill(A("m3", 0, 6), 6, 0)
    gfill(A("kd", 0, 93, 3), 31, 1)
    gfill(A("kd", 1, 93, 3), 31, int(KK))
    gfill(A("m3t", 32, 64), 32, 0)
    gfill(A("em", 0, 128, 2), 64, LOW)
    gfill(A("ek", 0, 128, 2), 64, LOW)
    gfill(A("xs", 0, 64), 64, 0)
    gfill(A("wr", 0, 64), 64, 0)
    gfill(A("f0", 128, 256, 2), 64, LOW)
    gfill(A("f1", 130, 256, 4), 32, LOW)
    gfill(A("tau", 1, 256, 4), 64, 0)
    gfill(A("wa", 0, 224), 224, 0)
    gfill(A("ta", 428, 432), 4, 0)
    for w in ("w2", "w4"):
        gfill(A(w, 0, 16), 16, 0)
        gfill(A(w, 208, 224), 16, 0)
    for t in ("zt", "ht"):
        for i in range(2):
            gfill(A(t, 512 * i + 384, 512 * i + 512), 128, 0)
    iota(A("kv"), [[1, 192]], 384)
    iota(A("pre"), [[1, 400]], 0)

    def E(b):
        return A("qe", 128 * b, 128 * b + 128), A("se", 128 * b, 128 * b + 128)

    def U(i):
        if i == 0:
            return A("qu"), A("su")
        return A("qup", 128 * i - 128, 128 * i), A("sup", 128 * i - 128, 128 * i)

    def X(n, c0=0):
        return A("qx", c0, n), A("sx", c0, n)

    qbase = {10: 0, 8: 320, 6: 576, 0: 768, 2: 960, 4: 1152}
    width = {10: 320, 8: 256, 6: 192, 0: 192, 2: 192, 4: 128}
    count["sent"] = 0

    def shared(c):
        r = T.rank_of(c)
        sets = [topo.engines(c, T.cores[r ^ e]) for e in STEP]
        return [x for x in sets[0] if all(x in s for s in sets)]

    def quant_x(src):
        quant(*X(384, 256), A(src, 1024, 1536))
        quant(*X(256), A(src, 0, 1024))

    def slot(b0, t):
        return A("cmp", 4 * qbase[b0] + t, 4 * (qbase[b0] + width[b0]), 4)

    def srows(b0):
        for t in (0, 2, 1, 3):
            n = 2 * b0 + t
            act(slot(b0, t), P(1 + t % 2, 0, width[b0]), FN.Sign,
                bias=A("ts", 16 * n, 16 * n + 1), scale=-1.0, accum=A("rs", 80 * n + 32, 80 * n + 33))

    def sdiag(b0):
        for t in (0, 2, 1, 3):
            n = 2 * b0 + t
            act(A("dg", 64 * (n - 8), 64 * (n - 7)), P(1 + t % 2, 32 * b0, 32 * b0 + 64), FN.Sign,
                bias=A("ts", 16 * n, 16 * n + 1), scale=-1.0, accum=A("rs", 80 * n + 16, 80 * n + 17))

    def vrows(b0):
        for t in (0, 2, 1, 3):
            n = 2 * b0 + t
            ts(slot(b0, t), P(3 + t % 2, 0, width[b0]), A("ts", 16 * n, 16 * n + 1), OP.is_lt, 2.0, OP.mult)

    def cq(b0):
        return A("qc", qbase[b0], qbase[b0] + width[b0]), A("sc", qbase[b0], qbase[b0] + width[b0])

    def cquant(b0):
        quant(*cq(b0), A("cmp", 4 * qbase[b0], 4 * (qbase[b0] + width[b0])))

    def csum(b0, start=False, stop=False):
        mm(5, width[b0], A("qg"), A("sg"), *cq(b0), start, stop)

    def unpack(b, bank):
        act(A("fz", 576 * b, 576 * b + 384), P(bank, 0, 384), FN.Copy)

    quant_x("xt")
    for rnd, e in enumerate(STEP):
        peer = T.cores[rank ^ e]
        mm(7, 128, *U(0), *X(384, 256))
        mm(0, 256, *U(0), *X(256))
        mm(1, 384, *U(1), *X(384))
        mm(3, 192, *U(1), *X(192))
        mm(2, 384, *U(2), *X(384))
        mm(4, 192, *U(2), *X(192))
        if rnd == 0:
            quant_e(0)
            quant_e(1)
        tr(A("ts", 256, 384), P(7, 0, 128))
        tr(A("ts", 0, 192), P(0, 0, 192))
        tr(A("ts", 192, 256), P(0, 192, 256))
        mm(6, 384, *E(0), *X(384))
        mm(7, 384, *E(1), *X(384))
        srows(10)
        vrows(0)
        srows(8)
        vrows(2)
        cquant(0)
        cquant(10)
        csum(10, start=True)
        csum(0)
        srows(6)
        vrows(4)
        cquant(2)
        cquant(8)
        cquant(4)
        csum(2)
        csum(8)
        csum(4)
        cquant(6)
        csum(6, stop=True)
        for b0 in (4, 6, 8, 10):
            sdiag(b0)
        cp(A("stl", 0, 24), A("ts", 0, 384, 16))
        if rnd == 0:
            quant_e(2)
            quant_e(3)
            fill(A("rs", 48, 1920, 80), BIG / 2)
            fill(A("rw", 3, 120, 5), -BIG)
            fill(A("kd", 2, 93, 3), 1.0 / KK)
        mm(1, 384, *E(2), *X(384))
        mm(2, 384, *E(3), *X(384))
        if rnd == 0:
            late_constants()
        unpack(0, 6)
        unpack(1, 7)
        tr(A("sml"), A("stl"))
        tr(A("rs", 0, 1600, 5), P(5, 0, 320))
        scan(A("ww"), A("rw"), A("rs", 0, 1920, 16), 0.0, OP.mult, OP.add)
        tt(A("yb", 0, 24), A("stl", 0, 24), A("ww", 3, 120, 5), OP.max)
        tt(A("ya", 0, 24), A("stl", 0, 24), A("ww", 3, 120, 5), OP.min)
        for y, m0, far, op in (("yb", 0, FAR, OP.min), ("ya", 56, -FAR, OP.max)):
            for p in range(2):
                scan(A("m1", m0 + p, m0 + 56, 2), A(y, p, 56, 2), A(y, p, 56, 2), far, op, op)
        if rnd == 0:
            ts(A("mk", 161, 192), A("cf", 1, 32), n_, OP.is_le)
        tr(A("m1t", 0, 32), A("m1", 24, 56))
        tr(A("m1t", 32, 64), A("m1", 80, 112))
        if rnd == 0:
            tt(A("mk", 65, 96), A("mk", 33, 64), A("mk", 161, 192), OP.mult)
            tt(A("mk", 129, 160), A("mk", 33, 64), A("mk", 161, 192), OP.mult)
        red(A("ab", 1, 2), A("m1t", 0, 32), OP.min)
        red(A("ab", 0, 1), A("m1t", 32, 64), OP.max)
        for k, (col, op) in enumerate(((1, OP.is_gt), (1, OP.is_ge), (0, OP.is_ge))):
            ts(A("fl", 161 * k + 65, 161 * k + 97), A("sml"), A("ab", col, col + 1), op)
        scan(A("m2", 0, 64), A("mk", 96, 160), A("fl", 65, 129), 0.0, OP.mult, OP.add)
        for k in (1, 2):
            scan(A("m2", 96 * k, 96 * k + 96), A("mk", 0, 96), A("fl", 161 * k + 65, 161 * k + 161), 0.0, OP.mult, OP.add)
        tr(A("fl", 32, 64), A("m2", 32, 64))
        for k in (1, 2):
            tr(A("fl", 161 * k, 161 * k + 64), A("m2", 96 * k + 32, 96 * k + 96))
        for k, c0, init, buf, ph in ((0, 32, 192.0, "sb", 1), (1, 32, 192.0, "sb", 0), (1, 0, 0.0, "sa", 1), (2, 0, 0.0, "sb", 2)):
            scan(A(buf, 3 * c0 + ph, 291, 3), A("on", c0, 97), A("fl", 161 * k + c0, 161 * k + 97), init, OP.mult, OP.add)
        scan(A("bb"), A("sa", 192, 291), A("sb", 192, 291), 0.0, OP.max, OP.min)
        bc, bp = A("bb", 5, 99, 3), A("bb", 2, 96, 3)
        tr(A("bt"), bc)
        tt(A("ns", 0, 32), bc, bp, OP.is_equal)
        lin(A("vx", 0, 384, 16), A("bt", 0, 24))
        tt(A("ee", 3, 72, 6), A("bt", 1, 24, 2), A("bt", 0, 24, 2), OP.subtract)
        for a in range(1, 4):
            tt(B("ee", a, 0, 72, 6), B("bt", a, 0, 24, 2), B("bt", a - 1, 1, 24, 2), OP.subtract)
        tt(A("ns", 32, 64), A("ns", 0, 32), A("cc"), OP.mult)
        for p in (1, 0):
            scan(A("m3", 6 + 3 * p, 191 + 3 * p, 2), A("kd"), A("ee", 3 * p, 185 + 3 * p, 2), 0.0, OP.mult, OP.max)
        em = A("em", 65, 128, 2)
        tr(em, A("ee", 0, 96, 3))
        for d in range(2):
            tt(A("xs", 64 + d, 128, 2), A("ns", 32, 64), bc, OP.add)
        tr(A("em", 1, 64, 2), A("m3", 0, 96, 3))
        tr(A("m3t", 0, 32), A("m3", 96, 192, 3))
        tr(A("ek", 1, 64, 2), A("m3", 2, 98, 3))
        lin(A("ek", 65, 128, 2), em, KK)
        for d in range(2):
            lin(A("wr", 64 + d, 128, 2), em, KK + 1.0, 191.0 - KK)
        if rnd == 0:
            ts(A("offk", 0, 5), A("ci2", 12, 17), 431.0, OP.min)
            ts(A("offk", 6, 7), A("ci2", 18, 19), 431.0, OP.min)
        tr(A("vr", 0, 128), A("vx", 0, 128))
        scan(A("f1", 1, 256, 2), A("xs"), A("em"), 0.0, OP.subtract, OP.max)
        scan(A("f1", 0, 256, 4), A("m3t"), A("m3t"), 0.0, OP.max, OP.max)
        scan(A("f0", 1, 256, 2), A("wr"), A("ek"), 0.0, OP.subtract, OP.max)
        tr(A("vr", 128, 384), A("vx", 128, 384))
        scan(A("tau", 64, 192), A("f0", 128, 256), A("f1", 128, 256), 0.0, OP.subtract, OP.max)
        unpack(2, 1)
        unpack(3, 2)
        if rnd == 0:
            cp(A("ob", 0, 12), ident)
        tr(A("tbt", 0, 64), A("tau", 1, 256, 4))
        tr(A("tbt", 64, 96), A("tau", 65, 192, 4))
        if rnd == 0:
            cp(A("ob", 16, 28), ident)
            cp(A("offk", 10, 11, 1, 0, 64), A("col", 20, 21, 1, 0, 64))
            cp(A("offk", 10, 11, 1, 64, 128), A("offk", 2, 3, 1, 64, 128))
        cp(A("offs"), ind(A("tbt"), A("offk", 0, 2)))
        cp(ind(A("wa", 16, 592), A("offs", 0, 24)), A("vr"))

        def turn(w):
            tr(A("ta", 0, 224), A(w, 0, 224))
            tr(A("ta", 224, 416), A(w, 16, 208))

        def step(out, o0, win, w0, off, c0, cut):
            w = A(win, w0, w0 + 192)
            act(A(out, o0, o0 + 16 * cut), ind(w, A(off, c0, c0 + cut)), FN.Copy)
            if cut < 12:
                cp(A(out, o0 + 16 * cut, o0 + 192), ind(w, A(off, c0 + cut, c0 + 12)))

        turn("wa")
        cp(A("oa"), ind(A("ta"), A("offk", 2, 5)))
        for a in (1, 3):
            cp(B("ob", a, 0, 32), B("oa", a - 1, 0, 32))
        step("w1", 0, "wa", 16, "oa", 32, 8)
        step("w2", 16, "w1", 0, "ob", 0, 6)
        step("w3", 0, "w2", 16, "ob", 16, 12)
        quant(A("ql%d" % rnd, 0, 128), A("sl%d" % rnd, 0, 128), A("zero"))
        for a in (2, 3):
            tr(B("ta", a, 0, 224), B("w2", 1, 0, 224))
            tr(B("ta", a, 224, 416), B("w2", 1, 16, 208))
        cp(A("od"), ind(A("ta"), A("offk", 10, 11)))
        step("w4", 16, "w3", 0, "od", 0, 6)
        lin(A("iw"), A("pre"), None, nh16)
        turn("w4")
        ts(A("offz"), ind(A("ta"), A("offk", 6, 7)), 192.0, OP.add)
        qz, sz, qh, sh, ql, sl = ("%s%d" % (s, rnd) for s in ("qz", "sz", "qh", "sh", "ql", "sl"))
        first, second = "arr%d0" % rnd, "arr%d1" % rnd
        eng = shared(core)
        rid, pid = topo.addr(peer)[:2]
        mask = sum(1 << x for x in eng)

        def send(arr, q, z, c0):
            for src, dst in ((bytes_(A(q, 0, 96)), bytes_(A(ql, c0, c0 + 96))), (A(z, 0, 96), A(sl, c0, c0 + 96))):
                count["sent"] += len(eng)
                issue("G", lambda: g.remote_dma(dst[0], src[0], T.sem[arr], T.sem["sent"], pid, rid, mask), [], [src], sem="sent", inc=0)
            count[arr] = 2 * len(shared(peer))

        def layer(q, z, banks):
            for b in range(4):
                mm(banks[b], 128, A("qw", 128 * b, 128 * b + 128), A("sw", 128 * b, 128 * b + 128), q, z)

        def make_h(i, banks, c0):
            for b in range(4):
                o, src = A("ht", 512 * i + b, 512 * i + 384, 4), P(banks[b], c0, c0 + 96)
                if b % 2 == 1:
                    act(o, src, FN.Relu, scale=0.015625)
                else:
                    ts(o, src, 0.0, OP.max, 0.015625, OP.mult)

        for i in range(2):
            for b in (2, 0, 3, 1):
                src = ind(A("fz", 576 * b, 576 * b + 384), A("offz", 6 * i, 6 * i + 6))
                if b >= 2:
                    act(A("zt", 512 * i + b, 512 * i + 384, 4), src, FN.Copy)
                else:
                    cp(A("zt", 512 * i + b, 512 * i + 384, 4), src)
        quant(A(qz, 0, 128), A(sz, 0, 128), A("zt", 0, 512))
        send(first, qz, sz, 128)
        ts(A("offi"), ind(A("ta"), A("offk", 6, 7)), h192, OP.add)
        if rnd == 0:
            ts(A("offk", 8, 10), A("ci2", 20, 22), 767.0, OP.min)
        quant(A(qz, 128, 256), A(sz, 128, 256), A("zt", 512, 1024))
        layer(A(qz, 128, 256), A(sz, 128, 256), (3, 4, 5, 0))
        cp(ind(A("iw"), A("offi", 0, 12)), A("kv"))
        make_h(1, (3, 4, 5, 0), 0)
        quant(A(qh), A(sh), A("ht", 512, 1024))
        send(second, qh, sh, 224)
        tr(A("ti", 0, 384), A("iw", 0, 384))
        wait("P", first, count[first])
        layer(A(ql, 96, 224), A(sl, 96, 224), (6, 7, 1, 2))
        tr(A("ti", 384, 768), A("iw", 16, 400))
        make_h(0, (6, 7, 1, 2), 32)
        cp(A("offx"), ind(A("ti"), A("offk", 8, 10)))
        quant(A("qo"), A("so"), A("ht", 0, 512))
        if rnd == 1:
            quant(A("qv"), A("sv"), A("vt"))
        if rnd == 2:
            act(A("plr"), ind(A("pre"), A("offz", 0, 12)), FN.Copy)
            for l in range(8):
                dma("Y", ext(T.pl[l:l + 1, :]), A("plr", 0, 192, 1, 16 * l, 16 * l + 1))
        planes = (0, 2, 3, 1)
        dbanks = ((1, 6, 7, 2), (3, 5, 0, 4))
        for b, bank in zip(planes, dbanks[0]):
            mm(bank, 128, *E(b), A("qo"), A("so"))
        wait("P", second, count[second])
        for b, bank in zip(planes, dbanks[1]):
            mm(bank, 128, *E(b), A(ql, 192, 320), A(sl, 192, 320))
        for b, bank in zip(planes, dbanks[0]):
            tt(A("fz", 576 * b + 384, 576 * b + 480), P(bank, 0, 96), A("zt", b, 384, 4), OP.add)

        def take(eng, b, m0, m1):
            o, src = A("xn", 64 * m0 + b, 64 * m1, 4), ind(A("fz", 576 * b, 576 * b + 576), A("offx", m0, m1))
            if eng == "S":
                act(o, src, FN.Copy)
            else:
                cp(o, src)

        cut = 24 if rnd < 2 else 16
        for b, bank in zip(planes, dbanks[1]):
            tt(A("fz", 576 * b + 480, 576 * b + 576), P(bank, 32, 128), A("zt", 512 + b, 896, 4), OP.add)
            if b < 2:
                take("S", b, 0, cut)
        if rnd < 2:
            take("S", 2, 0, 2)
            take("V", 2, 2, 24)
            take("V", 3, 0, 24)
            quant_x("xn")

    take("V", 2, 0, 16)
    take("V", 3, 0, 16)
    for b in range(4):
        take("SSVV"[b], b, 16, 24)
    for c0, c1, bank in ((0, 256, 0), (256, 384, 3)):
        quant(*X(c1, c0), A("xn", 4 * c0, 4 * c1))
        mm(bank, c1 - c0, A("qv"), A("sv"), *X(c1, c0))
        dma("Y", ext(T.oc[:, 4 * c0:4 * c1]), bytes_(A("qx", c0, c1)))
    act(A("yo", 0, 256), P(0, 0, 256), FN.Copy)
    dma("S", ext(T.y[:, 0:256]), A("yo", 0, 256))
    cp(A("yo", 256, 384), P(3, 0, 128))
    for a in range(4):
        dma("Y", ext(T.osc[4 * a:4 * a + 4, :]), A("sx", 0, 384, 1, 32 * a, 32 * a + 4))
    dma("S", ext(T.y[:, 256:384]), A("yo", 256, 384))
    for s in sorted(count, key=lambda s: int(s[1:]) if s[0] == "d" else -1):
        if count[s]:
            g.wait_ge(T.sem[s], count[s])
